import numpy as np
import ml_dtypes


def mxq(x, axis, fmt="e4m3"):
    dtype, down = {"e4m3": (ml_dtypes.float8_e4m3fn, 7), "e5m2": (ml_dtypes.float8_e5m2, 14)}[fmt]
    v = np.moveaxis(np.asarray(x, np.float32).astype(ml_dtypes.bfloat16).astype(np.float64), axis, -1)
    blocks = v.reshape(v.shape[:-1] + (-1, 32))
    amax = np.abs(blocks).max(-1, keepdims=True)
    byte = np.maximum(np.where(amax > 0, np.frexp(amax)[1] - 1 + 127, 0) - down, 1)
    scale = np.exp2(byte - 127.0)
    codes = (blocks / scale).astype(np.float32).astype(dtype).astype(np.float64)
    return np.moveaxis((codes * scale).reshape(v.shape), -1, axis)


WIDE = False


def mx_kscale(k):
    if not WIDE:
        return np.ones(k)
    levels = np.array([10, -10, 5, -5, 0])
    if k % 512:
        return np.exp2(np.random.permutation(np.resize(levels, k // 32))).repeat(32)
    a = np.empty((k // 512, 16))
    for p in range(k // 512):
        a[p, :8] = np.random.permutation(np.resize(levels, 8))
        for g in range(8):
            far = levels[np.abs(levels - a[p, g]) >= 10]
            a[p, g + 8] = far[np.random.randint(len(far))]
    return np.exp2(a.ravel()).repeat(32)


def f64(x):
    return np.asarray(x).astype(np.float64)


def striped(idx):
    return np.tile(idx.reshape(-1, 16).T, (8, 1)).astype(np.uint16)


def unstriped(offs):
    return offs[:16].T.reshape(-1).astype(np.int64)


def striped8(idx):
    return np.concatenate([x.reshape(-1, 16).T for x in idx]).astype(np.uint16)


def runs(offs, k):
    lists = np.stack([offs[16 * r : 16 * r + 16].T.reshape(-1) for r in range(8)]).astype(np.int64)
    return lists[np.arange(k) % 512 // 64]


def pack_weight(w):
    k, n = w.shape
    w = f64(np.asarray(w, np.float32).astype(ml_dtypes.bfloat16)).reshape(k // 32, 32, n)
    amax = np.abs(w).max(1)
    byte = np.clip(np.where(amax > 0, np.frexp(amax)[1] - 1 + 127 - 7, 1), 1, 254)
    scaled = (w * np.exp2(127.0 - byte)[:, None, :]).reshape(k, n).astype(np.float32)
    words = np.ascontiguousarray(scaled.reshape(k // 512, 128, 4, n).transpose(0, 1, 3, 2)).astype(ml_dtypes.float8_e4m3fn).view(np.uint8)
    return words, np.ascontiguousarray(byte.astype(np.uint8).reshape(k // 512, 16, n))


def unpack_weight(words, scales):
    g, p, n, _ = words.shape
    vals = np.ascontiguousarray(words).view(ml_dtypes.float8_e4m3fn).astype(np.float64) * np.repeat(np.exp2(scales.astype(np.float64) - 127.0), 8, axis=1)[..., None]
    return vals.transpose(0, 1, 3, 2).reshape(g * 512, n)


K, T, S, N, H = 512, 2048, 512, 512, 512
P = 2 ** 7


def setup_inputs():
    n = np.random.standard_normal
    s = mx_kscale(K)[:, None]
    u = mx_kscale(H)
    packed_xT = pack_weight(n((K, T)) * s)
    return {
        "x_words": packed_xT[0],
        "x_scales": packed_xT[1],
        "w1": (n((K, H)) / np.sqrt(K) / s).astype(np.float32),
        "w2": (n((K, H)) / np.sqrt(K) / s * u).astype(np.float32),
        "w3": (n((K, H)) / np.sqrt(K) / s * u).astype(np.float32),
        "dir1": np.tile(np.random.uniform(-1, 1, S), (P, 1)).astype(np.float32),
        "dir2": np.tile(np.random.uniform(-1, 1, S), (P, 1)).astype(np.float32),
        "w4": (n((H, N)) / np.sqrt(H) / u[:, None]).astype(np.float32),
        "offs": striped(np.random.permutation(T)[:S]),
        "p1": striped8(np.stack([np.random.permutation(S) for _ in range(8)])),
        "p2": striped8(np.stack([np.random.permutation(S) for _ in range(8)])),
    }


def reference(x_words, x_scales, w1, w2, w3, dir1, dir2, w4, offs, p1, p2):
    xq = unpack_weight(x_words, x_scales)[:, unstriped(offs)]
    y = mxq(f64(w1), 0, "e4m3").T @ xq
    e = mxq(f64(w2), 0, "e4m3").T @ xq
    q = mxq(f64(w3), 0, "e4m3").T @ xq
    z = (y[np.arange(H)[:, None], runs(p1, H)]) * (e[np.arange(H)[:, None], runs(p1, H)]) + (q[np.arange(H)[:, None], runs(p1, H)]) * f64(dir1)[:1] + (y[np.arange(H)[:, None], runs(p2, H)]) * (e[np.arange(H)[:, None], runs(p2, H)]) + (q[np.arange(H)[:, None], runs(p2, H)]) * f64(dir2)[:1]
    return mxq(f64(w4), 0, "e4m3").T @ mxq(z, 0, "e4m3")

@@ -1,0 +1,250 @@
+from contextlib import ExitStack
+
+import concourse.mybir as mybir
+from concourse.masks import make_identity
+
+K, T, S, H, N = 512, 2048, 512, 512, 512
+FLOPS = 2 * K * H * S * 3 + 2 * H * N * S
+
+F32 = mybir.dt.float32
+BF16 = mybir.dt.bfloat16
+I32 = mybir.dt.int32
+U32 = mybir.dt.uint32
+U16 = mybir.dt.uint16
+U8 = mybir.dt.uint8
+FP8X4 = mybir.dt.float8_e4m3fn_x4
+MULT = mybir.AluOpType.mult
+ADD = mybir.AluOpType.add
+
+P = 128
+PACK = 4
+LIST = 16
+
+
+def tile_picked_painn8_none_p_kernel(
+    tc, x_words, x_scales, w1, w2, w3, dir1, dir2, w4, offs, p1, p2, out
+):
+    nc = tc.nc
+    with ExitStack() as ctx:
+        lists = ctx.enter_context(tc.tile_pool(name="lists", bufs=1))
+        sb = ctx.enter_context(tc.tile_pool(name="sb", bufs=1))
+        psum = ctx.enter_context(tc.psum_pool(name="psum", bufs=1))
+
+        def bank(b, name):
+            return psum.tile([P, 512], F32, tag="bank%d" % b, name=name)
+
+        offs_sb = lists.tile([P, S // LIST], U16, name="offs_sb")
+        p1_sb = lists.tile([P, S // LIST], U16, name="p1_sb")
+        p2_sb = lists.tile([P, S // LIST], U16, name="p2_sb")
+
+        words_all = sb.tile([P, T], I32, name="words_all", align_bytes=64)
+        scales_all = sb.tile([P, T], U8, name="scales_all", align_bytes=64)
+        nc.vector.memset(scales_all[:].bitcast(I32), 0)
+
+        nc.sync.dma_start(words_all[:], x_words[0].rearrange("p n t -> p (n t)").bitcast(I32))
+        nc.sync.dma_start(offs_sb[:], offs)
+        for quad in range(4):
+            nc.sync.dma_start(
+                scales_all[32 * quad : 32 * quad + 4, :].bitcast(I32),
+                x_scales[0, 4 * quad : 4 * quad + 4, :].bitcast(I32),
+            )
+        w3_rows = w3.rearrange("(p j) c -> p j c", j=PACK)
+        w3_raw = []
+        for half in range(2):
+            raw = sb.tile([P, PACK, H // 2], F32, name="w3_raw%d" % half)
+            nc.sync.dma_start(raw[:], w3_rows[:, :, half * (H // 2) : (half + 1) * (H // 2)])
+            w3_raw.append(raw)
+        dir1_sb = sb.tile([P, S], F32, name="dir1_sb")
+        dir2_sb = sb.tile([P, S], F32, name="dir2_sb")
+        nc.sync.dma_start(p1_sb[:], p1)
+        nc.sync.dma_start(dir1_sb[:], dir1)
+        nc.sync.dma_start(p2_sb[:], p2)
+        nc.sync.dma_start(dir2_sb[:], dir2)
+        w_raw = {}
+        for name, w in (("w1", w1), ("w2", w2), ("w4", w4)):
+            w_raw[name] = sb.tile([P, PACK, H], F32, name=name + "_raw")
+            nc.sync.dma_start(w_raw[name][:], w.rearrange("(p j) c -> p j c", j=PACK))
+
+        ident = sb.tile([P, P], F32, name="ident")
+        make_identity(nc, ident[:])
+
+        q_win = [sb.tile([P, 2 * S], F32, name="q_win%d" % t) for t in range(PACK)]
+        nc.vector.memset(q_win[0][:, S:], 0.0)
+        for t in range(1, PACK):
+            nc.scalar.copy(q_win[t][:, S:], q_win[0][:, S:])
+
+        x_codes = sb.tile([P, S], U32, name="x_codes", align_bytes=64)
+        x_plane = sb.tile([P, S], U8, name="x_plane", align_bytes=64)
+        nc.vector.tensor_copy(x_codes[:], words_all[:].bitcast(U32).indirect(offs_sb[:]))
+        nc.vector.tensor_copy(x_plane[:], scales_all[:].indirect(offs_sb[:]))
+
+        def dealt(grouped, m0, m1):
+            return grouped[:].rearrange("p (t m j) -> p m j t", t=PACK, j=PACK)[:, m0:m1]
+
+        def rows_of(raw):
+            return raw[:].rearrange("p j (m t) -> p m j t", t=PACK)
+
+        def mx_tiles(name, width):
+            codes = sb.tile([P, width], U32, name=name + "_codes", align_bytes=64)
+            plane = sb.tile([P, width], U8, name=name + "_plane", align_bytes=64)
+            return codes, plane
+
+        def product(acc, w_mx, tile_no, act_mx, atoms=slice(None)):
+            cols = slice(tile_no * P, (tile_no + 1) * P)
+            nc.tensor.matmul_mx(
+                out=acc,
+                lhsT=w_mx[0][:, cols].bitcast(FP8X4),
+                lhsT_scale=w_mx[1][:, cols],
+                rhs=act_mx[0][:, atoms].bitcast(FP8X4),
+                rhs_scale=act_mx[1][:, atoms],
+                start=True,
+                stop=True,
+            )
+
+        x_mx = (x_codes, x_plane)
+
+        w3_grouped = sb.tile([P, PACK * H], BF16, name="w3_grouped", align_bytes=64)
+        nc.scalar.copy(dealt(w3_grouped, 0, P // 2), rows_of(w3_raw[0]))
+        nc.vector.tensor_copy(dealt(w3_grouped, P // 2, P // 2 + 44), rows_of(w3_raw[1])[:, :44])
+        nc.scalar.copy(dealt(w3_grouped, P // 2 + 44, P), rows_of(w3_raw[1])[:, 44:])
+        w3_mx = mx_tiles("w3", H)
+        for t in range(PACK):
+            cols = slice(t * P, (t + 1) * P)
+            nc.vector.quantize_mx(
+                out=w3_mx[0][:, cols].bitcast(FP8X4),
+                scales=w3_mx[1][:, cols],
+                in_=w3_grouped[:, t * PACK * P : (t + 1) * PACK * P],
+            )
+            acc = bank(t, "q_acc%d" % t)
+            if t == 0:
+                other = bank(4, "q_acc_other")
+                low, high = slice(0, S // 2), slice(S // 2, S)
+                product(acc[:, low], w3_mx, t, x_mx, low)
+                product(other[:, low], w3_mx, t, x_mx, high)
+                nc.scalar.copy(q_win[t][:, low], acc[:, low])
+                nc.vector.tensor_copy(q_win[t][:, high], other[:, low])
+            else:
+                product(acc[:], w3_mx, t, x_mx)
+                nc.scalar.copy(q_win[t][:, :S], acc[:])
+
+        along = []
+
+        def along_directions(t, tag):
+            both = sb.tile([P, 2, S], F32, name="along%d" % t, tag=tag, align_bytes=64)
+            nc.vector.tensor_tensor(both[:, 0, :], q_win[t][:].indirect(p1_sb[:]), dir1_sb[:], MULT)
+            nc.vector.tensor_tensor(both[:, 1, :], q_win[t][:].indirect(p2_sb[:]), dir2_sb[:], MULT)
+            along.append(both)
+
+        def quantised(name, tag):
+            grouped = sb.tile([P, PACK * H], BF16, name=name + "_grouped", tag=tag, align_bytes=64)
+            if name == "w4":
+                nc.scalar.copy(
+                    grouped[:].rearrange("p (c i j) -> p c j i", i=4, j=PACK),
+                    w_raw[name][:].rearrange("p j (c i) -> p c j i", i=4),
+                )
+            else:
+                nc.scalar.copy(dealt(grouped, 0, P), rows_of(w_raw[name]))
+            mx = mx_tiles(name, H)
+            nc.vector.quantize_mx(out=mx[0][:].bitcast(FP8X4), scales=mx[1][:], in_=grouped[:])
+            return mx
+
+        w1_mx = quantised("w1", "w1_grouped")
+        y_acc = [bank(4 + t, "y_acc%d" % t) for t in range(PACK)]
+        for t in range(PACK):
+            product(y_acc[t][:], w1_mx, t, x_mx)
+        w2_mx = quantised("w2", "late")
+        m_win = [sb.tile([P, S], F32, name="m_win%d" % t) for t in range(PACK)]
+        e_sb = [sb.tile([P, S], F32, name="e_sb%d" % t) for t in range(PACK)]
+        for t in range(PACK):
+            acc = bank(t, "e_acc%d" % t)
+            product(acc[:], w2_mx, t, x_mx)
+            nc.scalar.copy(e_sb[t][:], acc[:])
+        for t in range(PACK - 1):
+            along_directions(t, "along%d" % t)
+        along_directions(PACK - 1, "late")
+        w4_mx = quantised("w4", "w4_grouped")
+
+        out_rows = out.rearrange("(a p) n -> p a n", p=P)
+
+        def gathered(name, t, c0, width, first, second):
+            entries = slice(c0 // LIST, (c0 + width) // LIST)
+            cols = slice(c0, c0 + width)
+            nc.vector.tensor_tensor(first, m_win[t][:].indirect(p1_sb[:, entries]), along[t][:, 0, cols], ADD)
+            nc.vector.tensor_tensor(second, m_win[t][:].indirect(p2_sb[:, entries]), along[t][:, 1, cols], ADD)
+
+        def summed_by_transposes(name, c0, width, sum_banks, back_bank):
+            blocks = width // P
+            back = bank(back_bank, name + "_back")
+            for u in range(2):
+                turned = bank(sum_banks[u], name + "_sum%d" % u)
+                for e in range(2):
+                    t = 2 * u + e
+                    if c0 == 0:
+                        nc.vector.tensor_tensor(m_win[t][:], y_acc[t][:], e_sb[t][:], MULT)
+                    first = sb.tile([P, width], F32, name=name + "_first%d" % t)
+                    second = sb.tile([P, width], F32, name=name + "_second%d" % t)
+                    gathered(name, t, c0, width, first[:], second[:])
+                    for blk in range(blocks):
+                        dst = turned[:, (2 * blk + e) * P : (2 * blk + e + 1) * P]
+                        cols = slice(blk * P, (blk + 1) * P)
+                        nc.tensor.matmul(dst, first[:, cols], ident[:], is_transpose=True, start=True, stop=False)
+                        nc.tensor.matmul(dst, second[:, cols], ident[:], is_transpose=True, start=False, stop=True)
+                pairs = sb.tile([P, 2 * width], BF16, name=name + "_pairs%d" % u)
+                nc.scalar.copy(
+                    pairs[:].rearrange("j (b p e) -> j b p e", e=2, p=P),
+                    turned[:, : 2 * width].rearrange("j (b e p) -> j b p e", e=2, p=P),
+                )
+                for blk in range(blocks):
+                    nc.tensor.transpose(
+                        back[:, u * width + blk * P : u * width + (blk + 1) * P],
+                        pairs[:].bitcast(F32)[:, blk * P : (blk + 1) * P],
+                        ident[:],
+                    )
+            grouped = sb.tile([P, 2 * width], F32, name=name + "_grouped", tag=name + "_grouped", align_bytes=64)
+            nc.scalar.copy(
+                grouped[:].rearrange("p (n u) -> p n u", u=2),
+                back[:, : 2 * width].rearrange("p (u n) -> p n u", u=2),
+            )
+            return grouped[:].bitcast(BF16)
+
+        def summed_on_vector(name, c0, width):
+            first = sb.tile([P, PACK, width], F32, name=name + "_first")
+            entries = slice(c0 // LIST, (c0 + width) // LIST)
+            cols = slice(c0, c0 + width)
+            for t in range(PACK):
+                nc.vector.tensor_tensor(first[:, t, :], m_win[t][:].indirect(p1_sb[:, entries]), along[t][:, 0, cols], ADD)
+            second = sb.tile([P, PACK, width], F32, name=name + "_second", tag="za_grouped", align_bytes=64)
+            for t in range(PACK):
+                nc.vector.tensor_tensor(second[:, t, :], m_win[t][:].indirect(p2_sb[:, entries]), along[t][:, 1, cols], ADD)
+            grouped = sb.tile([P, PACK * width], BF16, name=name + "_grouped", tag="zb_grouped", align_bytes=64)
+            nc.vector.tensor_tensor(
+                grouped[:].rearrange("p (c i t) -> p c t i", i=4, t=PACK),
+                first[:].rearrange("p t (c i) -> p c t i", i=4),
+                second[:].rearrange("p t (c i) -> p c t i", i=4),
+                ADD,
+            )
+            return grouped[:]
+
+        def last_layer(name, grouped, c0, width, out_banks, on_vector):
+            z_mx = mx_tiles(name, width)
+            nc.vector.quantize_mx(out=z_mx[0][:].bitcast(FP8X4), scales=z_mx[1][:], in_=grouped)
+            per_bank = PACK // len(out_banks)
+            for no, b in enumerate(out_banks):
+                acc = bank(b, name + "_out%d" % no)
+                for a in range(per_bank):
+                    product(acc[:, a * width : (a + 1) * width], w4_mx, no * per_bank + a, z_mx)
+                staged = sb.tile([P, per_bank, width], F32, name=name + "_staged%d" % no)
+                src = acc[:, : per_bank * width].rearrange("p (a n) -> p a n", a=per_bank)
+                dst = out_rows[:, no * per_bank : (no + 1) * per_bank, c0 : c0 + width]
+                if no in on_vector:
+                    nc.vector.tensor_copy(staged[:], src)
+                else:
+                    nc.scalar.copy(staged[:], src)
+                nc.sync.dma_start(dst, staged[:])
+
+        za = summed_by_transposes("za", 0, 256, (0, 1), 2)
+        zb = summed_by_transposes("zb", 256, 128, (3, 2), 7)
+        last_layer("za", za, 0, 256, (4, 5), ())
+        last_layer("zb", zb, 256, 128, (0,), ())
+        zc = summed_on_vector("zc", 384, 128)
+        last_layer("zc", zc, 384, 128, (1, 6), (1,))

@@ -78,11 +78,11 @@ def tile_picked_painn8_none_p_kernel(
         nc.vector.tensor_copy(x_codes[:], words_all[:].bitcast(U32).indirect(offs_sb[:]))
         nc.vector.tensor_copy(x_plane[:], scales_all[:].indirect(offs_sb[:]))
 
-        def dealt(grouped, m0, m1):
-            return grouped[:].rearrange("p (t m j) -> p m j t", t=PACK, j=PACK)[:, m0:m1]
+        def dealt(grouped):
+            return grouped.rearrange("p (e m j) -> p m j e", e=2, j=PACK)
 
-        def rows_of(raw):
-            return raw[:].rearrange("p j (m t) -> p m j t", t=PACK)
+        def rows_of(raw, u):
+            return raw[:].rearrange("p j (m t) -> p m j t", t=PACK)[:, :, :, 2 * u : 2 * u + 2]
 
         def mx_tiles(name, width):
             codes = sb.tile([P, width], U32, name=name + "_codes", align_bytes=64)
@@ -103,17 +103,18 @@ def tile_picked_painn8_none_p_kernel(
 
         x_mx = (x_codes, x_plane)
 
-        w3_grouped = sb.tile([P, PACK * H], BF16, name="w3_grouped", align_bytes=64)
-        nc.scalar.copy(dealt(w3_grouped, 0, P // 2), rows_of(w3_raw[0]))
-        nc.vector.tensor_copy(dealt(w3_grouped, P // 2, P // 2 + 44), rows_of(w3_raw[1])[:, :44])
-        nc.scalar.copy(dealt(w3_grouped, P // 2 + 44, P), rows_of(w3_raw[1])[:, 44:])
+        w3_grouped = [sb.tile([P, 2 * H], BF16, name="w3_grouped%d" % u, align_bytes=64) for u in range(2)]
+        for u in range(2):
+            nc.scalar.copy(dealt(w3_grouped[u][:])[:, : P // 2], rows_of(w3_raw[0], u))
+        nc.vector.tensor_copy(dealt(w3_grouped[0][:])[:, P // 2 :], rows_of(w3_raw[1], 0))
+        nc.scalar.copy(dealt(w3_grouped[1][:])[:, P // 2 :], rows_of(w3_raw[1], 1))
         w3_mx = mx_tiles("w3", H)
         for t in range(PACK):
             cols = slice(t * P, (t + 1) * P)
             nc.vector.quantize_mx(
                 out=w3_mx[0][:, cols].bitcast(FP8X4),
                 scales=w3_mx[1][:, cols],
-                in_=w3_grouped[:, t * PACK * P : (t + 1) * PACK * P],
+                in_=w3_grouped[t // 2][:, t % 2 * PACK * P : (t % 2 + 1) * PACK * P],
             )
             acc = bank(t, "q_acc%d" % t)
             if t == 0:
@@ -127,52 +128,54 @@ def tile_picked_painn8_none_p_kernel(
                 product(acc[:], w3_mx, t, x_mx)
                 nc.scalar.copy(q_win[t][:, :S], acc[:])
 
-        along = []
-
-        def along_directions(t, tag):
-            both = sb.tile([P, 2, S], F32, name="along%d" % t, tag=tag, align_bytes=64)
-            nc.vector.tensor_tensor(both[:, 0, :], q_win[t][:].indirect(p1_sb[:]), dir1_sb[:], MULT)
-            nc.vector.tensor_tensor(both[:, 1, :], q_win[t][:].indirect(p2_sb[:]), dir2_sb[:], MULT)
-            along.append(both)
-
-        def quantised(name, tag):
-            grouped = sb.tile([P, PACK * H], BF16, name=name + "_grouped", tag=tag, align_bytes=64)
-            if name == "w4":
-                nc.scalar.copy(
-                    grouped[:].rearrange("p (c i j) -> p c j i", i=4, j=PACK),
-                    w_raw[name][:].rearrange("p j (c i) -> p c j i", i=4),
-                )
-            else:
-                nc.scalar.copy(dealt(grouped, 0, P), rows_of(w_raw[name]))
+        def hidden_weights(name):
             mx = mx_tiles(name, H)
-            nc.vector.quantize_mx(out=mx[0][:].bitcast(FP8X4), scales=mx[1][:], in_=grouped[:])
+            for u in range(2):
+                grouped = sb.tile([P, 2 * H], BF16, name=name + "_grouped%d" % u, tag=name + "_half%d" % u, align_bytes=64)
+                nc.scalar.copy(dealt(grouped[:]), rows_of(w_raw[name], u))
+                cols = slice(u * 2 * P, (u + 1) * 2 * P)
+                nc.vector.quantize_mx(out=mx[0][:, cols].bitcast(FP8X4), scales=mx[1][:, cols], in_=grouped[:])
             return mx
 
-        w1_mx = quantised("w1", "w1_grouped")
+        w1_mx = hidden_weights("w1")
         y_acc = [bank(4 + t, "y_acc%d" % t) for t in range(PACK)]
         for t in range(PACK):
             product(y_acc[t][:], w1_mx, t, x_mx)
-        w2_mx = quantised("w2", "late")
+        w2_mx = hidden_weights("w2")
         m_win = [sb.tile([P, S], F32, name="m_win%d" % t) for t in range(PACK)]
         e_sb = [sb.tile([P, S], F32, name="e_sb%d" % t) for t in range(PACK)]
         for t in range(PACK):
             acc = bank(t, "e_acc%d" % t)
             product(acc[:], w2_mx, t, x_mx)
             nc.scalar.copy(e_sb[t][:], acc[:])
-        for t in range(PACK - 1):
-            along_directions(t, "along%d" % t)
-        along_directions(PACK - 1, "late")
-        w4_mx = quantised("w4", "w4_grouped")
+
+        reused = {(2, 0): "w1_half0", (2, 1): "w1_half1", (3, 0): "w2_half0", (3, 1): "w2_half1"}
+        along = {}
+        for t in range(PACK):
+            for side, (places, direction) in enumerate(((p1_sb, dir1_sb), (p2_sb, dir2_sb))):
+                name = "along%d_%d" % (t, side)
+                along[t, side] = sb.tile([P, S], F32, name=name, tag=reused.get((t, side), name), align_bytes=64)
+                nc.vector.tensor_tensor(along[t, side][:], q_win[t][:].indirect(places[:]), direction[:], MULT)
+
+        w4_grouped = sb.tile([P, PACK * N], BF16, name="w4_grouped", align_bytes=64)
+        for half in range(2):
+            cols = slice(half * N // 4, (half + 1) * N // 4)
+            nc.scalar.copy(
+                w4_grouped[:].rearrange("p (c i j) -> p c j i", i=2, j=PACK)[:, cols],
+                w_raw["w4"][:].rearrange("p j (c i) -> p c j i", i=2)[:, cols],
+            )
+        w4_mx = mx_tiles("w4", N)
+        nc.vector.quantize_mx(out=w4_mx[0][:].bitcast(FP8X4), scales=w4_mx[1][:], in_=w4_grouped[:])
 
         out_rows = out.rearrange("(a p) n -> p a n", p=P)
 
         def gathered(name, t, c0, width, first, second):
             entries = slice(c0 // LIST, (c0 + width) // LIST)
             cols = slice(c0, c0 + width)
-            nc.vector.tensor_tensor(first, m_win[t][:].indirect(p1_sb[:, entries]), along[t][:, 0, cols], ADD)
-            nc.vector.tensor_tensor(second, m_win[t][:].indirect(p2_sb[:, entries]), along[t][:, 1, cols], ADD)
+            nc.vector.tensor_tensor(first, m_win[t][:].indirect(p1_sb[:, entries]), along[t, 0][:, cols], ADD)
+            nc.vector.tensor_tensor(second, m_win[t][:].indirect(p2_sb[:, entries]), along[t, 1][:, cols], ADD)
 
-        def summed_by_transposes(name, c0, width, sum_banks, back_bank):
+        def summed_by_transposes(name, c0, width, sum_banks, back_bank, grouped):
             blocks = width // P
             back = bank(back_bank, name + "_back")
             for u in range(2):
@@ -200,30 +203,11 @@ def tile_picked_painn8_none_p_kernel(
                         pairs[:].bitcast(F32)[:, blk * P : (blk + 1) * P],
                         ident[:],
                     )
-            grouped = sb.tile([P, 2 * width], F32, name=name + "_grouped", tag=name + "_grouped", align_bytes=64)
             nc.scalar.copy(
-                grouped[:].rearrange("p (n u) -> p n u", u=2),
+                grouped.rearrange("p (n u) -> p n u", u=2),
                 back[:, : 2 * width].rearrange("p (u n) -> p n u", u=2),
             )
-            return grouped[:].bitcast(BF16)
-
-        def summed_on_vector(name, c0, width):
-            first = sb.tile([P, PACK, width], F32, name=name + "_first")
-            entries = slice(c0 // LIST, (c0 + width) // LIST)
-            cols = slice(c0, c0 + width)
-            for t in range(PACK):
-                nc.vector.tensor_tensor(first[:, t, :], m_win[t][:].indirect(p1_sb[:, entries]), along[t][:, 0, cols], ADD)
-            second = sb.tile([P, PACK, width], F32, name=name + "_second", tag="za_grouped", align_bytes=64)
-            for t in range(PACK):
-                nc.vector.tensor_tensor(second[:, t, :], m_win[t][:].indirect(p2_sb[:, entries]), along[t][:, 1, cols], ADD)
-            grouped = sb.tile([P, PACK * width], BF16, name=name + "_grouped", tag="zb_grouped", align_bytes=64)
-            nc.vector.tensor_tensor(
-                grouped[:].rearrange("p (c i t) -> p c t i", i=4, t=PACK),
-                first[:].rearrange("p t (c i) -> p c t i", i=4),
-                second[:].rearrange("p t (c i) -> p c t i", i=4),
-                ADD,
-            )
-            return grouped[:]
+            return grouped.bitcast(BF16)
 
         def last_layer(name, grouped, c0, width, out_banks, on_vector):
             z_mx = mx_tiles(name, width)
@@ -242,9 +226,28 @@ def tile_picked_painn8_none_p_kernel(
                     nc.scalar.copy(staged[:], src)
                 nc.sync.dma_start(dst, staged[:])
 
-        za = summed_by_transposes("za", 0, 256, (0, 1), 2)
-        zb = summed_by_transposes("zb", 256, 128, (3, 2), 7)
-        last_layer("za", za, 0, 256, (4, 5), ())
-        last_layer("zb", zb, 256, 128, (0,), ())
-        zc = summed_on_vector("zc", 384, 128)
-        last_layer("zc", zc, 384, 128, (1, 6), (1,))
+        half = S // 2
+        first = sb.tile([P, PACK * half], F32, name="zc_first")
+        second = sb.tile([P, PACK * half], F32, name="zc_second", align_bytes=64)
+        za = summed_by_transposes("za", 0, half, (0, 1), 2, second[:, 2 * half :])
+        last_layer("za", za, 0, half, (4, 5), ())
+        entries = slice(half // LIST, S // LIST)
+        for side, (places, summed) in enumerate(((p1_sb, first), (p2_sb, second))):
+            for t in range(PACK):
+                nc.vector.tensor_tensor(
+                    summed[:, t * half : (t + 1) * half],
+                    m_win[t][:].indirect(places[:, entries]),
+                    along[t, side][:, half:],
+                    ADD,
+                )
+        grouped = [sb.tile([P, PACK * P], BF16, name="zc_grouped%d" % h, align_bytes=64) for h in range(2)]
+        for h in range(2):
+            pairs = slice(h * P // 2, (h + 1) * P // 2)
+            nc.vector.tensor_tensor(
+                grouped[h][:].rearrange("p (c i t) -> p c t i", i=2, t=PACK),
+                first[:].rearrange("p (t c i) -> p c t i", i=2, t=PACK)[:, pairs],
+                second[:].rearrange("p (t c i) -> p c t i", i=2, t=PACK)[:, pairs],
+                ADD,
+            )
+        last_layer("zb", grouped[0][:], half, P, (0, 3), (1,))
+        last_layer("zc", grouped[1][:], half + P, P, (1, 6), (1,))

@@ -43,26 +43,21 @@ def tile_picked_painn8_none_p_kernel(
 
         nc.sync.dma_start(words_all[:], x_words[0].rearrange("p n t -> p (n t)").bitcast(I32))
         nc.sync.dma_start(offs_sb[:], offs)
+        nc.sync.dma_start(p1_sb[:], p1)
         for quad in range(4):
             nc.sync.dma_start(
                 scales_all[32 * quad : 32 * quad + 4, :].bitcast(I32),
                 x_scales[0, 4 * quad : 4 * quad + 4, :].bitcast(I32),
             )
-        w3_rows = w3.rearrange("(p j) c -> p j c", j=PACK)
-        w3_raw = []
-        for half in range(2):
-            raw = sb.tile([P, PACK, H // 2], F32, name="w3_raw%d" % half)
-            nc.sync.dma_start(raw[:], w3_rows[:, :, half * (H // 2) : (half + 1) * (H // 2)])
-            w3_raw.append(raw)
+        w_raw = {"w3": sb.tile([P, PACK, H], F32, name="w3_raw")}
+        nc.sync.dma_start(w_raw["w3"][:], w3.rearrange("(p j) c -> p j c", j=PACK))
         dir1_sb = sb.tile([P, S], F32, name="dir1_sb")
         dir2_sb = sb.tile([P, S], F32, name="dir2_sb")
-        nc.sync.dma_start(p1_sb[:], p1)
         nc.sync.dma_start(dir1_sb[:], dir1)
         nc.sync.dma_start(p2_sb[:], p2)
         nc.sync.dma_start(dir2_sb[:], dir2)
-        w_raw = {}
         for name, w in (("w1", w1), ("w2", w2), ("w4", w4)):
-            w_raw[name] = sb.tile([P, PACK, H], F32, name=name + "_raw")
+            w_raw[name] = sb.tile([P, PACK, H], F32, name=name + "_raw", tag=name + "_raw")
             nc.sync.dma_start(w_raw[name][:], w.rearrange("(p j) c -> p j c", j=PACK))
 
         ident = sb.tile([P, P], F32, name="ident")
@@ -104,10 +99,9 @@ def tile_picked_painn8_none_p_kernel(
         x_mx = (x_codes, x_plane)
 
         w3_grouped = [sb.tile([P, 2 * H], BF16, name="w3_grouped%d" % u, align_bytes=64) for u in range(2)]
-        for u in range(2):
-            nc.scalar.copy(dealt(w3_grouped[u][:])[:, : P // 2], rows_of(w3_raw[0], u))
-        nc.vector.tensor_copy(dealt(w3_grouped[0][:])[:, P // 2 :], rows_of(w3_raw[1], 0))
-        nc.scalar.copy(dealt(w3_grouped[1][:])[:, P // 2 :], rows_of(w3_raw[1], 1))
+        nc.vector.tensor_copy(dealt(w3_grouped[0][:])[:, :80], rows_of(w_raw["w3"], 0)[:, :80])
+        nc.scalar.copy(dealt(w3_grouped[0][:])[:, 80:], rows_of(w_raw["w3"], 0)[:, 80:])
+        nc.scalar.copy(dealt(w3_grouped[1][:]), rows_of(w_raw["w3"], 1))
         w3_mx = mx_tiles("w3", H)
         for t in range(PACK):
             cols = slice(t * P, (t + 1) * P)
@@ -122,19 +116,18 @@ def tile_picked_painn8_none_p_kernel(
                 low, high = slice(0, S // 2), slice(S // 2, S)
                 product(acc[:, low], w3_mx, t, x_mx, low)
                 product(other[:, low], w3_mx, t, x_mx, high)
-                nc.scalar.copy(q_win[t][:, low], acc[:, low])
-                nc.vector.tensor_copy(q_win[t][:, high], other[:, low])
+                nc.vector.tensor_copy(q_win[t][:, low], acc[:, low])
+                nc.scalar.copy(q_win[t][:, high], other[:, low])
             else:
                 product(acc[:], w3_mx, t, x_mx)
                 nc.scalar.copy(q_win[t][:, :S], acc[:])
 
         def hidden_weights(name):
-            mx = mx_tiles(name, H)
+            grouped = sb.tile([P, PACK * H], BF16, name=name + "_grouped", align_bytes=64)
             for u in range(2):
-                grouped = sb.tile([P, 2 * H], BF16, name=name + "_grouped%d" % u, tag=name + "_half%d" % u, align_bytes=64)
-                nc.scalar.copy(dealt(grouped[:]), rows_of(w_raw[name], u))
-                cols = slice(u * 2 * P, (u + 1) * 2 * P)
-                nc.vector.quantize_mx(out=mx[0][:, cols].bitcast(FP8X4), scales=mx[1][:, cols], in_=grouped[:])
+                nc.scalar.copy(dealt(grouped[:, u * 2 * H : (u + 1) * 2 * H]), rows_of(w_raw[name], u))
+            mx = mx_tiles(name, H)
+            nc.vector.quantize_mx(out=mx[0][:].bitcast(FP8X4), scales=mx[1][:], in_=grouped[:])
             return mx
 
         w1_mx = hidden_weights("w1")
@@ -149,13 +142,14 @@ def tile_picked_painn8_none_p_kernel(
             product(acc[:], w2_mx, t, x_mx)
             nc.scalar.copy(e_sb[t][:], acc[:])
 
-        reused = {(2, 0): "w1_half0", (2, 1): "w1_half1", (3, 0): "w2_half0", (3, 1): "w2_half1"}
         along = {}
-        for t in range(PACK):
+        for t, tag in enumerate(("along0", "along1", "w1_raw", "w2_raw")):
+            both = sb.tile([P, 2 * S], F32, name="along%d" % t, tag=tag)
             for side, (places, direction) in enumerate(((p1_sb, dir1_sb), (p2_sb, dir2_sb))):
-                name = "along%d_%d" % (t, side)
-                along[t, side] = sb.tile([P, S], F32, name=name, tag=reused.get((t, side), name), align_bytes=64)
-                nc.vector.tensor_tensor(along[t, side][:], q_win[t][:].indirect(places[:]), direction[:], MULT)
+                along[t, side] = both[:, side * S : (side + 1) * S]
+                nc.vector.tensor_tensor(along[t, side], q_win[t][:].indirect(places[:]), direction[:], MULT)
+        for t in range(PACK):
+            nc.vector.tensor_tensor(m_win[t][:], y_acc[t][:], e_sb[t][:], MULT)
 
         w4_grouped = sb.tile([P, PACK * N], BF16, name="w4_grouped", align_bytes=64)
         for half in range(2):
@@ -182,8 +176,6 @@ def tile_picked_painn8_none_p_kernel(
                 turned = bank(sum_banks[u], name + "_sum%d" % u)
                 for e in range(2):
                     t = 2 * u + e
-                    if c0 == 0:
-                        nc.vector.tensor_tensor(m_win[t][:], y_acc[t][:], e_sb[t][:], MULT)
                     first = sb.tile([P, width], F32, name=name + "_first%d" % t)
                     second = sb.tile([P, width], F32, name=name + "_second%d" % t)
                     gathered(name, t, c0, width, first[:], second[:])
@@ -228,8 +220,9 @@ def tile_picked_painn8_none_p_kernel(
 
         half = S // 2
         first = sb.tile([P, PACK * half], F32, name="zc_first")
-        second = sb.tile([P, PACK * half], F32, name="zc_second", align_bytes=64)
-        za = summed_by_transposes("za", 0, half, (0, 1), 2, second[:, 2 * half :])
+        second = sb.tile([P, PACK * half], F32, name="zc_second")
+        za_words = sb.tile([P, 2 * half], F32, name="za_words", tag="z_grouped0", align_bytes=64)
+        za = summed_by_transposes("za", 0, half, (0, 1), 2, za_words[:])
         last_layer("za", za, 0, half, (4, 5), ())
         entries = slice(half // LIST, S // LIST)
         for side, (places, summed) in enumerate(((p1_sb, first), (p2_sb, second))):
@@ -240,14 +233,15 @@ def tile_picked_painn8_none_p_kernel(
                     along[t, side][:, half:],
                     ADD,
                 )
-        grouped = [sb.tile([P, PACK * P], BF16, name="zc_grouped%d" % h, align_bytes=64) for h in range(2)]
+        z_rest = sb.tile([P, PACK * half], BF16, name="z_rest", tag="z_grouped0", align_bytes=64)
+        grouped = [z_rest[:, h * PACK * P : (h + 1) * PACK * P] for h in range(2)]
         for h in range(2):
             pairs = slice(h * P // 2, (h + 1) * P // 2)
             nc.vector.tensor_tensor(
-                grouped[h][:].rearrange("p (c i t) -> p c t i", i=2, t=PACK),
+                grouped[h].rearrange("p (c i t) -> p c t i", i=2, t=PACK),
                 first[:].rearrange("p (t c i) -> p c t i", i=2, t=PACK)[:, pairs],
                 second[:].rearrange("p (t c i) -> p c t i", i=2, t=PACK)[:, pairs],
                 ADD,
             )
-        last_layer("zb", grouped[0][:], half, P, (0, 3), (1,))
-        last_layer("zc", grouped[1][:], half + P, P, (1, 6), (1,))
+        last_layer("zb", grouped[0], half, P, (0, 3), (1,))
+        last_layer("zc", grouped[1], half + P, P, (1, 6), (1,))

@@ -19,6 +19,11 @@ ADD = mybir.AluOpType.add
 P = 128
 PACK = 4
 LIST = 16
+BANK = 512
+QUADRANTS = 4
+HALF = S // 2
+VECTOR_SHARE = 80
+WARM_UP_PASSES = 3
 
 
 def tile_picked_painn8_none_p_kernel(
@@ -31,7 +36,7 @@ def tile_picked_painn8_none_p_kernel(
         psum = ctx.enter_context(tc.psum_pool(name="psum", bufs=1))
 
         def bank(b, name):
-            return psum.tile([P, 512], F32, tag="bank%d" % b, name=name)
+            return psum.tile([P, BANK], F32, tag="bank%d" % b, name=name)
 
         offs_sb = lists.tile([P, S // LIST], U16, name="offs_sb")
         p1_sb = lists.tile([P, S // LIST], U16, name="p1_sb")
@@ -44,7 +49,7 @@ def tile_picked_painn8_none_p_kernel(
         nc.sync.dma_start(words_all[:], x_words[0].rearrange("p n t -> p (n t)").bitcast(I32))
         nc.sync.dma_start(offs_sb[:], offs)
         nc.sync.dma_start(p1_sb[:], p1)
-        for quad in range(4):
+        for quad in range(QUADRANTS):
             nc.sync.dma_start(
                 scales_all[32 * quad : 32 * quad + 4, :].bitcast(I32),
                 x_scales[0, 4 * quad : 4 * quad + 4, :].bitcast(I32),
@@ -72,6 +77,7 @@ def tile_picked_painn8_none_p_kernel(
         x_plane = sb.tile([P, S], U8, name="x_plane", align_bytes=64)
         nc.vector.tensor_copy(x_codes[:], words_all[:].bitcast(U32).indirect(offs_sb[:]))
         nc.vector.tensor_copy(x_plane[:], scales_all[:].indirect(offs_sb[:]))
+        x_mx = (x_codes, x_plane)
 
         def dealt(grouped):
             return grouped.rearrange("p (e m j) -> p m j e", e=2, j=PACK)
@@ -96,11 +102,9 @@ def tile_picked_painn8_none_p_kernel(
                 stop=True,
             )
 
-        x_mx = (x_codes, x_plane)
-
         w3_grouped = [sb.tile([P, 2 * H], BF16, name="w3_grouped%d" % u, align_bytes=64) for u in range(2)]
-        nc.vector.tensor_copy(dealt(w3_grouped[0][:])[:, :80], rows_of(w_raw["w3"], 0)[:, :80])
-        nc.scalar.copy(dealt(w3_grouped[0][:])[:, 80:], rows_of(w_raw["w3"], 0)[:, 80:])
+        nc.vector.tensor_copy(dealt(w3_grouped[0][:])[:, :VECTOR_SHARE], rows_of(w_raw["w3"], 0)[:, :VECTOR_SHARE])
+        nc.scalar.copy(dealt(w3_grouped[0][:])[:, VECTOR_SHARE:], rows_of(w_raw["w3"], 0)[:, VECTOR_SHARE:])
         nc.scalar.copy(dealt(w3_grouped[1][:]), rows_of(w_raw["w3"], 1))
         w3_mx = mx_tiles("w3", H)
         for t in range(PACK):
@@ -112,8 +116,8 @@ def tile_picked_painn8_none_p_kernel(
             )
             acc = bank(t, "q_acc%d" % t)
             if t == 0:
-                other = bank(4, "q_acc_other")
-                low, high = slice(0, S // 2), slice(S // 2, S)
+                other = bank(PACK, "q_acc_other")
+                low, high = slice(0, HALF), slice(HALF, S)
                 product(acc[:, low], w3_mx, t, x_mx, low)
                 product(other[:, low], w3_mx, t, x_mx, high)
                 nc.vector.tensor_copy(q_win[t][:, low], acc[:, low])
@@ -131,7 +135,7 @@ def tile_picked_painn8_none_p_kernel(
             return mx
 
         w1_mx = hidden_weights("w1")
-        y_acc = [bank(4 + t, "y_acc%d" % t) for t in range(PACK)]
+        y_acc = [bank(PACK + t, "y_acc%d" % t) for t in range(PACK)]
         for t in range(PACK):
             product(y_acc[t][:], w1_mx, t, x_mx)
         w2_mx = hidden_weights("w2")
@@ -148,58 +152,25 @@ def tile_picked_painn8_none_p_kernel(
             for side, (places, direction) in enumerate(((p1_sb, dir1_sb), (p2_sb, dir2_sb))):
                 along[t, side] = both[:, side * S : (side + 1) * S]
                 nc.vector.tensor_tensor(along[t, side], q_win[t][:].indirect(places[:]), direction[:], MULT)
+
         for t in range(PACK):
             nc.vector.tensor_tensor(m_win[t][:], y_acc[t][:], e_sb[t][:], MULT)
 
         w4_grouped = sb.tile([P, PACK * N], BF16, name="w4_grouped", align_bytes=64)
-        for half in range(2):
-            cols = slice(half * N // 4, (half + 1) * N // 4)
+        for part in range(2):
+            column_pairs = slice(part * N // 4, (part + 1) * N // 4)
             nc.scalar.copy(
-                w4_grouped[:].rearrange("p (c i j) -> p c j i", i=2, j=PACK)[:, cols],
-                w_raw["w4"][:].rearrange("p j (c i) -> p c j i", i=2)[:, cols],
+                w4_grouped[:].rearrange("p (c i j) -> p c j i", i=2, j=PACK)[:, column_pairs],
+                w_raw["w4"][:].rearrange("p j (c i) -> p c j i", i=2)[:, column_pairs],
             )
         w4_mx = mx_tiles("w4", N)
         nc.vector.quantize_mx(out=w4_mx[0][:].bitcast(FP8X4), scales=w4_mx[1][:], in_=w4_grouped[:])
 
         out_rows = out.rearrange("(a p) n -> p a n", p=P)
 
-        def gathered(name, t, c0, width, first, second):
-            entries = slice(c0 // LIST, (c0 + width) // LIST)
-            cols = slice(c0, c0 + width)
-            nc.vector.tensor_tensor(first, m_win[t][:].indirect(p1_sb[:, entries]), along[t, 0][:, cols], ADD)
-            nc.vector.tensor_tensor(second, m_win[t][:].indirect(p2_sb[:, entries]), along[t, 1][:, cols], ADD)
-
-        def summed_by_transposes(name, c0, width, sum_banks, back_bank, grouped):
-            blocks = width // P
-            back = bank(back_bank, name + "_back")
-            for u in range(2):
-                turned = bank(sum_banks[u], name + "_sum%d" % u)
-                for e in range(2):
-                    t = 2 * u + e
-                    first = sb.tile([P, width], F32, name=name + "_first%d" % t)
-                    second = sb.tile([P, width], F32, name=name + "_second%d" % t)
-                    gathered(name, t, c0, width, first[:], second[:])
-                    for blk in range(blocks):
-                        dst = turned[:, (2 * blk + e) * P : (2 * blk + e + 1) * P]
-                        cols = slice(blk * P, (blk + 1) * P)
-                        nc.tensor.matmul(dst, first[:, cols], ident[:], is_transpose=True, start=True, stop=False)
-                        nc.tensor.matmul(dst, second[:, cols], ident[:], is_transpose=True, start=False, stop=True)
-                pairs = sb.tile([P, 2 * width], BF16, name=name + "_pairs%d" % u)
-                nc.scalar.copy(
-                    pairs[:].rearrange("j (b p e) -> j b p e", e=2, p=P),
-                    turned[:, : 2 * width].rearrange("j (b e p) -> j b p e", e=2, p=P),
-                )
-                for blk in range(blocks):
-                    nc.tensor.transpose(
-                        back[:, u * width + blk * P : u * width + (blk + 1) * P],
-                        pairs[:].bitcast(F32)[:, blk * P : (blk + 1) * P],
-                        ident[:],
-                    )
-            nc.scalar.copy(
-                grouped.rearrange("p (n u) -> p n u", u=2),
-                back[:, : 2 * width].rearrange("p (u n) -> p n u", u=2),
-            )
-            return grouped.bitcast(BF16)
+        def fetch_and_add(summed, t, side, c0):
+            places = (p1_sb, p2_sb)[side][:, c0 // LIST : (c0 + HALF) // LIST]
+            nc.vector.tensor_tensor(summed, m_win[t][:].indirect(places), along[t, side][:, c0 : c0 + HALF], ADD)
 
         def last_layer(name, grouped, c0, width, out_banks, on_vector):
             z_mx = mx_tiles(name, width)
@@ -218,30 +189,63 @@ def tile_picked_painn8_none_p_kernel(
                     nc.scalar.copy(staged[:], src)
                 nc.sync.dma_start(dst, staged[:])
 
-        half = S // 2
-        first = sb.tile([P, PACK * half], F32, name="zc_first")
-        second = sb.tile([P, PACK * half], F32, name="zc_second")
-        za_words = sb.tile([P, 2 * half], F32, name="za_words", tag="z_grouped0", align_bytes=64)
-        za = summed_by_transposes("za", 0, half, (0, 1), 2, za_words[:])
-        last_layer("za", za, 0, half, (4, 5), ())
-        entries = slice(half // LIST, S // LIST)
-        for side, (places, summed) in enumerate(((p1_sb, first), (p2_sb, second))):
-            for t in range(PACK):
-                nc.vector.tensor_tensor(
-                    summed[:, t * half : (t + 1) * half],
-                    m_win[t][:].indirect(places[:, entries]),
-                    along[t, side][:, half:],
-                    ADD,
+        rest_sums = [sb.tile([P, PACK * HALF], F32, name=name) for name in ("zc_first", "zc_second")]
+        za_words = sb.tile([P, 2 * HALF], F32, name="za_words", tag="z_grouped0", align_bytes=64)
+
+        blocks = HALF // P
+        back = bank(2, "za_back")
+        for u in range(2):
+            turned = bank(u, "za_sum%d" % u)
+            for e in range(2):
+                t = 2 * u + e
+                sums = [sb.tile([P, HALF], F32, name=name % t) for name in ("za_first%d", "za_second%d")]
+                for side in range(2):
+                    fetch_and_add(sums[side][:], t, side, 0)
+                for blk in range(blocks):
+                    dst = turned[:, (2 * blk + e) * P : (2 * blk + e + 1) * P]
+                    for side in range(2):
+                        nc.tensor.matmul(
+                            dst,
+                            sums[side][:, blk * P : (blk + 1) * P],
+                            ident[:],
+                            is_transpose=True,
+                            start=(side == 0),
+                            stop=(side == 1),
+                        )
+            pairs = sb.tile([P, 2 * HALF], BF16, name="za_pairs%d" % u)
+            nc.scalar.copy(
+                pairs[:].rearrange("j (b p e) -> j b p e", e=2, p=P),
+                turned[:, : 2 * HALF].rearrange("j (b e p) -> j b p e", e=2, p=P),
+            )
+            for blk in range(blocks):
+                nc.tensor.transpose(
+                    back[:, u * HALF + blk * P : u * HALF + (blk + 1) * P],
+                    pairs[:].bitcast(F32)[:, blk * P : (blk + 1) * P],
+                    ident[:],
                 )
-        z_rest = sb.tile([P, PACK * half], BF16, name="z_rest", tag="z_grouped0", align_bytes=64)
-        grouped = [z_rest[:, h * PACK * P : (h + 1) * PACK * P] for h in range(2)]
-        for h in range(2):
-            pairs = slice(h * P // 2, (h + 1) * P // 2)
+        nc.scalar.copy(
+            za_words[:].rearrange("p (n u) -> p n u", u=2),
+            back[:, : 2 * HALF].rearrange("p (u n) -> p n u", u=2),
+        )
+
+        unread = bank(2, "warm_up")
+        for t in range(WARM_UP_PASSES):
+            product(unread[:], w1_mx, t, x_mx)
+
+        last_layer("za", za_words[:].bitcast(BF16), 0, HALF, (4, 5), ())
+
+        for side in range(2):
+            for t in range(PACK):
+                fetch_and_add(rest_sums[side][:, t * HALF : (t + 1) * HALF], t, side, HALF)
+        z_rest = sb.tile([P, PACK * HALF], BF16, name="z_rest", tag="z_grouped0", align_bytes=64)
+        rest_grouped = [z_rest[:, blk * PACK * P : (blk + 1) * PACK * P] for blk in range(blocks)]
+        for blk in range(blocks):
+            atom_pairs = slice(blk * P // 2, (blk + 1) * P // 2)
             nc.vector.tensor_tensor(
-                grouped[h].rearrange("p (c i t) -> p c t i", i=2, t=PACK),
-                first[:].rearrange("p (t c i) -> p c t i", i=2, t=PACK)[:, pairs],
-                second[:].rearrange("p (t c i) -> p c t i", i=2, t=PACK)[:, pairs],
+                rest_grouped[blk].rearrange("p (c i t) -> p c t i", i=2, t=PACK),
+                rest_sums[0][:].rearrange("p (t c i) -> p c t i", i=2, t=PACK)[:, atom_pairs],
+                rest_sums[1][:].rearrange("p (t c i) -> p c t i", i=2, t=PACK)[:, atom_pairs],
                 ADD,
             )
-        last_layer("zb", grouped[0], half, P, (0, 3), (1,))
-        last_layer("zc", grouped[1], half + P, P, (1, 6), (1,))
+        last_layer("zb", rest_grouped[0], HALF, P, (0, 3), (1,))
+        last_layer("zc", rest_grouped[1], HALF + P, P, (1, 6), (1,))

@@ -21,9 +21,6 @@ PACK = 4
 LIST = 16
 BANK = 512
 QUADRANTS = 4
-HALF = S // 2
-VECTOR_SHARE = 80
-WARM_UP_PASSES = 3
 
 
 def tile_picked_painn8_none_p_kernel(
@@ -38,40 +35,40 @@ def tile_picked_painn8_none_p_kernel(
         def bank(b, name):
             return psum.tile([P, BANK], F32, tag="bank%d" % b, name=name)
 
+        def by_rows(w):
+            return w.rearrange("(p j) c -> p j c", j=PACK)
+
         offs_sb = lists.tile([P, S // LIST], U16, name="offs_sb")
         p1_sb = lists.tile([P, S // LIST], U16, name="p1_sb")
         p2_sb = lists.tile([P, S // LIST], U16, name="p2_sb")
+        places = (p1_sb, p2_sb)
 
         words_all = sb.tile([P, T], I32, name="words_all", align_bytes=64)
         scales_all = sb.tile([P, T], U8, name="scales_all", align_bytes=64)
-        nc.vector.memset(scales_all[:].bitcast(I32), 0)
+        nc.gpsimd.memset(scales_all[:].bitcast(I32), 0)
 
+        w3_raw = [sb.tile([P, PACK, H // 2], F32, name="w3_raw%d" % h) for h in range(2)]
         nc.sync.dma_start(words_all[:], x_words[0].rearrange("p n t -> p (n t)").bitcast(I32))
         nc.sync.dma_start(offs_sb[:], offs)
-        nc.sync.dma_start(p1_sb[:], p1)
+        nc.sync.dma_start(w3_raw[0][:], by_rows(w3)[:, :, : H // 2])
         for quad in range(QUADRANTS):
             nc.sync.dma_start(
                 scales_all[32 * quad : 32 * quad + 4, :].bitcast(I32),
                 x_scales[0, 4 * quad : 4 * quad + 4, :].bitcast(I32),
             )
-        w_raw = {"w3": sb.tile([P, PACK, H], F32, name="w3_raw")}
-        nc.sync.dma_start(w_raw["w3"][:], w3.rearrange("(p j) c -> p j c", j=PACK))
-        dir1_sb = sb.tile([P, S], F32, name="dir1_sb")
-        dir2_sb = sb.tile([P, S], F32, name="dir2_sb")
-        nc.sync.dma_start(dir1_sb[:], dir1)
-        nc.sync.dma_start(p2_sb[:], p2)
-        nc.sync.dma_start(dir2_sb[:], dir2)
-        for name, w in (("w1", w1), ("w2", w2), ("w4", w4)):
-            w_raw[name] = sb.tile([P, PACK, H], F32, name=name + "_raw", tag=name + "_raw")
-            nc.sync.dma_start(w_raw[name][:], w.rearrange("(p j) c -> p j c", j=PACK))
+        nc.sync.dma_start(w3_raw[1][:], by_rows(w3)[:, :, H // 2 :])
+        directions = [sb.tile([P, S], F32, name="dir%d_sb" % (side + 1)) for side in range(2)]
+        for side, (place_list, direction) in enumerate(((p1, dir1), (p2, dir2))):
+            nc.sync.dma_start(places[side][:], place_list)
+            nc.sync.dma_start(directions[side][:], direction)
+        w1_raw, w2_raw, w4_raw = [
+            sb.tile([P, PACK, H], F32, name=name, tag=name) for name in ("w1_raw", "w2_raw", "w4_raw")
+        ]
+        for raw, w in ((w1_raw, w1), (w2_raw, w2), (w4_raw, w4)):
+            nc.sync.dma_start(raw[:], by_rows(w))
 
         ident = sb.tile([P, P], F32, name="ident")
         make_identity(nc, ident[:])
-
-        q_win = [sb.tile([P, 2 * S], F32, name="q_win%d" % t) for t in range(PACK)]
-        nc.vector.memset(q_win[0][:, S:], 0.0)
-        for t in range(1, PACK):
-            nc.scalar.copy(q_win[t][:, S:], q_win[0][:, S:])
 
         x_codes = sb.tile([P, S], U32, name="x_codes", align_bytes=64)
         x_plane = sb.tile([P, S], U8, name="x_plane", align_bytes=64)
@@ -90,6 +87,10 @@ def tile_picked_painn8_none_p_kernel(
             plane = sb.tile([P, width], U8, name=name + "_plane", align_bytes=64)
             return codes, plane
 
+        def quantise(mx, first, grouped):
+            cols = slice(first, first + grouped.shape[1] // PACK)
+            nc.vector.quantize_mx(out=mx[0][:, cols].bitcast(FP8X4), scales=mx[1][:, cols], in_=grouped)
+
         def product(acc, w_mx, tile_no, act_mx, atoms=slice(None)):
             cols = slice(tile_no * P, (tile_no + 1) * P)
             nc.tensor.matmul_mx(
@@ -102,79 +103,123 @@ def tile_picked_painn8_none_p_kernel(
                 stop=True,
             )
 
+        q_win = [sb.tile([P, 2 * S], F32, name="q_win%d" % t) for t in range(PACK)]
+        for t in range(PACK):
+            nc.vector.memset(q_win[t][:, S:], 0.0)
         w3_grouped = [sb.tile([P, 2 * H], BF16, name="w3_grouped%d" % u, align_bytes=64) for u in range(2)]
-        nc.vector.tensor_copy(dealt(w3_grouped[0][:])[:, :VECTOR_SHARE], rows_of(w_raw["w3"], 0)[:, :VECTOR_SHARE])
-        nc.scalar.copy(dealt(w3_grouped[0][:])[:, VECTOR_SHARE:], rows_of(w_raw["w3"], 0)[:, VECTOR_SHARE:])
-        nc.scalar.copy(dealt(w3_grouped[1][:]), rows_of(w_raw["w3"], 1))
+        spare = [grouped[:] for grouped in w3_grouped]
+
+        half_m = P // 2
         w3_mx = mx_tiles("w3", H)
-        for t in range(PACK):
-            cols = slice(t * P, (t + 1) * P)
-            nc.vector.quantize_mx(
-                out=w3_mx[0][:, cols].bitcast(FP8X4),
-                scales=w3_mx[1][:, cols],
-                in_=w3_grouped[t // 2][:, t % 2 * PACK * P : (t % 2 + 1) * PACK * P],
-            )
+        for u in range(2):
+            nc.scalar.copy(dealt(spare[u])[:, :half_m], rows_of(w3_raw[0], u))
+        nc.vector.tensor_copy(dealt(spare[0])[:, half_m:], rows_of(w3_raw[1], 0))
+        nc.scalar.copy(dealt(spare[1])[:, half_m:], rows_of(w3_raw[1], 1))
+        quantise(w3_mx, 0, spare[0][:, : PACK * P])
+        quantise(w3_mx, P, spare[0][:, PACK * P :])
+        low, high = slice(0, S // 2), slice(S // 2, S)
+        q_low, q_high = bank(0, "q_low"), bank(4, "q_high")
+        product(q_low[:, low], w3_mx, 0, x_mx, low)
+        product(q_high[:, low], w3_mx, 0, x_mx, high)
+        nc.vector.tensor_copy(q_win[0][:, low], q_low[:, low])
+        nc.scalar.copy(q_win[0][:, high], q_high[:, low])
+        quantise(w3_mx, 2 * P, spare[1])
+        for t in range(1, PACK):
             acc = bank(t, "q_acc%d" % t)
-            if t == 0:
-                other = bank(PACK, "q_acc_other")
-                low, high = slice(0, HALF), slice(HALF, S)
-                product(acc[:, low], w3_mx, t, x_mx, low)
-                product(other[:, low], w3_mx, t, x_mx, high)
-                nc.vector.tensor_copy(q_win[t][:, low], acc[:, low])
-                nc.scalar.copy(q_win[t][:, high], other[:, low])
-            else:
-                product(acc[:], w3_mx, t, x_mx)
-                nc.scalar.copy(q_win[t][:, :S], acc[:])
+            product(acc[:], w3_mx, t, x_mx)
+            nc.scalar.copy(q_win[t][:, :S], acc[:])
 
-        def hidden_weights(name):
-            grouped = sb.tile([P, PACK * H], BF16, name=name + "_grouped", align_bytes=64)
+        w1_mx, w2_mx = mx_tiles("w1", H), mx_tiles("w2", H)
+        w1_grouped = sb.tile([P, PACK * H], BF16, name="w1_grouped", align_bytes=64)
+        w2_grouped = sb.tile([P, PACK * H], BF16, name="w2_grouped", align_bytes=64)
+        pair_cols = [slice(u * 2 * H, (u + 1) * 2 * H) for u in range(2)]
+        for raw, grouped in ((w1_raw, w1_grouped), (w2_raw, w2_grouped)):
             for u in range(2):
-                nc.scalar.copy(dealt(grouped[:, u * 2 * H : (u + 1) * 2 * H]), rows_of(w_raw[name], u))
-            mx = mx_tiles(name, H)
-            nc.vector.quantize_mx(out=mx[0][:].bitcast(FP8X4), scales=mx[1][:], in_=grouped[:])
-            return mx
-
-        w1_mx = hidden_weights("w1")
-        y_acc = [bank(PACK + t, "y_acc%d" % t) for t in range(PACK)]
+                nc.scalar.copy(dealt(grouped[:, pair_cols[u]]), rows_of(raw, u))
+        quantise(w1_mx, 0, w1_grouped[:])
+        for u in range(2):
+            quantise(w2_mx, 2 * u * P, w2_grouped[:, pair_cols[u]])
+        y_sb = [sb.tile([P, S], F32, name="y_sb%d" % t) for t in range(PACK)]
         for t in range(PACK):
-            product(y_acc[t][:], w1_mx, t, x_mx)
-        w2_mx = hidden_weights("w2")
-        m_win = [sb.tile([P, S], F32, name="m_win%d" % t) for t in range(PACK)]
-        e_sb = [sb.tile([P, S], F32, name="e_sb%d" % t) for t in range(PACK)]
+            acc = bank(PACK + t, "y_acc%d" % t)
+            product(acc[:], w1_mx, t, x_mx)
+            nc.scalar.copy(y_sb[t][:], acc[:])
+        e_acc = [bank(t, "e_acc%d" % t) for t in range(PACK)]
         for t in range(PACK):
-            acc = bank(t, "e_acc%d" % t)
-            product(acc[:], w2_mx, t, x_mx)
-            nc.scalar.copy(e_sb[t][:], acc[:])
+            product(e_acc[t][:], w2_mx, t, x_mx)
 
+        free = sb.tile([P, 5 * S], F32, name="along_free")
+        after_w1 = sb.tile([P, 2 * S], F32, name="along_after_w1", tag="w1_raw")
+        after_w2 = sb.tile([P, S], F32, name="along_after_w2", tag="w2_raw")
+        homes = [free[:, n * S : (n + 1) * S] for n in range(5)] + [after_w1[:, :S], after_w1[:, S:], after_w2[:]]
         along = {}
-        for t, tag in enumerate(("along0", "along1", "w1_raw", "w2_raw")):
-            both = sb.tile([P, 2 * S], F32, name="along%d" % t, tag=tag)
-            for side, (places, direction) in enumerate(((p1_sb, dir1_sb), (p2_sb, dir2_sb))):
-                along[t, side] = both[:, side * S : (side + 1) * S]
-                nc.vector.tensor_tensor(along[t, side], q_win[t][:].indirect(places[:]), direction[:], MULT)
-
         for t in range(PACK):
-            nc.vector.tensor_tensor(m_win[t][:], y_acc[t][:], e_sb[t][:], MULT)
+            for side in range(2):
+                along[t, side] = homes[2 * t + side]
+                nc.vector.tensor_tensor(along[t, side], q_win[t][:].indirect(places[side][:]), directions[side][:], MULT)
 
         w4_grouped = sb.tile([P, PACK * N], BF16, name="w4_grouped", align_bytes=64)
         for part in range(2):
             column_pairs = slice(part * N // 4, (part + 1) * N // 4)
             nc.scalar.copy(
                 w4_grouped[:].rearrange("p (c i j) -> p c j i", i=2, j=PACK)[:, column_pairs],
-                w_raw["w4"][:].rearrange("p j (c i) -> p c j i", i=2)[:, column_pairs],
+                w4_raw[:].rearrange("p j (c i) -> p c j i", i=2)[:, column_pairs],
             )
-        w4_mx = mx_tiles("w4", N)
-        nc.vector.quantize_mx(out=w4_mx[0][:].bitcast(FP8X4), scales=w4_mx[1][:], in_=w4_grouped[:])
+
+        m_win = [sb.tile([P, S], F32, name="m_win%d" % t) for t in range(PACK)]
+
+        def gate(t):
+            nc.vector.tensor_tensor(m_win[t][:], e_acc[t][:], y_sb[t][:], MULT)
+
+        def fetch_and_add(summed, t, side, c0, width):
+            entries = places[side][:, c0 // LIST : (c0 + width) // LIST]
+            nc.vector.tensor_tensor(summed, m_win[t][:].indirect(entries), along[t, side][:, c0 : c0 + width], ADD)
 
         out_rows = out.rearrange("(a p) n -> p a n", p=P)
+        w4_mx = mx_tiles("w4", N)
 
-        def fetch_and_add(summed, t, side, c0):
-            places = (p1_sb, p2_sb)[side][:, c0 // LIST : (c0 + HALF) // LIST]
-            nc.vector.tensor_tensor(summed, m_win[t][:].indirect(places), along[t, side][:, c0 : c0 + HALF], ADD)
+        def turned_sums(name, c0, width, sum_banks, back_bank, pair_words, before_tile):
+            blocks = width // P
+            back = bank(back_bank, name + "_back")
+            for u in range(2):
+                turned = bank(sum_banks[u], name + "_sum%d" % u)
+                for e in range(2):
+                    t = 2 * u + e
+                    before_tile(t)
+                    sums = [sb.tile([P, width], F32, name="%s_part%d_%d" % (name, t, side)) for side in range(2)]
+                    for side in range(2):
+                        fetch_and_add(sums[side][:], t, side, c0, width)
+                    for blk in range(blocks):
+                        for side in range(2):
+                            nc.tensor.matmul(
+                                turned[:, (2 * blk + e) * P : (2 * blk + e + 1) * P],
+                                sums[side][:, blk * P : (blk + 1) * P],
+                                ident[:],
+                                is_transpose=True,
+                                start=(side == 0),
+                                stop=(side == 1),
+                            )
+                pairs = pair_words[u]
+                nc.scalar.copy(
+                    pairs.bitcast(BF16).rearrange("j (b p e) -> j b p e", e=2, p=P),
+                    turned[:, : 2 * width].rearrange("j (b e p) -> j b p e", e=2, p=P),
+                )
+                for blk in range(blocks):
+                    nc.tensor.transpose(
+                        back[:, u * width + blk * P : u * width + (blk + 1) * P],
+                        pairs[:, blk * P : (blk + 1) * P],
+                        ident[:],
+                    )
+            words = sb.tile([P, 2 * width], F32, name=name + "_words", align_bytes=64)
+            nc.scalar.copy(
+                words[:].rearrange("p (n u) -> p n u", u=2),
+                back[:, : 2 * width].rearrange("p (u n) -> p n u", u=2),
+            )
+            return words[:].bitcast(BF16)
 
         def last_layer(name, grouped, c0, width, out_banks, on_vector):
             z_mx = mx_tiles(name, width)
-            nc.vector.quantize_mx(out=z_mx[0][:].bitcast(FP8X4), scales=z_mx[1][:], in_=grouped)
+            quantise(z_mx, 0, grouped)
             per_bank = PACK // len(out_banks)
             for no, b in enumerate(out_banks):
                 acc = bank(b, name + "_out%d" % no)
@@ -189,63 +234,30 @@ def tile_picked_painn8_none_p_kernel(
                     nc.scalar.copy(staged[:], src)
                 nc.sync.dma_start(dst, staged[:])
 
-        rest_sums = [sb.tile([P, PACK * HALF], F32, name=name) for name in ("zc_first", "zc_second")]
-        za_words = sb.tile([P, 2 * HALF], F32, name="za_words", tag="z_grouped0", align_bytes=64)
+        def gate_ahead(t):
+            if t + 1 < PACK:
+                gate(t + 1)
 
-        blocks = HALF // P
-        back = bank(2, "za_back")
-        for u in range(2):
-            turned = bank(u, "za_sum%d" % u)
-            for e in range(2):
-                t = 2 * u + e
-                sums = [sb.tile([P, HALF], F32, name=name % t) for name in ("za_first%d", "za_second%d")]
-                for side in range(2):
-                    fetch_and_add(sums[side][:], t, side, 0)
-                for blk in range(blocks):
-                    dst = turned[:, (2 * blk + e) * P : (2 * blk + e + 1) * P]
-                    for side in range(2):
-                        nc.tensor.matmul(
-                            dst,
-                            sums[side][:, blk * P : (blk + 1) * P],
-                            ident[:],
-                            is_transpose=True,
-                            start=(side == 0),
-                            stop=(side == 1),
-                        )
-            pairs = sb.tile([P, 2 * HALF], BF16, name="za_pairs%d" % u)
-            nc.scalar.copy(
-                pairs[:].rearrange("j (b p e) -> j b p e", e=2, p=P),
-                turned[:, : 2 * HALF].rearrange("j (b e p) -> j b p e", e=2, p=P),
-            )
-            for blk in range(blocks):
-                nc.tensor.transpose(
-                    back[:, u * HALF + blk * P : u * HALF + (blk + 1) * P],
-                    pairs[:].bitcast(F32)[:, blk * P : (blk + 1) * P],
-                    ident[:],
-                )
-        nc.scalar.copy(
-            za_words[:].rearrange("p (n u) -> p n u", u=2),
-            back[:, : 2 * HALF].rearrange("p (u n) -> p n u", u=2),
-        )
+        first = sb.tile([P, PACK * P], F32, name="zc_first")
+        second = sb.tile([P, PACK * P], F32, name="zc_second")
+        za_pairs = [sb.tile([P, 2 * P], F32, name="za_pairs%d" % u) for u in range(2)]
+        zb_pairs0 = sb.tile([P, P], F32, name="zb_pairs0")
+        gate(0)
+        za = turned_sums("za", 0, 2 * P, (4, 5), 6, [pairs[:] for pairs in za_pairs], gate_ahead)
+        quantise(w4_mx, 0, w4_grouped[:])
+        zb = turned_sums("zb", 2 * P, P, (7, 0), 1, [zb_pairs0[:], second[:, 5 * P // 2 : 7 * P // 2]], lambda t: None)
+        last_layer("za", za, 0, 2 * P, (2, 3), ())
+        last_layer("zb", zb, 2 * P, P, (4,), ())
 
-        unread = bank(2, "warm_up")
-        for t in range(WARM_UP_PASSES):
-            product(unread[:], w1_mx, t, x_mx)
-
-        last_layer("za", za_words[:].bitcast(BF16), 0, HALF, (4, 5), ())
-
-        for side in range(2):
+        c0 = 3 * P
+        for side, sums in enumerate((first, second)):
             for t in range(PACK):
-                fetch_and_add(rest_sums[side][:, t * HALF : (t + 1) * HALF], t, side, HALF)
-        z_rest = sb.tile([P, PACK * HALF], BF16, name="z_rest", tag="z_grouped0", align_bytes=64)
-        rest_grouped = [z_rest[:, blk * PACK * P : (blk + 1) * PACK * P] for blk in range(blocks)]
-        for blk in range(blocks):
-            atom_pairs = slice(blk * P // 2, (blk + 1) * P // 2)
-            nc.vector.tensor_tensor(
-                rest_grouped[blk].rearrange("p (c i t) -> p c t i", i=2, t=PACK),
-                rest_sums[0][:].rearrange("p (t c i) -> p c t i", i=2, t=PACK)[:, atom_pairs],
-                rest_sums[1][:].rearrange("p (t c i) -> p c t i", i=2, t=PACK)[:, atom_pairs],
-                ADD,
-            )
-        last_layer("zb", rest_grouped[0], HALF, P, (0, 3), (1,))
-        last_layer("zc", rest_grouped[1], HALF + P, P, (1, 6), (1,))
+                fetch_and_add(sums[:, t * P : (t + 1) * P], t, side, c0, P)
+        zc = sb.tile([P, PACK * P], BF16, name="zc_grouped", align_bytes=64)
+        nc.vector.tensor_tensor(
+            zc[:].rearrange("p (c i t) -> p c t i", i=2, t=PACK),
+            first[:].rearrange("p (t c i) -> p c t i", i=2, t=PACK),
+            second[:].rearrange("p (t c i) -> p c t i", i=2, t=PACK),
+            ADD,
+        )
+        last_layer("zc", zc[:], c0, P, (5, 6), (1,))

@@ -30,6 +30,7 @@ def tile_picked_painn8_none_p_kernel(
     with ExitStack() as ctx:
         lists = ctx.enter_context(tc.tile_pool(name="lists", bufs=1))
         sb = ctx.enter_context(tc.tile_pool(name="sb", bufs=1))
+        shared = ctx.enter_context(tc.tile_pool(name="shared", bufs=1))
         psum = ctx.enter_context(tc.psum_pool(name="psum", bufs=1))
 
         def bank(b, name):
@@ -57,7 +58,7 @@ def tile_picked_painn8_none_p_kernel(
                 x_scales[0, 4 * quad : 4 * quad + 4, :].bitcast(I32),
             )
         nc.sync.dma_start(w3_raw[1][:], by_rows(w3)[:, :, H // 2 :])
-        directions = [sb.tile([P, S], F32, name="dir%d_sb" % (side + 1)) for side in range(2)]
+        directions = [sb.tile([P, S], F32, name=name, tag=name) for name in ("dir1_sb", "dir2_sb")]
         for side, (place_list, direction) in enumerate(((p1, dir1), (p2, dir2))):
             nc.sync.dma_start(places[side][:], place_list)
             nc.sync.dma_start(directions[side][:], direction)
@@ -103,7 +104,8 @@ def tile_picked_painn8_none_p_kernel(
                 stop=True,
             )
 
-        q_win = [sb.tile([P, 2 * S], F32, name="q_win%d" % t) for t in range(PACK)]
+        q_win = [sb.tile([P, 2 * S], F32, name="q_win%d" % t) for t in range(PACK - 1)]
+        q_win.append(shared.tile([P, 2 * S], F32, name="q_win3", offset=0))
         for t in range(PACK):
             nc.vector.memset(q_win[t][:, S:], 0.0)
         w3_grouped = [sb.tile([P, 2 * H], BF16, name="w3_grouped%d" % u, align_bytes=64) for u in range(2)]
@@ -139,37 +141,51 @@ def tile_picked_painn8_none_p_kernel(
         quantise(w1_mx, 0, w1_grouped[:])
         for u in range(2):
             quantise(w2_mx, 2 * u * P, w2_grouped[:, pair_cols[u]])
-        y_sb = [sb.tile([P, S], F32, name="y_sb%d" % t) for t in range(PACK)]
-        for t in range(PACK):
-            acc = bank(PACK + t, "y_acc%d" % t)
-            product(acc[:], w1_mx, t, x_mx)
-            nc.scalar.copy(y_sb[t][:], acc[:])
+        last_factors = sb.tile([P, 2 * S], F32, name="last_factors")
+        w4_home = sb.tile([P, 2 * S], F32, name="w4_home", align_bytes=64)
+        y_tiles = [sb.tile([P, S], F32, name="y_sb%d" % t) for t in range(PACK - 1)]
+        e_first = sb.tile([P, S], F32, name="e_sb1")
+        y_sb = [tile[:] for tile in y_tiles] + [last_factors[:, :S]]
+        e_sb = {1: e_first[:], 2: w4_home[:, S:], 3: last_factors[:, S:]}
+        y_acc = [bank(PACK + t, "y_acc%d" % t) for t in range(PACK)]
         e_acc = [bank(t, "e_acc%d" % t) for t in range(PACK)]
         for t in range(PACK):
+            product(y_acc[t][:], w1_mx, t, x_mx)
+        for t in range(PACK):
             product(e_acc[t][:], w2_mx, t, x_mx)
+        for t in range(PACK):
+            nc.scalar.copy(y_sb[t], y_acc[t][:])
+            if t > 0:
+                nc.scalar.copy(e_sb[t], e_acc[t][:])
 
         free = sb.tile([P, 5 * S], F32, name="along_free")
-        after_w1 = sb.tile([P, 2 * S], F32, name="along_after_w1", tag="w1_raw")
-        after_w2 = sb.tile([P, S], F32, name="along_after_w2", tag="w2_raw")
-        homes = [free[:, n * S : (n + 1) * S] for n in range(5)] + [after_w1[:, :S], after_w1[:, S:], after_w2[:]]
+        after_w1 = sb.tile([P, S], F32, name="along_after_w1", tag="w1_raw")
+        after_w2 = sb.tile([P, 2 * S], F32, name="along_after_w2", tag="w2_raw")
+        homes = [free[:, n * S : (n + 1) * S] for n in range(5)] + [after_w1[:], after_w2[:, :S], after_w2[:, S:]]
         along = {}
         for t in range(PACK):
             for side in range(2):
                 along[t, side] = homes[2 * t + side]
                 nc.vector.tensor_tensor(along[t, side], q_win[t][:].indirect(places[side][:]), directions[side][:], MULT)
 
-        w4_grouped = sb.tile([P, PACK * N], BF16, name="w4_grouped", align_bytes=64)
+        m_win = [sb.tile([P, S], F32, name="m_win%d" % t, tag=tag) for t, tag in enumerate(("m_win0", "dir2_sb"))]
+        m_win += [shared.tile([P, S], F32, name="m_win%d" % t, offset=(t - 2) * 4 * S) for t in (2, 3)]
+        nc.vector.tensor_tensor(m_win[0][:], e_acc[0][:], y_sb[0], MULT)
+        for t in range(1, PACK):
+            nc.gpsimd.tensor_tensor(m_win[t][:], e_sb[t], y_sb[t], MULT)
+
+        w4_grouped = w4_home[:].bitcast(BF16)
         for part in range(2):
             column_pairs = slice(part * N // 4, (part + 1) * N // 4)
             nc.scalar.copy(
-                w4_grouped[:].rearrange("p (c i j) -> p c j i", i=2, j=PACK)[:, column_pairs],
+                w4_grouped.rearrange("p (c i j) -> p c j i", i=2, j=PACK)[:, column_pairs],
                 w4_raw[:].rearrange("p j (c i) -> p c j i", i=2)[:, column_pairs],
             )
 
-        m_win = [sb.tile([P, S], F32, name="m_win%d" % t) for t in range(PACK)]
 
-        def gate(t):
-            nc.vector.tensor_tensor(m_win[t][:], e_acc[t][:], y_sb[t][:], MULT)
+        def fetch(fetched, t, side, c0, width):
+            entries = places[side][:, c0 // LIST : (c0 + width) // LIST]
+            nc.vector.tensor_copy(fetched, m_win[t][:].indirect(entries))
 
         def fetch_and_add(summed, t, side, c0, width):
             entries = places[side][:, c0 // LIST : (c0 + width) // LIST]
@@ -178,26 +194,31 @@ def tile_picked_painn8_none_p_kernel(
         out_rows = out.rearrange("(a p) n -> p a n", p=P)
         w4_mx = mx_tiles("w4", N)
 
-        def turned_sums(name, c0, width, sum_banks, back_bank, pair_words, before_tile):
+        def turned_sums(name, c0, width, sum_banks, back_bank, pair_words, parts, plain_tiles):
             blocks = width // P
             back = bank(back_bank, name + "_back")
             for u in range(2):
                 turned = bank(sum_banks[u], name + "_sum%d" % u)
                 for e in range(2):
                     t = 2 * u + e
-                    before_tile(t)
-                    sums = [sb.tile([P, width], F32, name="%s_part%d_%d" % (name, t, side)) for side in range(2)]
+                    sums = [parts[t][:, side * width : (side + 1) * width] for side in range(2)]
+                    terms = list(sums)
+                    if t in plain_tiles:
+                        terms = [along[t, side][:, c0 : c0 + width] for side in range(2)] + terms
                     for side in range(2):
-                        fetch_and_add(sums[side][:], t, side, c0, width)
+                        if t in plain_tiles:
+                            fetch(sums[side], t, side, c0, width)
+                        else:
+                            fetch_and_add(sums[side], t, side, c0, width)
                     for blk in range(blocks):
-                        for side in range(2):
+                        for no, term in enumerate(terms):
                             nc.tensor.matmul(
                                 turned[:, (2 * blk + e) * P : (2 * blk + e + 1) * P],
-                                sums[side][:, blk * P : (blk + 1) * P],
+                                term[:, blk * P : (blk + 1) * P],
                                 ident[:],
                                 is_transpose=True,
-                                start=(side == 0),
-                                stop=(side == 1),
+                                start=(no == 0),
+                                stop=(no == len(terms) - 1),
                             )
                 pairs = pair_words[u]
                 nc.scalar.copy(
@@ -234,18 +255,16 @@ def tile_picked_painn8_none_p_kernel(
                     nc.scalar.copy(staged[:], src)
                 nc.sync.dma_start(dst, staged[:])
 
-        def gate_ahead(t):
-            if t + 1 < PACK:
-                gate(t + 1)
-
         first = sb.tile([P, PACK * P], F32, name="zc_first")
         second = sb.tile([P, PACK * P], F32, name="zc_second")
-        za_pairs = [sb.tile([P, 2 * P], F32, name="za_pairs%d" % u) for u in range(2)]
+        za_pairs0 = sb.tile([P, 2 * P], F32, name="za_pairs0")
+        za_tiles = [sb.tile([P, S], F32, name="za_parts%d" % t) for t in range(PACK - 1)]
+        za_parts = [tile[:] for tile in za_tiles] + [first[:]]
+        zb_parts = [last_factors[:, 2 * t * P : 2 * (t + 1) * P] for t in range(PACK)]
         zb_pairs0 = sb.tile([P, P], F32, name="zb_pairs0")
-        gate(0)
-        za = turned_sums("za", 0, 2 * P, (4, 5), 6, [pairs[:] for pairs in za_pairs], gate_ahead)
-        quantise(w4_mx, 0, w4_grouped[:])
-        zb = turned_sums("zb", 2 * P, P, (7, 0), 1, [zb_pairs0[:], second[:, 5 * P // 2 : 7 * P // 2]], lambda t: None)
+        za = turned_sums("za", 0, 2 * P, (4, 5), 6, [za_pairs0[:], second[:, : 2 * P]], za_parts, (0, 1, 2))
+        quantise(w4_mx, 0, w4_grouped)
+        zb = turned_sums("zb", 2 * P, P, (7, 0), 1, [zb_pairs0[:], second[:, 5 * P // 2 : 7 * P // 2]], zb_parts, ())
         last_layer("za", za, 0, 2 * P, (2, 3), ())
         last_layer("zb", zb, 2 * P, P, (4,), ())
 

@@ -58,7 +58,7 @@ def tile_picked_painn8_none_p_kernel(
                 x_scales[0, 4 * quad : 4 * quad + 4, :].bitcast(I32),
             )
         nc.sync.dma_start(w3_raw[1][:], by_rows(w3)[:, :, H // 2 :])
-        directions = [sb.tile([P, S], F32, name=name, tag=name) for name in ("dir1_sb", "dir2_sb")]
+        directions = [sb.tile([P, S], F32, name=name) for name in ("dir1_sb", "dir2_sb")]
         for side, (place_list, direction) in enumerate(((p1, dir1), (p2, dir2))):
             nc.sync.dma_start(places[side][:], place_list)
             nc.sync.dma_start(directions[side][:], direction)
@@ -104,8 +104,7 @@ def tile_picked_painn8_none_p_kernel(
                 stop=True,
             )
 
-        q_win = [sb.tile([P, 2 * S], F32, name="q_win%d" % t) for t in range(PACK - 1)]
-        q_win.append(shared.tile([P, 2 * S], F32, name="q_win3", offset=0))
+        q_win = [sb.tile([P, 2 * S], F32, name="q_win%d" % t) for t in range(PACK)]
         for t in range(PACK):
             nc.vector.memset(q_win[t][:, S:], 0.0)
         w3_grouped = [sb.tile([P, 2 * H], BF16, name="w3_grouped%d" % u, align_bytes=64) for u in range(2)]
@@ -141,12 +140,9 @@ def tile_picked_painn8_none_p_kernel(
         quantise(w1_mx, 0, w1_grouped[:])
         for u in range(2):
             quantise(w2_mx, 2 * u * P, w2_grouped[:, pair_cols[u]])
-        last_factors = sb.tile([P, 2 * S], F32, name="last_factors")
-        w4_home = sb.tile([P, 2 * S], F32, name="w4_home", align_bytes=64)
-        y_tiles = [sb.tile([P, S], F32, name="y_sb%d" % t) for t in range(PACK - 1)]
-        e_first = sb.tile([P, S], F32, name="e_sb1")
-        y_sb = [tile[:] for tile in y_tiles] + [last_factors[:, :S]]
-        e_sb = {1: e_first[:], 2: w4_home[:, S:], 3: last_factors[:, S:]}
+        y_sb = [sb.tile([P, S], F32, name="y_sb%d" % t) for t in range(PACK)]
+        e_sb = {t: sb.tile([P, S], F32, name="e_sb%d" % t) for t in (1, 2)}
+        e_sb[3] = shared.tile([P, S], F32, name="e_sb3", offset=0, align_bytes=64)
         y_acc = [bank(PACK + t, "y_acc%d" % t) for t in range(PACK)]
         e_acc = [bank(t, "e_acc%d" % t) for t in range(PACK)]
         for t in range(PACK):
@@ -154,93 +150,121 @@ def tile_picked_painn8_none_p_kernel(
         for t in range(PACK):
             product(e_acc[t][:], w2_mx, t, x_mx)
         for t in range(PACK):
-            nc.scalar.copy(y_sb[t], y_acc[t][:])
+            nc.scalar.copy(y_sb[t][:], y_acc[t][:])
             if t > 0:
-                nc.scalar.copy(e_sb[t], e_acc[t][:])
+                nc.scalar.copy(e_sb[t][:], e_acc[t][:])
 
-        free = sb.tile([P, 5 * S], F32, name="along_free")
-        after_w1 = sb.tile([P, S], F32, name="along_after_w1", tag="w1_raw")
-        after_w2 = sb.tile([P, 2 * S], F32, name="along_after_w2", tag="w2_raw")
-        homes = [free[:, n * S : (n + 1) * S] for n in range(5)] + [after_w1[:], after_w2[:, :S], after_w2[:, S:]]
+        early = sb.tile([P, 4 * S], F32, name="along_early")
+        late = [sb.tile([P, 2 * S], F32, name="along_late%d" % side, tag=tag) for side, tag in enumerate(("w1_raw", "w2_raw"))]
         along = {}
-        for t in range(PACK):
-            for side in range(2):
-                along[t, side] = homes[2 * t + side]
-                nc.vector.tensor_tensor(along[t, side], q_win[t][:].indirect(places[side][:]), directions[side][:], MULT)
+        for t, side in ((0, 0), (0, 1), (1, 0), (1, 1), (2, 0), (3, 0), (2, 1), (3, 1)):
+            if t < 2:
+                along[t, side] = early[:, (2 * t + side) * S : (2 * t + side + 1) * S]
+            else:
+                along[t, side] = late[side][:, (t - 2) * S : (t - 1) * S]
+            nc.vector.tensor_tensor(along[t, side], q_win[t][:].indirect(places[side][:]), directions[side][:], MULT)
 
-        m_win = [sb.tile([P, S], F32, name="m_win%d" % t, tag=tag) for t, tag in enumerate(("m_win0", "dir2_sb"))]
-        m_win += [shared.tile([P, S], F32, name="m_win%d" % t, offset=(t - 2) * 4 * S) for t in (2, 3)]
-        nc.vector.tensor_tensor(m_win[0][:], e_acc[0][:], y_sb[0], MULT)
+        m_win = [q_win[t] for t in (0, 3, 1, 2)]
+        nc.vector.tensor_tensor(m_win[0][:, :S], e_acc[0][:], y_sb[0][:], MULT)
+        half = S // 2
+        both_first = sb.tile([P, 2, half], F32, name="both_first")
+        nc.gpsimd.tensor_tensor(
+            both_first[:],
+            late[0][:].rearrange("p (t n) -> p t n", t=2)[:, :, :half],
+            late[1][:].rearrange("p (t n) -> p t n", t=2)[:, :, :half],
+            ADD,
+        )
         for t in range(1, PACK):
-            nc.gpsimd.tensor_tensor(m_win[t][:], e_sb[t], y_sb[t], MULT)
+            nc.gpsimd.tensor_tensor(m_win[t][:, :S], e_sb[t][:], y_sb[t][:], MULT)
 
-        w4_grouped = w4_home[:].bitcast(BF16)
+        def summed(name, b, blocks, dst):
+            turned = bank(b, name + "_turned")
+            count = len(blocks[0])
+            for no in range(count):
+                for blk, terms in enumerate(blocks):
+                    nc.tensor.matmul(
+                        turned[:, blk * P : (blk + 1) * P],
+                        terms[no],
+                        ident[:],
+                        is_transpose=True,
+                        start=(no == 0 and blk == 0),
+                        stop=(no == count - 1 and blk == len(blocks) - 1),
+                    )
+            width = len(blocks) * P
+            held = sb.tile([P, width], F32, name=name + "_held")
+            nc.scalar.copy(held[:], turned[:, :width])
+            back = bank(b, name + "_back")
+            for blk in range(len(blocks)):
+                nc.tensor.transpose(back[:, blk * P : (blk + 1) * P], held[:, blk * P : (blk + 1) * P], ident[:])
+            return back
+
+        def block(values, blk):
+            return values[:, blk * P : (blk + 1) * P]
+
+        fetched = {}
+        for t in range(2):
+            for side in range(2):
+                fetched[t, side] = sb.tile([P, S], F32, name="fetched%d_%d" % (t, side))
+                nc.vector.tensor_copy(fetched[t, side][:], m_win[t][:].indirect(places[side][:]))
+
+        def terms_of(t, blk):
+            return [block(values, blk) for values in (along[t, 0], along[t, 1], fetched[t, 0], fetched[t, 1])]
+
+        z_slots = sb.tile([P, 7 * half], F32, name="z_slots")
+
+        def slot(t, first):
+            no = t + 3 if first else t
+            return z_slots[:, no * half : (no + 1) * half]
+
+        both_second = sb.tile([P, 2, half], F32, name="both_second")
+        back = summed("both", 7, [[block(along[t, side], blk) for side in range(2)] for t in (2, 3) for blk in (2, 3)], None)
+        nc.scalar.copy(both_second[:].rearrange("p t n -> p (t n)"), back[:])
+        w4_grouped = sb.tile([P, PACK * N], BF16, name="w4_grouped", align_bytes=64)
         for part in range(2):
             column_pairs = slice(part * N // 4, (part + 1) * N // 4)
             nc.scalar.copy(
-                w4_grouped.rearrange("p (c i j) -> p c j i", i=2, j=PACK)[:, column_pairs],
+                w4_grouped[:].rearrange("p (c i j) -> p c j i", i=2, j=PACK)[:, column_pairs],
                 w4_raw[:].rearrange("p j (c i) -> p c j i", i=2)[:, column_pairs],
             )
 
+        back = summed("z0", 4, [terms_of(0, blk) for blk in (2, 3, 0, 1)], None)
+        nc.scalar.copy(
+            z_slots[:].rearrange("p (s n) -> p s n", n=half)[:, 0:4:3],
+            back[:].rearrange("p (s n) -> p s n", n=half),
+        )
+        back = summed("z1_first", 5, [terms_of(1, blk) for blk in (0, 1)], None)
+        nc.scalar.copy(slot(1, True), back[:, :half])
+        back = summed("z1_second", 6, [terms_of(1, blk) for blk in (2, 3)], None)
+        nc.scalar.copy(slot(1, False), back[:, :half])
 
-        def fetch(fetched, t, side, c0, width):
-            entries = places[side][:, c0 // LIST : (c0 + width) // LIST]
-            nc.vector.tensor_copy(fetched, m_win[t][:].indirect(entries))
+        partial3 = sb.tile([P, S], F32, name="partial3")
+        partial = {2: y_sb[3], 3: partial3}
 
-        def fetch_and_add(summed, t, side, c0, width):
-            entries = places[side][:, c0 // LIST : (c0 + width) // LIST]
-            nc.vector.tensor_tensor(summed, m_win[t][:].indirect(entries), along[t, side][:, c0 : c0 + width], ADD)
+        def chained(first, both):
+            c0 = 0 if first else half
+            entries = [places[side][:, c0 // LIST : (c0 + half) // LIST] for side in range(2)]
+            for t in (2, 3):
+                nc.vector.tensor_tensor(partial[t][:, c0 : c0 + half], m_win[t][:].indirect(entries[0]), both[:, t - 2, :], ADD)
+            return [
+                lambda t=t: nc.vector.tensor_tensor(
+                    slot(t, first), m_win[t][:].indirect(entries[1]), partial[t][:, c0 : c0 + half], ADD
+                )
+                for t in (2, 3)
+            ]
 
         out_rows = out.rearrange("(a p) n -> p a n", p=P)
-        w4_mx = mx_tiles("w4", N)
+        w4_codes = shared.tile([P, N], U32, name="w4_codes", offset=0, align_bytes=64)
+        w4_plane = sb.tile([P, N], U8, name="w4_plane", align_bytes=64)
+        w4_mx = (w4_codes, w4_plane)
 
-        def turned_sums(name, c0, width, sum_banks, back_bank, pair_words, parts, plain_tiles):
-            blocks = width // P
-            back = bank(back_bank, name + "_back")
-            for u in range(2):
-                turned = bank(sum_banks[u], name + "_sum%d" % u)
-                for e in range(2):
-                    t = 2 * u + e
-                    sums = [parts[t][:, side * width : (side + 1) * width] for side in range(2)]
-                    terms = list(sums)
-                    if t in plain_tiles:
-                        terms = [along[t, side][:, c0 : c0 + width] for side in range(2)] + terms
-                    for side in range(2):
-                        if t in plain_tiles:
-                            fetch(sums[side], t, side, c0, width)
-                        else:
-                            fetch_and_add(sums[side], t, side, c0, width)
-                    for blk in range(blocks):
-                        for no, term in enumerate(terms):
-                            nc.tensor.matmul(
-                                turned[:, (2 * blk + e) * P : (2 * blk + e + 1) * P],
-                                term[:, blk * P : (blk + 1) * P],
-                                ident[:],
-                                is_transpose=True,
-                                start=(no == 0),
-                                stop=(no == len(terms) - 1),
-                            )
-                pairs = pair_words[u]
-                nc.scalar.copy(
-                    pairs.bitcast(BF16).rearrange("j (b p e) -> j b p e", e=2, p=P),
-                    turned[:, : 2 * width].rearrange("j (b e p) -> j b p e", e=2, p=P),
-                )
-                for blk in range(blocks):
-                    nc.tensor.transpose(
-                        back[:, u * width + blk * P : u * width + (blk + 1) * P],
-                        pairs[:, blk * P : (blk + 1) * P],
-                        ident[:],
-                    )
-            words = sb.tile([P, 2 * width], F32, name=name + "_words", align_bytes=64)
-            nc.scalar.copy(
-                words[:].rearrange("p (n u) -> p n u", u=2),
-                back[:, : 2 * width].rearrange("p (u n) -> p n u", u=2),
-            )
-            return words[:].bitcast(BF16)
+        def rounded(name, copy, first, a0, width):
+            grouped = sb.tile([P, PACK * width], BF16, name=name + "_grouped", align_bytes=64)
+            s0 = 3 if first else 0
+            src = z_slots[:, s0 * half : (s0 + PACK) * half].rearrange("p (t c i) -> p c t i", t=PACK, i=4)
+            copy(grouped[:].rearrange("p (c i t) -> p c t i", t=PACK, i=4), src[:, a0 // 4 : (a0 + width) // 4])
+            return grouped
 
-        def last_layer(name, grouped, c0, width, out_banks, on_vector):
-            z_mx = mx_tiles(name, width)
-            quantise(z_mx, 0, grouped)
+        def last_layer(name, z_mx, c0, width, out_banks, on_vector):
             per_bank = PACK // len(out_banks)
             for no, b in enumerate(out_banks):
                 acc = bank(b, name + "_out%d" % no)
@@ -255,28 +279,18 @@ def tile_picked_painn8_none_p_kernel(
                     nc.scalar.copy(staged[:], src)
                 nc.sync.dma_start(dst, staged[:])
 
-        first = sb.tile([P, PACK * P], F32, name="zc_first")
-        second = sb.tile([P, PACK * P], F32, name="zc_second")
-        za_pairs0 = sb.tile([P, 2 * P], F32, name="za_pairs0")
-        za_tiles = [sb.tile([P, S], F32, name="za_parts%d" % t) for t in range(PACK - 1)]
-        za_parts = [tile[:] for tile in za_tiles] + [first[:]]
-        zb_parts = [last_factors[:, 2 * t * P : 2 * (t + 1) * P] for t in range(PACK)]
-        zb_pairs0 = sb.tile([P, P], F32, name="zb_pairs0")
-        za = turned_sums("za", 0, 2 * P, (4, 5), 6, [za_pairs0[:], second[:, : 2 * P]], za_parts, (0, 1, 2))
-        quantise(w4_mx, 0, w4_grouped)
-        zb = turned_sums("zb", 2 * P, P, (7, 0), 1, [zb_pairs0[:], second[:, 5 * P // 2 : 7 * P // 2]], zb_parts, ())
-        last_layer("za", za, 0, 2 * P, (2, 3), ())
-        last_layer("zb", zb, 2 * P, P, (4,), ())
-
-        c0 = 3 * P
-        for side, sums in enumerate((first, second)):
-            for t in range(PACK):
-                fetch_and_add(sums[:, t * P : (t + 1) * P], t, side, c0, P)
-        zc = sb.tile([P, PACK * P], BF16, name="zc_grouped", align_bytes=64)
-        nc.vector.tensor_tensor(
-            zc[:].rearrange("p (c i t) -> p c t i", i=2, t=PACK),
-            first[:].rearrange("p (t c i) -> p c t i", i=2, t=PACK),
-            second[:].rearrange("p (t c i) -> p c t i", i=2, t=PACK),
-            ADD,
-        )
-        last_layer("zc", zc[:], c0, P, (5, 6), (1,))
+        for finish in chained(True, both_first):
+            finish()
+        quantise(w4_mx, 0, w4_grouped[:])
+        za = rounded("za", nc.scalar.copy, True, 0, half)
+        za_mx = mx_tiles("za", half)
+        quantise(za_mx, 0, za[:])
+        last_layer("za", za_mx, 0, half, (0, 1), ())
+        for finish in chained(False, both_second):
+            finish()
+        grouped = [rounded(name, nc.vector.tensor_copy, False, a0, P) for name, a0 in (("zb", 0), ("zc", P))]
+        z_mx = [mx_tiles(name, P) for name in ("zb", "zc")]
+        for no in range(2):
+            quantise(z_mx[no], 0, grouped[no][:])
+        last_layer("zb", z_mx[0], half, P, (2, 3), (1,))
+        last_layer("zc", z_mx[1], half + P, P, (4, 5), (1,))

@@ -20,7 +20,7 @@ P = 128
 PACK = 4
 LIST = 16
 BANK = 512
-QUADRANTS = 4
+VECTOR_SHARE = 80
 
 
 def tile_picked_painn8_none_p_kernel(
@@ -46,22 +46,19 @@ def tile_picked_painn8_none_p_kernel(
 
         words_all = sb.tile([P, T], I32, name="words_all", align_bytes=64)
         scales_all = sb.tile([P, T], U8, name="scales_all", align_bytes=64)
-        nc.gpsimd.memset(scales_all[:].bitcast(I32), 0)
+        nc.vector.memset(scales_all[:].bitcast(I32), 0)
 
-        w3_raw = [sb.tile([P, PACK, H // 2], F32, name="w3_raw%d" % h) for h in range(2)]
+        w3_raw = sb.tile([P, PACK, H], F32, name="w3_raw")
         nc.sync.dma_start(words_all[:], x_words[0].rearrange("p n t -> p (n t)").bitcast(I32))
         nc.sync.dma_start(offs_sb[:], offs)
-        nc.sync.dma_start(w3_raw[0][:], by_rows(w3)[:, :, : H // 2])
-        for quad in range(QUADRANTS):
-            nc.sync.dma_start(
-                scales_all[32 * quad : 32 * quad + 4, :].bitcast(I32),
-                x_scales[0, 4 * quad : 4 * quad + 4, :].bitcast(I32),
-            )
-        nc.sync.dma_start(w3_raw[1][:], by_rows(w3)[:, :, H // 2 :])
+        nc.sync.dma_start(p1_sb[:], p1)
+        for row in range(4):
+            nc.sync.dma_start(scales_all[row:P:32, :].bitcast(I32), x_scales[0, row:16:4, :].bitcast(I32))
+        nc.sync.dma_start(w3_raw[:], by_rows(w3))
         directions = [sb.tile([P, S], F32, name=name) for name in ("dir1_sb", "dir2_sb")]
-        for side, (place_list, direction) in enumerate(((p1, dir1), (p2, dir2))):
-            nc.sync.dma_start(places[side][:], place_list)
-            nc.sync.dma_start(directions[side][:], direction)
+        nc.sync.dma_start(directions[0][:], dir1)
+        nc.sync.dma_start(p2_sb[:], p2)
+        nc.sync.dma_start(directions[1][:], dir2)
         w1_raw, w2_raw, w4_raw = [
             sb.tile([P, PACK, H], F32, name=name, tag=name) for name in ("w1_raw", "w2_raw", "w4_raw")
         ]
@@ -110,12 +107,10 @@ def tile_picked_painn8_none_p_kernel(
         w3_grouped = [sb.tile([P, 2 * H], BF16, name="w3_grouped%d" % u, align_bytes=64) for u in range(2)]
         spare = [grouped[:] for grouped in w3_grouped]
 
-        half_m = P // 2
         w3_mx = mx_tiles("w3", H)
-        for u in range(2):
-            nc.scalar.copy(dealt(spare[u])[:, :half_m], rows_of(w3_raw[0], u))
-        nc.vector.tensor_copy(dealt(spare[0])[:, half_m:], rows_of(w3_raw[1], 0))
-        nc.scalar.copy(dealt(spare[1])[:, half_m:], rows_of(w3_raw[1], 1))
+        nc.vector.tensor_copy(dealt(spare[0])[:, :VECTOR_SHARE], rows_of(w3_raw, 0)[:, :VECTOR_SHARE])
+        nc.scalar.copy(dealt(spare[0])[:, VECTOR_SHARE:], rows_of(w3_raw, 0)[:, VECTOR_SHARE:])
+        nc.scalar.copy(dealt(spare[1]), rows_of(w3_raw, 1))
         quantise(w3_mx, 0, spare[0][:, : PACK * P])
         quantise(w3_mx, P, spare[0][:, PACK * P :])
         low, high = slice(0, S // 2), slice(S // 2, S)

@@ -20,7 +20,7 @@ P = 128
 PACK = 4
 LIST = 16
 BANK = 512
-VECTOR_SHARE = 80
+ROWS = 8
 
 
 def tile_picked_painn8_none_p_kernel(
@@ -59,11 +59,13 @@ def tile_picked_painn8_none_p_kernel(
         nc.sync.dma_start(directions[0][:], dir1)
         nc.sync.dma_start(p2_sb[:], p2)
         nc.sync.dma_start(directions[1][:], dir2)
-        w1_raw, w2_raw, w4_raw = [
-            sb.tile([P, PACK, H], F32, name=name, tag=name) for name in ("w1_raw", "w2_raw", "w4_raw")
-        ]
-        for raw, w in ((w1_raw, w1), (w2_raw, w2), (w4_raw, w4)):
-            nc.sync.dma_start(raw[:], by_rows(w))
+        w1_home = sb.tile([P, S + PACK * H], F32, name="w1_home")
+        w1_raw = w1_home[:, S:].rearrange("p (j c) -> p j c", j=PACK)
+        w2_raw, w4_raw = [sb.tile([P, PACK, H], F32, name=name, tag=name) for name in ("w2_raw", "w4_raw")]
+        nc.sync.dma_start(w1_raw, by_rows(w1))
+        nc.sync.dma_start(w2_raw[:], by_rows(w2))
+        for t in range(PACK):
+            nc.sync.dma_start(w4_raw[:, t, :], w4.rearrange("(b t r) c -> t b r c", t=PACK, r=ROWS)[t])
 
         ident = sb.tile([P, P], F32, name="ident")
         make_identity(nc, ident[:])
@@ -74,11 +76,11 @@ def tile_picked_painn8_none_p_kernel(
         nc.vector.tensor_copy(x_plane[:], scales_all[:].indirect(offs_sb[:]))
         x_mx = (x_codes, x_plane)
 
-        def dealt(grouped):
-            return grouped.rearrange("p (e m j) -> p m j e", e=2, j=PACK)
-
-        def rows_of(raw, u):
-            return raw[:].rearrange("p j (m t) -> p m j t", t=PACK)[:, :, :, 2 * u : 2 * u + 2]
+        def round_tile(copy, grouped, raw, t):
+            copy(
+                grouped[:, t * H : (t + 1) * H].rearrange("p (b h i j) -> p b h j i", h=2, i=4, j=PACK),
+                raw.rearrange("p j (b t h i) -> p t b h j i", t=PACK, h=2, i=4)[:, t],
+            )
 
         def mx_tiles(name, width):
             codes = sb.tile([P, width], U32, name=name + "_codes", align_bytes=64)
@@ -104,22 +106,21 @@ def tile_picked_painn8_none_p_kernel(
         q_win = [sb.tile([P, 2 * S], F32, name="q_win%d" % t) for t in range(PACK)]
         for t in range(PACK):
             nc.vector.memset(q_win[t][:, S:], 0.0)
-        w3_grouped = [sb.tile([P, 2 * H], BF16, name="w3_grouped%d" % u, align_bytes=64) for u in range(2)]
-        spare = [grouped[:] for grouped in w3_grouped]
-
         w3_mx = mx_tiles("w3", H)
-        nc.vector.tensor_copy(dealt(spare[0])[:, :VECTOR_SHARE], rows_of(w3_raw, 0)[:, :VECTOR_SHARE])
-        nc.scalar.copy(dealt(spare[0])[:, VECTOR_SHARE:], rows_of(w3_raw, 0)[:, VECTOR_SHARE:])
-        nc.scalar.copy(dealt(spare[1]), rows_of(w3_raw, 1))
-        quantise(w3_mx, 0, spare[0][:, : PACK * P])
-        quantise(w3_mx, P, spare[0][:, PACK * P :])
+        w3_grouped = sb.tile([P, PACK * H], BF16, name="w3_grouped", align_bytes=64)
+        round_tile(nc.vector.tensor_copy, w3_grouped, w3_raw[:], 0)
+        quantise(w3_mx, 0, w3_grouped[:, :H])
+        for t in (1, 3):
+            round_tile(nc.scalar.copy, w3_grouped, w3_raw[:], t)
+        round_tile(nc.vector.tensor_copy, w3_grouped, w3_raw[:], 2)
+        quantise(w3_mx, P, w3_grouped[:, H : 2 * H])
+        quantise(w3_mx, 2 * P, w3_grouped[:, 2 * H :])
         low, high = slice(0, S // 2), slice(S // 2, S)
         q_low, q_high = bank(0, "q_low"), bank(4, "q_high")
         product(q_low[:, low], w3_mx, 0, x_mx, low)
         product(q_high[:, low], w3_mx, 0, x_mx, high)
         nc.vector.tensor_copy(q_win[0][:, low], q_low[:, low])
         nc.scalar.copy(q_win[0][:, high], q_high[:, low])
-        quantise(w3_mx, 2 * P, spare[1])
         for t in range(1, PACK):
             acc = bank(t, "q_acc%d" % t)
             product(acc[:], w3_mx, t, x_mx)
@@ -129,9 +130,9 @@ def tile_picked_painn8_none_p_kernel(
         w1_grouped = sb.tile([P, PACK * H], BF16, name="w1_grouped", align_bytes=64)
         w2_grouped = sb.tile([P, PACK * H], BF16, name="w2_grouped", align_bytes=64)
         pair_cols = [slice(u * 2 * H, (u + 1) * 2 * H) for u in range(2)]
-        for raw, grouped in ((w1_raw, w1_grouped), (w2_raw, w2_grouped)):
-            for u in range(2):
-                nc.scalar.copy(dealt(grouped[:, pair_cols[u]]), rows_of(raw, u))
+        for raw, grouped in ((w1_raw, w1_grouped), (w2_raw[:], w2_grouped)):
+            for t in range(PACK):
+                round_tile(nc.scalar.copy, grouped, raw, t)
         quantise(w1_mx, 0, w1_grouped[:])
         for u in range(2):
             quantise(w2_mx, 2 * u * P, w2_grouped[:, pair_cols[u]])
@@ -150,7 +151,8 @@ def tile_picked_painn8_none_p_kernel(
                 nc.scalar.copy(e_sb[t][:], e_acc[t][:])
 
         early = sb.tile([P, 4 * S], F32, name="along_early")
-        late = [sb.tile([P, 2 * S], F32, name="along_late%d" % side, tag=tag) for side, tag in enumerate(("w1_raw", "w2_raw"))]
+        late_second = sb.tile([P, 2 * S], F32, name="along_late1", tag="w2_raw")
+        late = [w1_home[:, : 2 * S], late_second[:]]
         along = {}
         for t, side in ((0, 0), (0, 1), (1, 0), (1, 1), (2, 0), (3, 0), (2, 1), (3, 1)):
             if t < 2:
@@ -159,20 +161,20 @@ def tile_picked_painn8_none_p_kernel(
                 along[t, side] = late[side][:, (t - 2) * S : (t - 1) * S]
             nc.vector.tensor_tensor(along[t, side], q_win[t][:].indirect(places[side][:]), directions[side][:], MULT)
 
-        m_win = [q_win[t] for t in (0, 3, 1, 2)]
+        m_win = [q_win[0], q_win[3]] + [sb.tile([P, S], F32, name="m_win%d" % t) for t in (2, 3)]
         nc.vector.tensor_tensor(m_win[0][:, :S], e_acc[0][:], y_sb[0][:], MULT)
         half = S // 2
         both_first = sb.tile([P, 2, half], F32, name="both_first")
         nc.gpsimd.tensor_tensor(
             both_first[:],
-            late[0][:].rearrange("p (t n) -> p t n", t=2)[:, :, :half],
-            late[1][:].rearrange("p (t n) -> p t n", t=2)[:, :, :half],
+            late[0].rearrange("p (t n) -> p t n", t=2)[:, :, :half],
+            late[1].rearrange("p (t n) -> p t n", t=2)[:, :, :half],
             ADD,
         )
         for t in range(1, PACK):
             nc.gpsimd.tensor_tensor(m_win[t][:, :S], e_sb[t][:], y_sb[t][:], MULT)
 
-        def summed(name, b, blocks, dst):
+        def summed(name, b, blocks):
             turned = bank(b, name + "_turned")
             count = len(blocks[0])
             for no in range(count):
@@ -205,61 +207,63 @@ def tile_picked_painn8_none_p_kernel(
         def terms_of(t, blk):
             return [block(values, blk) for values in (along[t, 0], along[t, 1], fetched[t, 0], fetched[t, 1])]
 
-        z_slots = sb.tile([P, 7 * half], F32, name="z_slots")
-
-        def slot(t, first):
-            no = t + 3 if first else t
-            return z_slots[:, no * half : (no + 1) * half]
+        za = sb.tile([P, PACK * half], F32, name="za")
+        z_late = sb.tile([P, 7 * P], F32, name="z_late")
+        late_slots = z_late[:].rearrange("p (s n) -> p s n", n=P)
+        chunks = {"a": (0, half, za[:]), "b": (half, P, z_late[:, 3 * P :]), "c": (half + P, P, z_late[:, : PACK * P])}
 
         both_second = sb.tile([P, 2, half], F32, name="both_second")
-        back = summed("both", 7, [[block(along[t, side], blk) for side in range(2)] for t in (2, 3) for blk in (2, 3)], None)
+        back = summed("both", 7, [[block(along[t, side], blk) for side in range(2)] for t in (2, 3) for blk in (2, 3)])
         nc.scalar.copy(both_second[:].rearrange("p t n -> p (t n)"), back[:])
         w4_grouped = sb.tile([P, PACK * N], BF16, name="w4_grouped", align_bytes=64)
         for part in range(2):
-            column_pairs = slice(part * N // 4, (part + 1) * N // 4)
+            column_pairs = slice(part * N // 8, (part + 1) * N // 8)
             nc.scalar.copy(
-                w4_grouped[:].rearrange("p (c i j) -> p c j i", i=2, j=PACK)[:, column_pairs],
-                w4_raw[:].rearrange("p j (c i) -> p c j i", i=2)[:, column_pairs],
+                w4_grouped[:].rearrange("p (c i j) -> p c j i", i=4, j=PACK)[:, column_pairs],
+                w4_raw[:].rearrange("p j (c i) -> p c j i", i=4)[:, column_pairs],
             )
 
-        back = summed("z0", 4, [terms_of(0, blk) for blk in (2, 3, 0, 1)], None)
-        nc.scalar.copy(
-            z_slots[:].rearrange("p (s n) -> p s n", n=half)[:, 0:4:3],
-            back[:].rearrange("p (s n) -> p s n", n=half),
-        )
-        back = summed("z1_first", 5, [terms_of(1, blk) for blk in (0, 1)], None)
-        nc.scalar.copy(slot(1, True), back[:, :half])
-        back = summed("z1_second", 6, [terms_of(1, blk) for blk in (2, 3)], None)
-        nc.scalar.copy(slot(1, False), back[:, :half])
+        back = summed("z0", 4, [terms_of(0, blk) for blk in (0, 1, 3, 2)])
+        nc.scalar.copy(za[:, :half], back[:, :half])
+        nc.scalar.copy(late_slots[:, 0:4:3], back[:, half:].rearrange("p (s n) -> p s n", n=P))
+        back = summed("z1_first", 5, [terms_of(1, blk) for blk in (0, 1)])
+        nc.scalar.copy(za[:, half:S], back[:, :half])
+        back = summed("z1_second", 6, [terms_of(1, blk) for blk in (3, 2)])
+        nc.scalar.copy(late_slots[:, 1:5:3], back[:, :half].rearrange("p (s n) -> p s n", n=P))
 
-        partial3 = sb.tile([P, S], F32, name="partial3")
-        partial = {2: y_sb[3], 3: partial3}
+        partial3 = sb.tile([P, half + P], F32, name="partial3")
+        partial = {("a", 2): y_sb[3][:, :half], ("b", 2): y_sb[3][:, half : half + P], ("c", 2): za[:, :P]}
+        partial.update({("a", 3): partial3[:, :half], ("b", 3): partial3[:, half:], ("c", 3): za[:, P : 2 * P]})
+        both = {"a": both_first[:], "b": both_second[:, :, :P], "c": both_second[:, :, P:]}
 
-        def chained(first, both):
-            c0 = 0 if first else half
-            entries = [places[side][:, c0 // LIST : (c0 + half) // LIST] for side in range(2)]
+        def chained(name):
+            c0, width, z = chunks[name]
+            entries = [places[side][:, c0 // LIST : (c0 + width) // LIST] for side in range(2)]
             for t in (2, 3):
-                nc.vector.tensor_tensor(partial[t][:, c0 : c0 + half], m_win[t][:].indirect(entries[0]), both[:, t - 2, :], ADD)
-            return [
-                lambda t=t: nc.vector.tensor_tensor(
-                    slot(t, first), m_win[t][:].indirect(entries[1]), partial[t][:, c0 : c0 + half], ADD
+                nc.vector.tensor_tensor(partial[name, t], m_win[t][:].indirect(entries[0]), both[name][:, t - 2, :], ADD)
+            for t in (2, 3):
+                nc.vector.tensor_tensor(
+                    z[:, t * width : (t + 1) * width], m_win[t][:].indirect(entries[1]), partial[name, t], ADD
                 )
-                for t in (2, 3)
-            ]
 
         out_rows = out.rearrange("(a p) n -> p a n", p=P)
         w4_codes = shared.tile([P, N], U32, name="w4_codes", offset=0, align_bytes=64)
         w4_plane = sb.tile([P, N], U8, name="w4_plane", align_bytes=64)
         w4_mx = (w4_codes, w4_plane)
 
-        def rounded(name, copy, first, a0, width):
+        def rounded(name, copy):
+            c0, width, z = chunks[name]
             grouped = sb.tile([P, PACK * width], BF16, name=name + "_grouped", align_bytes=64)
-            s0 = 3 if first else 0
-            src = z_slots[:, s0 * half : (s0 + PACK) * half].rearrange("p (t c i) -> p c t i", t=PACK, i=4)
-            copy(grouped[:].rearrange("p (c i t) -> p c t i", t=PACK, i=4), src[:, a0 // 4 : (a0 + width) // 4])
+            copy(
+                grouped[:].rearrange("p (c i t) -> p c t i", t=PACK, i=4),
+                z.rearrange("p (t c i) -> p c t i", t=PACK, i=4),
+            )
             return grouped
 
-        def last_layer(name, z_mx, c0, width, out_banks, on_vector):
+        def last_layer(name, grouped, out_banks, on_vector):
+            c0, width, z = chunks[name]
+            z_mx = mx_tiles("z" + name, width)
+            quantise(z_mx, 0, grouped[:])
             per_bank = PACK // len(out_banks)
             for no, b in enumerate(out_banks):
                 acc = bank(b, name + "_out%d" % no)
@@ -274,18 +278,12 @@ def tile_picked_painn8_none_p_kernel(
                     nc.scalar.copy(staged[:], src)
                 nc.sync.dma_start(dst, staged[:])
 
-        for finish in chained(True, both_first):
-            finish()
+        chained("a")
         quantise(w4_mx, 0, w4_grouped[:])
-        za = rounded("za", nc.scalar.copy, True, 0, half)
-        za_mx = mx_tiles("za", half)
-        quantise(za_mx, 0, za[:])
-        last_layer("za", za_mx, 0, half, (0, 1), ())
-        for finish in chained(False, both_second):
-            finish()
-        grouped = [rounded(name, nc.vector.tensor_copy, False, a0, P) for name, a0 in (("zb", 0), ("zc", P))]
-        z_mx = [mx_tiles(name, P) for name in ("zb", "zc")]
-        for no in range(2):
-            quantise(z_mx[no], 0, grouped[no][:])
-        last_layer("zb", z_mx[0], half, P, (2, 3), (1,))
-        last_layer("zc", z_mx[1], half + P, P, (4, 5), (1,))
+        a_grouped = rounded("a", nc.scalar.copy)
+        chained("b")
+        b_grouped = rounded("b", nc.scalar.copy)
+        last_layer("a", a_grouped, (0, 1), ())
+        chained("c")
+        last_layer("b", b_grouped, (2,), ())
+        last_layer("c", rounded("c", nc.vector.tensor_copy), (3, 4, 5, 6), (1, 3))

@@ -20,6 +20,7 @@ P = 128
 PACK = 4
 LIST = 16
 BANK = 512
+VECTOR_COLUMNS = 256
 ROWS = 8
 
 
@@ -139,6 +140,7 @@ def tile_picked_painn8_none_p_kernel(
         y_sb = [sb.tile([P, S], F32, name="y_sb%d" % t) for t in range(PACK)]
         e_sb = {t: sb.tile([P, S], F32, name="e_sb%d" % t) for t in (1, 2)}
         e_sb[3] = shared.tile([P, S], F32, name="e_sb3", offset=0, align_bytes=64)
+        on_gpsimd = {1: slice(VECTOR_COLUMNS, S), 2: slice(0, S), 3: slice(0, S)}
         y_acc = [bank(PACK + t, "y_acc%d" % t) for t in range(PACK)]
         e_acc = [bank(t, "e_acc%d" % t) for t in range(PACK)]
         for t in range(PACK):
@@ -148,7 +150,7 @@ def tile_picked_painn8_none_p_kernel(
         for t in range(PACK):
             nc.scalar.copy(y_sb[t][:], y_acc[t][:])
             if t > 0:
-                nc.scalar.copy(e_sb[t][:], e_acc[t][:])
+                nc.scalar.copy(e_sb[t][:, on_gpsimd[t]], e_acc[t][:, on_gpsimd[t]])
 
         early = sb.tile([P, 4 * S], F32, name="along_early")
         late_second = sb.tile([P, 2 * S], F32, name="along_late1", tag="w2_raw")
@@ -163,6 +165,9 @@ def tile_picked_painn8_none_p_kernel(
 
         m_win = [q_win[0], q_win[3]] + [sb.tile([P, S], F32, name="m_win%d" % t) for t in (2, 3)]
         nc.vector.tensor_tensor(m_win[0][:, :S], e_acc[0][:], y_sb[0][:], MULT)
+        nc.vector.tensor_tensor(
+            m_win[1][:, :VECTOR_COLUMNS], e_acc[1][:, :VECTOR_COLUMNS], y_sb[1][:, :VECTOR_COLUMNS], MULT
+        )
         half = S // 2
         both_first = sb.tile([P, 2, half], F32, name="both_first")
         nc.gpsimd.tensor_tensor(
@@ -172,9 +177,10 @@ def tile_picked_painn8_none_p_kernel(
             ADD,
         )
         for t in range(1, PACK):
-            nc.gpsimd.tensor_tensor(m_win[t][:, :S], e_sb[t][:], y_sb[t][:], MULT)
+            cols = on_gpsimd[t]
+            nc.gpsimd.tensor_tensor(m_win[t][:, cols], e_sb[t][:, cols], y_sb[t][:, cols], MULT)
 
-        def summed(name, b, blocks):
+        def summed(name, b, blocks, held_tag):
             turned = bank(b, name + "_turned")
             count = len(blocks[0])
             for no in range(count):
@@ -188,7 +194,7 @@ def tile_picked_painn8_none_p_kernel(
                         stop=(no == count - 1 and blk == len(blocks) - 1),
                     )
             width = len(blocks) * P
-            held = sb.tile([P, width], F32, name=name + "_held")
+            held = sb.tile([P, width], F32, name=name + "_held", tag=held_tag)
             nc.scalar.copy(held[:], turned[:, :width])
             back = bank(b, name + "_back")
             for blk in range(len(blocks)):
@@ -207,13 +213,18 @@ def tile_picked_painn8_none_p_kernel(
         def terms_of(t, blk):
             return [block(values, blk) for values in (along[t, 0], along[t, 1], fetched[t, 0], fetched[t, 1])]
 
-        za = sb.tile([P, PACK * half], F32, name="za")
-        z_late = sb.tile([P, 7 * P], F32, name="z_late")
-        late_slots = z_late[:].rearrange("p (s n) -> p s n", n=P)
-        chunks = {"a": (0, half, za[:]), "b": (half, P, z_late[:, 3 * P :]), "c": (half + P, P, z_late[:, : PACK * P])}
+        z_flat = sb.tile([P, 7 * PACK * half], F32, name="z_home")
+        z_home = z_flat[:].rearrange("p (s x) -> p s x", s=7)
+        za = z_home[:, 4, :]
+        late_slots = z_home[:, :, :P]
+        chunks = {
+            "a": (0, half, za.rearrange("p (t n) -> p t n", t=PACK)),
+            "b": (half, P, late_slots[:, 3:]),
+            "c": (half + P, P, late_slots[:, :PACK]),
+        }
 
         both_second = sb.tile([P, 2, half], F32, name="both_second")
-        back = summed("both", 7, [[block(along[t, side], blk) for side in range(2)] for t in (2, 3) for blk in (2, 3)])
+        back = summed("both", 7, [[block(along[t, side], blk) for side in range(2)] for t in (2, 3) for blk in (2, 3)], "both_held")
         nc.scalar.copy(both_second[:].rearrange("p t n -> p (t n)"), back[:])
         w4_grouped = sb.tile([P, PACK * N], BF16, name="w4_grouped", align_bytes=64)
         for part in range(2):
@@ -223,28 +234,27 @@ def tile_picked_painn8_none_p_kernel(
                 w4_raw[:].rearrange("p j (c i) -> p c j i", i=4)[:, column_pairs],
             )
 
-        back = summed("z0", 4, [terms_of(0, blk) for blk in (0, 1, 3, 2)])
+        back = summed("z0", 4, [terms_of(0, blk) for blk in (0, 1, 3, 2)], "w4_raw")
         nc.scalar.copy(za[:, :half], back[:, :half])
         nc.scalar.copy(late_slots[:, 0:4:3], back[:, half:].rearrange("p (s n) -> p s n", n=P))
-        back = summed("z1_first", 5, [terms_of(1, blk) for blk in (0, 1)])
+        back = summed("z1_first", 5, [terms_of(1, blk) for blk in (0, 1)], "z1_first_held")
         nc.scalar.copy(za[:, half:S], back[:, :half])
-        back = summed("z1_second", 6, [terms_of(1, blk) for blk in (3, 2)])
-        nc.scalar.copy(late_slots[:, 1:5:3], back[:, :half].rearrange("p (s n) -> p s n", n=P))
+        z1_second = summed("z1_second", 6, [terms_of(1, blk) for blk in (3, 2)], "z1_second_held")
+        nc.scalar.copy(late_slots[:, 1, :], z1_second[:, :P])
 
         partial3 = sb.tile([P, half + P], F32, name="partial3")
-        partial = {("a", 2): y_sb[3][:, :half], ("b", 2): y_sb[3][:, half : half + P], ("c", 2): za[:, :P]}
-        partial.update({("a", 3): partial3[:, :half], ("b", 3): partial3[:, half:], ("c", 3): za[:, P : 2 * P]})
+        partial = {("a", 2): y_sb[3][:, :half], ("b", 2): y_sb[3][:, half : half + P], ("c", 2): za[:, S : S + P]}
+        partial.update({("a", 3): partial3[:, :half], ("b", 3): partial3[:, half:], ("c", 3): za[:, S + P : S + 2 * P]})
         both = {"a": both_first[:], "b": both_second[:, :, :P], "c": both_second[:, :, P:]}
 
-        def chained(name):
+        def chained(name, between):
             c0, width, z = chunks[name]
             entries = [places[side][:, c0 // LIST : (c0 + width) // LIST] for side in range(2)]
             for t in (2, 3):
                 nc.vector.tensor_tensor(partial[name, t], m_win[t][:].indirect(entries[0]), both[name][:, t - 2, :], ADD)
+            between()
             for t in (2, 3):
-                nc.vector.tensor_tensor(
-                    z[:, t * width : (t + 1) * width], m_win[t][:].indirect(entries[1]), partial[name, t], ADD
-                )
+                nc.vector.tensor_tensor(z[:, t, :], m_win[t][:].indirect(entries[1]), partial[name, t], ADD)
 
         out_rows = out.rearrange("(a p) n -> p a n", p=P)
         w4_codes = shared.tile([P, N], U32, name="w4_codes", offset=0, align_bytes=64)
@@ -256,7 +266,7 @@ def tile_picked_painn8_none_p_kernel(
             grouped = sb.tile([P, PACK * width], BF16, name=name + "_grouped", align_bytes=64)
             copy(
                 grouped[:].rearrange("p (c i t) -> p c t i", t=PACK, i=4),
-                z.rearrange("p (t c i) -> p c t i", t=PACK, i=4),
+                z.rearrange("p t (c i) -> p c t i", i=4),
             )
             return grouped
 
@@ -269,21 +279,25 @@ def tile_picked_painn8_none_p_kernel(
                 acc = bank(b, name + "_out%d" % no)
                 for a in range(per_bank):
                     product(acc[:, a * width : (a + 1) * width], w4_mx, no * per_bank + a, z_mx)
-                staged = sb.tile([P, per_bank, width], F32, name=name + "_staged%d" % no)
+                if name == "a":
+                    staged = z_home[:, 4 + no, :S].rearrange("p (a n) -> p a n", a=per_bank)
+                else:
+                    staged_tile = sb.tile([P, per_bank, width], F32, name=name + "_staged%d" % no)
+                    staged = staged_tile[:]
                 src = acc[:, : per_bank * width].rearrange("p (a n) -> p a n", a=per_bank)
                 dst = out_rows[:, no * per_bank : (no + 1) * per_bank, c0 : c0 + width]
                 if no in on_vector:
-                    nc.vector.tensor_copy(staged[:], src)
+                    nc.vector.tensor_copy(staged, src)
                 else:
-                    nc.scalar.copy(staged[:], src)
-                nc.sync.dma_start(dst, staged[:])
+                    nc.scalar.copy(staged, src)
+                nc.sync.dma_start(dst, staged)
 
-        chained("a")
-        quantise(w4_mx, 0, w4_grouped[:])
+        chained("a", lambda: None)
         a_grouped = rounded("a", nc.scalar.copy)
-        chained("b")
+        nc.scalar.copy(late_slots[:, 4, :], z1_second[:, P:half])
+        chained("b", lambda: quantise(w4_mx, 0, w4_grouped[:]))
         b_grouped = rounded("b", nc.scalar.copy)
         last_layer("a", a_grouped, (0, 1), ())
-        chained("c")
+        chained("c", lambda: None)
         last_layer("b", b_grouped, (2,), ())
         last_layer("c", rounded("c", nc.vector.tensor_copy), (3, 4, 5, 6), (1, 3))

@@ -20,7 +20,7 @@ P = 128
 PACK = 4
 LIST = 16
 BANK = 512
-VECTOR_COLUMNS = 256
+VECTOR_COLUMNS = 384
 ROWS = 8
 
 
@@ -56,13 +56,15 @@ def tile_picked_painn8_none_p_kernel(
         for row in range(4):
             nc.sync.dma_start(scales_all[row:P:32, :].bitcast(I32), x_scales[0, row:16:4, :].bitcast(I32))
         nc.sync.dma_start(w3_raw[:], by_rows(w3))
-        directions = [sb.tile([P, S], F32, name=name) for name in ("dir1_sb", "dir2_sb")]
+        directions = [sb.tile([P, S], F32, name=name, tag=name) for name in ("dir1_sb", "dir2_sb")]
         nc.sync.dma_start(directions[0][:], dir1)
         nc.sync.dma_start(p2_sb[:], p2)
         nc.sync.dma_start(directions[1][:], dir2)
         w1_home = sb.tile([P, S + PACK * H], F32, name="w1_home")
         w1_raw = w1_home[:, S:].rearrange("p (j c) -> p j c", j=PACK)
-        w2_raw, w4_raw = [sb.tile([P, PACK, H], F32, name=name, tag=name) for name in ("w2_raw", "w4_raw")]
+        w2_raw = sb.tile([P, PACK, H], F32, name="w2_raw", tag="w2_raw")
+        w4_home = sb.tile([P, PACK * N], F32, name="w4_home")
+        w4_raw = w4_home[:].rearrange("p (t c) -> p t c", t=PACK)
         nc.sync.dma_start(w1_raw, by_rows(w1))
         nc.sync.dma_start(w2_raw[:], by_rows(w2))
         for t in range(PACK):
@@ -137,18 +139,18 @@ def tile_picked_painn8_none_p_kernel(
         quantise(w1_mx, 0, w1_grouped[:])
         for u in range(2):
             quantise(w2_mx, 2 * u * P, w2_grouped[:, pair_cols[u]])
-        y_sb = [sb.tile([P, S], F32, name="y_sb%d" % t) for t in range(PACK)]
+        y_tiles = [sb.tile([P, S], F32, name="y_sb%d" % t) for t in range(PACK - 1)]
+        y3_home = sb.tile([P, 2 * S], F32, name="y3_home")
+        y_sb = [tile[:] for tile in y_tiles] + [y3_home[:, S // 2 : 3 * S // 2]]
         e_sb = {t: sb.tile([P, S], F32, name="e_sb%d" % t) for t in (1, 2)}
         e_sb[3] = shared.tile([P, S], F32, name="e_sb3", offset=0, align_bytes=64)
         on_gpsimd = {1: slice(VECTOR_COLUMNS, S), 2: slice(0, S), 3: slice(0, S)}
-        y_acc = [bank(PACK + t, "y_acc%d" % t) for t in range(PACK)]
         e_acc = [bank(t, "e_acc%d" % t) for t in range(PACK)]
         for t in range(PACK):
-            product(y_acc[t][:], w1_mx, t, x_mx)
-        for t in range(PACK):
+            y_acc = bank(4 + t % 2, "y_acc%d" % t)
+            product(y_acc[:], w1_mx, t, x_mx)
             product(e_acc[t][:], w2_mx, t, x_mx)
-        for t in range(PACK):
-            nc.scalar.copy(y_sb[t][:], y_acc[t][:])
+            nc.scalar.copy(y_sb[t], y_acc[:])
             if t > 0:
                 nc.scalar.copy(e_sb[t][:, on_gpsimd[t]], e_acc[t][:, on_gpsimd[t]])
 
@@ -163,8 +165,10 @@ def tile_picked_painn8_none_p_kernel(
                 along[t, side] = late[side][:, (t - 2) * S : (t - 1) * S]
             nc.vector.tensor_tensor(along[t, side], q_win[t][:].indirect(places[side][:]), directions[side][:], MULT)
 
-        m_win = [q_win[0], q_win[3]] + [sb.tile([P, S], F32, name="m_win%d" % t) for t in (2, 3)]
-        nc.vector.tensor_tensor(m_win[0][:, :S], e_acc[0][:], y_sb[0][:], MULT)
+        m_win = [q_win[0]] + [
+            sb.tile([P, S], F32, name="m_win%d" % t, tag=tag) for t, tag in ((1, "dir2_sb"), (2, "m_win2"), (3, "m_win3"))
+        ]
+        nc.vector.tensor_tensor(m_win[0][:, :S], e_acc[0][:], y_sb[0], MULT)
         nc.vector.tensor_tensor(
             m_win[1][:, :VECTOR_COLUMNS], e_acc[1][:, :VECTOR_COLUMNS], y_sb[1][:, :VECTOR_COLUMNS], MULT
         )
@@ -180,7 +184,7 @@ def tile_picked_painn8_none_p_kernel(
             cols = on_gpsimd[t]
             nc.gpsimd.tensor_tensor(m_win[t][:, cols], e_sb[t][:, cols], y_sb[t][:, cols], MULT)
 
-        def summed(name, b, blocks, held_tag):
+        def summed(name, b, blocks, row):
             turned = bank(b, name + "_turned")
             count = len(blocks[0])
             for no in range(count):
@@ -194,8 +198,8 @@ def tile_picked_painn8_none_p_kernel(
                         stop=(no == count - 1 and blk == len(blocks) - 1),
                     )
             width = len(blocks) * P
-            held = sb.tile([P, width], F32, name=name + "_held", tag=held_tag)
-            nc.scalar.copy(held[:], turned[:, :width])
+            held = w4_raw[:, row, :width]
+            nc.scalar.copy(held, turned[:, :width])
             back = bank(b, name + "_back")
             for blk in range(len(blocks)):
                 nc.tensor.transpose(back[:, blk * P : (blk + 1) * P], held[:, blk * P : (blk + 1) * P], ident[:])
@@ -205,99 +209,122 @@ def tile_picked_painn8_none_p_kernel(
             return values[:, blk * P : (blk + 1) * P]
 
         fetched = {}
-        for t in range(2):
+        for t, width in ((0, S), (1, half)):
             for side in range(2):
-                fetched[t, side] = sb.tile([P, S], F32, name="fetched%d_%d" % (t, side))
-                nc.vector.tensor_copy(fetched[t, side][:], m_win[t][:].indirect(places[side][:]))
+                fetched[t, side] = sb.tile([P, width], F32, name="fetched%d_%d" % (t, side))
+                nc.vector.tensor_copy(fetched[t, side][:], m_win[t][:].indirect(places[side][:, : width // LIST]))
 
         def terms_of(t, blk):
             return [block(values, blk) for values in (along[t, 0], along[t, 1], fetched[t, 0], fetched[t, 1])]
 
-        z_flat = sb.tile([P, 7 * PACK * half], F32, name="z_home")
-        z_home = z_flat[:].rearrange("p (s x) -> p s x", s=7)
-        za = z_home[:, 4, :]
-        late_slots = z_home[:, :, :P]
-        chunks = {
-            "a": (0, half, za.rearrange("p (t n) -> p t n", t=PACK)),
-            "b": (half, P, late_slots[:, 3:]),
-            "c": (half + P, P, late_slots[:, :PACK]),
-        }
+        def directions_of(t, blk):
+            return [block(along[t, side], blk) for side in range(2)]
 
-        both_second = sb.tile([P, 2, half], F32, name="both_second")
-        back = summed("both", 7, [[block(along[t, side], blk) for side in range(2)] for t in (2, 3) for blk in (2, 3)], "both_held")
-        nc.scalar.copy(both_second[:].rearrange("p t n -> p (t n)"), back[:])
+        z_home = sb.tile([P, 9 * half], F32, name="z_home", align_bytes=64)
+        slots = z_home[:].rearrange("p (s n) -> p s n", n=half)
+        z_first = slots[:, 5:, :]
+        chunks = {"a": (0, half, z_first), "b": (half, P, slots[:, 4:8, :P]), "c": (half + P, P, slots[:, :4, :P])}
+
         w4_grouped = sb.tile([P, PACK * N], BF16, name="w4_grouped", align_bytes=64)
         for part in range(2):
             column_pairs = slice(part * N // 8, (part + 1) * N // 8)
             nc.scalar.copy(
                 w4_grouped[:].rearrange("p (c i j) -> p c j i", i=4, j=PACK)[:, column_pairs],
-                w4_raw[:].rearrange("p j (c i) -> p c j i", i=4)[:, column_pairs],
+                w4_raw.rearrange("p j (c i) -> p c j i", i=4)[:, column_pairs],
             )
 
-        back = summed("z0", 4, [terms_of(0, blk) for blk in (0, 1, 3, 2)], "w4_raw")
-        nc.scalar.copy(za[:, :half], back[:, :half])
-        nc.scalar.copy(late_slots[:, 0:4:3], back[:, half:].rearrange("p (s n) -> p s n", n=P))
-        back = summed("z1_first", 5, [terms_of(1, blk) for blk in (0, 1)], "z1_first_held")
-        nc.scalar.copy(za[:, half:S], back[:, :half])
-        z1_second = summed("z1_second", 6, [terms_of(1, blk) for blk in (3, 2)], "z1_second_held")
-        nc.scalar.copy(late_slots[:, 1, :], z1_second[:, :P])
+        both_second = sb.tile([P, 3 * half], F32, name="both_second")
+        back = summed("both1", 4, [directions_of(1, blk) for blk in (2, 3)], 2)
+        nc.scalar.copy(both_second[:, :half], back[:, :half])
+        back = summed("both23", 5, [directions_of(t, blk) for t in (2, 3) for blk in (2, 3)], 3)
+        nc.scalar.copy(both_second[:, half:], back[:])
+        back = summed("z0", 6, [terms_of(0, blk) for blk in (0, 1, 3, 2)], 0)
+        nc.scalar.copy(z_first[:, 0, :], back[:, :half])
+        nc.scalar.copy(slots[:, 0:5:4, :P], back[:, half:].rearrange("p (s n) -> p s n", n=P))
+        back = summed("z1", 7, [terms_of(1, blk) for blk in (0, 1)], 1)
+        nc.scalar.copy(z_first[:, 1, :], back[:, :half])
 
-        partial3 = sb.tile([P, half + P], F32, name="partial3")
-        partial = {("a", 2): y_sb[3][:, :half], ("b", 2): y_sb[3][:, half : half + P], ("c", 2): za[:, S : S + P]}
-        partial.update({("a", 3): partial3[:, :half], ("b", 3): partial3[:, half:], ("c", 3): za[:, S + P : S + 2 * P]})
-        both = {"a": both_first[:], "b": both_second[:, :, :P], "c": both_second[:, :, P:]}
+        def entries(side, c0, width):
+            return places[side][:, c0 // LIST : (c0 + width) // LIST]
 
-        def chained(name, between):
-            c0, width, z = chunks[name]
-            entries = [places[side][:, c0 // LIST : (c0 + width) // LIST] for side in range(2)]
-            for t in (2, 3):
-                nc.vector.tensor_tensor(partial[name, t], m_win[t][:].indirect(entries[0]), both[name][:, t - 2, :], ADD)
-            between()
-            for t in (2, 3):
-                nc.vector.tensor_tensor(z[:, t, :], m_win[t][:].indirect(entries[1]), partial[name, t], ADD)
+        partial3 = sb.tile([P, half], F32, name="partial3")
+        first_partial = {2: y3_home[:, P : P + half], 3: partial3[:]}
+        second_partial = {
+            1: y3_home[:, P + half : P + 2 * half],
+            2: y3_home[:, P + 2 * half : P + 3 * half],
+            3: slots[:, 8, :],
+        }
+        for t in (2, 3):
+            nc.vector.tensor_tensor(first_partial[t], m_win[t][:].indirect(entries(0, 0, half)), both_first[:, t - 2, :], ADD)
+        for t in (2, 3):
+            nc.vector.tensor_tensor(z_first[:, t, :], m_win[t][:].indirect(entries(1, 0, half)), first_partial[t], ADD)
 
         out_rows = out.rearrange("(a p) n -> p a n", p=P)
         w4_codes = shared.tile([P, N], U32, name="w4_codes", offset=0, align_bytes=64)
         w4_plane = sb.tile([P, N], U8, name="w4_plane", align_bytes=64)
         w4_mx = (w4_codes, w4_plane)
+        quantise(w4_mx, 0, w4_grouped[:])
 
-        def rounded(name, copy):
-            c0, width, z = chunks[name]
-            grouped = sb.tile([P, PACK * width], BF16, name=name + "_grouped", align_bytes=64)
+        def round_chunk(name, copy, grouped):
             copy(
-                grouped[:].rearrange("p (c i t) -> p c t i", t=PACK, i=4),
-                z.rearrange("p t (c i) -> p c t i", i=4),
+                grouped.rearrange("p (c i t) -> p c t i", t=PACK, i=4),
+                chunks[name][2].rearrange("p t (c i) -> p c t i", i=4),
             )
-            return grouped
 
-        def last_layer(name, grouped, out_banks, on_vector):
-            c0, width, z = chunks[name]
-            z_mx = mx_tiles("z" + name, width)
-            quantise(z_mx, 0, grouped[:])
+        def multiply(name, z_mx, out_banks):
+            width = chunks[name][1]
             per_bank = PACK // len(out_banks)
-            for no, b in enumerate(out_banks):
-                acc = bank(b, name + "_out%d" % no)
-                for a in range(per_bank):
-                    product(acc[:, a * width : (a + 1) * width], w4_mx, no * per_bank + a, z_mx)
-                if name == "a":
-                    staged = z_home[:, 4 + no, :S].rearrange("p (a n) -> p a n", a=per_bank)
-                else:
-                    staged_tile = sb.tile([P, per_bank, width], F32, name=name + "_staged%d" % no)
-                    staged = staged_tile[:]
-                src = acc[:, : per_bank * width].rearrange("p (a n) -> p a n", a=per_bank)
-                dst = out_rows[:, no * per_bank : (no + 1) * per_bank, c0 : c0 + width]
-                if no in on_vector:
-                    nc.vector.tensor_copy(staged, src)
-                else:
-                    nc.scalar.copy(staged, src)
-                nc.sync.dma_start(dst, staged)
+            accs = [bank(b, name + "_out%d" % no) for no, b in enumerate(out_banks)]
+            for a in range(PACK):
+                col = a % per_bank * width
+                product(accs[a // per_bank][:, col : col + width], w4_mx, a, z_mx)
+            return accs
 
-        chained("a", lambda: None)
-        a_grouped = rounded("a", nc.scalar.copy)
-        nc.scalar.copy(late_slots[:, 4, :], z1_second[:, P:half])
-        chained("b", lambda: quantise(w4_mx, 0, w4_grouped[:]))
-        b_grouped = rounded("b", nc.scalar.copy)
-        last_layer("a", a_grouped, (0, 1), ())
-        chained("c", lambda: None)
-        last_layer("b", b_grouped, (2,), ())
-        last_layer("c", rounded("c", nc.vector.tensor_copy), (3, 4, 5, 6), (1, 3))
+        def store(name, accs, no, copy, home=None):
+            c0, width, z = chunks[name]
+            per_bank = PACK // len(accs)
+            if home is None:
+                home = sb.tile([P, per_bank * width], F32, name=name + "_staged%d" % no)[:]
+            staged = home.rearrange("p (a n) -> p a n", a=per_bank)
+            copy(staged, accs[no][:, : per_bank * width].rearrange("p (a n) -> p a n", a=per_bank))
+            nc.sync.dma_start(out_rows[:, no * per_bank : (no + 1) * per_bank, c0 : c0 + width], staged)
+
+        a_grouped = z_home[:, half : 3 * half].bitcast(BF16)
+        round_chunk("a", nc.scalar.copy, a_grouped)
+        a_codes = shared.tile([P, half], U32, name="a_codes", offset=4 * N, align_bytes=64)
+        a_plane = sb.tile([P, half], U8, name="a_plane", align_bytes=64)
+        a_mx = (a_codes, a_plane)
+        quantise(a_mx, 0, a_grouped)
+        a_out = multiply("a", a_mx, (0, 1))
+        store("a", a_out, 0, nc.scalar.copy)
+
+        for t in (1, 2, 3):
+            nc.vector.tensor_tensor(
+                second_partial[t],
+                m_win[t][:].indirect(entries(0, half, half)),
+                both_second[:, (t - 1) * half : t * half],
+                ADD,
+            )
+
+        def finish(name):
+            c0, width, z = chunks[name]
+            for t in (1, 2, 3):
+                partial = second_partial[t][:, c0 - half : c0 - half + width]
+                nc.vector.tensor_tensor(z[:, t, :], m_win[t][:].indirect(entries(1, c0, width)), partial, ADD)
+
+        finish("b")
+        b_grouped = shared.tile([P, PACK * P], BF16, name="b_grouped", offset=4 * N, align_bytes=64)
+        round_chunk("b", nc.scalar.copy, b_grouped[:])
+        store("a", a_out, 1, nc.scalar.copy)
+        finish("c")
+        b_mx, c_mx = mx_tiles("zb", P), mx_tiles("zc", P)
+        quantise(b_mx, 0, b_grouped[:])
+        c_grouped = slots[:, 7, :].bitcast(BF16)
+        round_chunk("c", nc.vector.tensor_copy, c_grouped)
+        quantise(c_mx, 0, c_grouped)
+        b_out = multiply("b", b_mx, (2, 3))
+        c_out = multiply("c", c_mx, (4, 5, 6, 7))
+        store("b", b_out, 0, nc.scalar.copy)
+        store("b", b_out, 1, nc.vector.tensor_copy, slots[:, 7, :])
+        for no in range(PACK):
+            store("c", c_out, no, nc.vector.tensor_copy if no % 2 else nc.scalar.copy)

@@ -20,7 +20,8 @@ P = 128
 PACK = 4
 LIST = 16
 BANK = 512
-VECTOR_COLUMNS = 384
+VECTOR_COLUMNS = 256
+VECTOR_ATOMS = 80
 ROWS = 8
 
 
@@ -265,10 +266,10 @@ def tile_picked_painn8_none_p_kernel(
         w4_mx = (w4_codes, w4_plane)
         quantise(w4_mx, 0, w4_grouped[:])
 
-        def round_chunk(name, copy, grouped):
+        def round_chunk(name, copy, grouped, fours=slice(None)):
             copy(
-                grouped.rearrange("p (c i t) -> p c t i", t=PACK, i=4),
-                chunks[name][2].rearrange("p t (c i) -> p c t i", i=4),
+                grouped.rearrange("p (c i t) -> p c t i", t=PACK, i=4)[:, fours],
+                chunks[name][2].rearrange("p t (c i) -> p c t i", i=4)[:, fours],
             )
 
         def multiply(name, z_mx, out_banks):
@@ -317,10 +318,11 @@ def tile_picked_painn8_none_p_kernel(
         round_chunk("b", nc.scalar.copy, b_grouped[:])
         store("a", a_out, 1, nc.scalar.copy)
         finish("c")
+        c_grouped = slots[:, 7, :].bitcast(BF16)
+        round_chunk("c", nc.scalar.copy, c_grouped, slice(VECTOR_ATOMS // 4, P // 4))
         b_mx, c_mx = mx_tiles("zb", P), mx_tiles("zc", P)
         quantise(b_mx, 0, b_grouped[:])
-        c_grouped = slots[:, 7, :].bitcast(BF16)
-        round_chunk("c", nc.vector.tensor_copy, c_grouped)
+        round_chunk("c", nc.vector.tensor_copy, c_grouped, slice(0, VECTOR_ATOMS // 4))
         quantise(c_mx, 0, c_grouped)
         b_out = multiply("b", b_mx, (2, 3))
         c_out = multiply("c", c_mx, (4, 5, 6, 7))

@@ -71,9 +71,6 @@ def tile_picked_painn8_none_p_kernel(
         for t in range(PACK):
             nc.sync.dma_start(w4_raw[:, t, :], w4.rearrange("(b t r) c -> t b r c", t=PACK, r=ROWS)[t])
 
-        ident = sb.tile([P, P], F32, name="ident")
-        make_identity(nc, ident[:])
-
         x_codes = sb.tile([P, S], U32, name="x_codes", align_bytes=64)
         x_plane = sb.tile([P, S], U8, name="x_plane", align_bytes=64)
         nc.vector.tensor_copy(x_codes[:], words_all[:].bitcast(U32).indirect(offs_sb[:]))
@@ -110,6 +107,10 @@ def tile_picked_painn8_none_p_kernel(
         q_win = [sb.tile([P, 2 * S], F32, name="q_win%d" % t) for t in range(PACK)]
         for t in range(PACK):
             nc.vector.memset(q_win[t][:, S:], 0.0)
+        ident = sb.tile([P, P], F32, name="ident")
+        nc.vector.memset(ident[:], 0.0)
+        make_identity(nc, ident[:], nomemset=True)
+
         w3_mx = mx_tiles("w3", H)
         w3_grouped = sb.tile([P, PACK * H], BF16, name="w3_grouped", align_bytes=64)
         round_tile(nc.vector.tensor_copy, w3_grouped, w3_raw[:], 0)
@@ -299,16 +300,17 @@ def tile_picked_painn8_none_p_kernel(
         a_out = multiply("a", a_mx, (0, 1))
         store("a", a_out, 0, nc.scalar.copy)
 
-        for t in (1, 2, 3):
-            nc.vector.tensor_tensor(
-                second_partial[t],
-                m_win[t][:].indirect(entries(0, half, half)),
-                both_second[:, (t - 1) * half : t * half],
-                ADD,
-            )
+        def begin(t, c0, width):
+            cols = slice(c0 - half, c0 - half + width)
+            summed_directions = both_second[:, (t - 1) * half : t * half][:, cols]
+            nc.vector.tensor_tensor(second_partial[t][:, cols], m_win[t][:].indirect(entries(0, c0, width)), summed_directions, ADD)
+
+        for t in (1, 2):
+            begin(t, half, half)
 
         def finish(name):
             c0, width, z = chunks[name]
+            begin(3, c0, width)
             for t in (1, 2, 3):
                 partial = second_partial[t][:, c0 - half : c0 - half + width]
                 nc.vector.tensor_tensor(z[:, t, :], m_win[t][:].indirect(entries(1, c0, width)), partial, ADD)

@@ -22,7 +22,7 @@ LIST = 16
 BANK = 512
 VECTOR_COLUMNS = 256
 VECTOR_ATOMS = 80
-ROWS = 8
+ROWS = 4
 
 
 def tile_picked_painn8_none_p_kernel(
@@ -79,8 +79,8 @@ def tile_picked_painn8_none_p_kernel(
 
         def round_tile(copy, grouped, raw, t):
             copy(
-                grouped[:, t * H : (t + 1) * H].rearrange("p (b h i j) -> p b h j i", h=2, i=4, j=PACK),
-                raw.rearrange("p j (b t h i) -> p t b h j i", t=PACK, h=2, i=4)[:, t],
+                grouped[:].rearrange("p (t g r j) -> p t g j r", t=PACK, r=ROWS, j=PACK)[:, t],
+                raw.rearrange("p j (g t r) -> p t g j r", t=PACK, r=ROWS)[:, t],
             )
 
         def mx_tiles(name, width):
@@ -135,9 +135,9 @@ def tile_picked_painn8_none_p_kernel(
         w1_grouped = sb.tile([P, PACK * H], BF16, name="w1_grouped", align_bytes=64)
         w2_grouped = sb.tile([P, PACK * H], BF16, name="w2_grouped", align_bytes=64)
         pair_cols = [slice(u * 2 * H, (u + 1) * 2 * H) for u in range(2)]
-        for raw, grouped in ((w1_raw, w1_grouped), (w2_raw[:], w2_grouped)):
-            for t in range(PACK):
-                round_tile(nc.scalar.copy, grouped, raw, t)
+        round_tile(nc.scalar.copy, w1_grouped, w1_raw, slice(None))
+        for u in range(2):
+            round_tile(nc.scalar.copy, w2_grouped, w2_raw[:], slice(2 * u, 2 * u + 2))
         quantise(w1_mx, 0, w1_grouped[:])
         for u in range(2):
             quantise(w2_mx, 2 * u * P, w2_grouped[:, pair_cols[u]])
@@ -310,11 +310,11 @@ def tile_picked_painn8_none_p_kernel(
 
         def finish(name):
             c0, width, z = chunks[name]
-            begin(3, c0, width)
             for t in (1, 2, 3):
                 partial = second_partial[t][:, c0 - half : c0 - half + width]
                 nc.vector.tensor_tensor(z[:, t, :], m_win[t][:].indirect(entries(1, c0, width)), partial, ADD)
 
+        begin(3, half, half)
         finish("b")
         b_grouped = shared.tile([P, PACK * P], BF16, name="b_grouped", offset=4 * N, align_bytes=64)
         round_chunk("b", nc.scalar.copy, b_grouped[:])

@@ -77,10 +77,16 @@ def tile_picked_painn8_none_p_kernel(
         nc.vector.tensor_copy(x_plane[:], scales_all[:].indirect(offs_sb[:]))
         x_mx = (x_codes, x_plane)
 
-        def round_tile(copy, grouped, raw, t):
+        def round_tile(copy, grouped, raw, t, blocks=slice(None)):
             copy(
-                grouped[:].rearrange("p (t g r j) -> p t g j r", t=PACK, r=ROWS, j=PACK)[:, t],
-                raw.rearrange("p j (g t r) -> p t g j r", t=PACK, r=ROWS)[:, t],
+                grouped.rearrange("p (g r j) -> p g j r", r=ROWS, j=PACK)[:, blocks],
+                raw.rearrange("p j (g t r) -> p t g j r", t=PACK, r=ROWS)[:, t, blocks],
+            )
+
+        def round_tiles(grouped, raw, tiles):
+            nc.scalar.copy(
+                grouped[:].rearrange("p (t g r j) -> p t g j r", t=PACK, r=ROWS, j=PACK)[:, tiles],
+                raw.rearrange("p j (g t r) -> p t g j r", t=PACK, r=ROWS)[:, tiles],
             )
 
         def mx_tiles(name, width):
@@ -111,33 +117,39 @@ def tile_picked_painn8_none_p_kernel(
         nc.vector.memset(ident[:], 0.0)
         make_identity(nc, ident[:], nomemset=True)
 
-        w3_mx = mx_tiles("w3", H)
-        w3_grouped = sb.tile([P, PACK * H], BF16, name="w3_grouped", align_bytes=64)
-        round_tile(nc.vector.tensor_copy, w3_grouped, w3_raw[:], 0)
-        quantise(w3_mx, 0, w3_grouped[:, :H])
+        w3_home = sb.tile([P, 7 * H // 2], BF16, name="w3_home", align_bytes=64)
+        w3_start = (0, 5 * H // 2, H // 2, 3 * H // 2)
+        w3_grouped = [w3_home[:, c0 : c0 + H] for c0 in w3_start]
+        w3_codes = sb.tile([P, 3 * P], U32, name="w3_codes", align_bytes=64)
+        w3_first = (w3_codes, sb.tile([P, P], U8, name="w3_plane0", align_bytes=64))
+        w3_mx = (w3_codes, sb.tile([P, 3 * P], U8, name="w3_plane", align_bytes=64))
+        blocks_half = H // (2 * PACK * ROWS)
+        round_tile(nc.vector.tensor_copy, w3_grouped[0], w3_raw[:], 0, slice(0, blocks_half))
+        round_tile(nc.scalar.copy, w3_grouped[0], w3_raw[:], 0, slice(blocks_half, 2 * blocks_half))
+        quantise(w3_first, 0, w3_grouped[0])
         for t in (1, 3):
-            round_tile(nc.scalar.copy, w3_grouped, w3_raw[:], t)
-        round_tile(nc.vector.tensor_copy, w3_grouped, w3_raw[:], 2)
-        quantise(w3_mx, P, w3_grouped[:, H : 2 * H])
-        quantise(w3_mx, 2 * P, w3_grouped[:, 2 * H :])
+            round_tile(nc.scalar.copy, w3_grouped[t], w3_raw[:], t)
+        round_tile(nc.vector.tensor_copy, w3_grouped[2], w3_raw[:], 2)
+        quantise(w3_mx, 2 * P, w3_grouped[1])
         low, high = slice(0, S // 2), slice(S // 2, S)
         q_low, q_high = bank(0, "q_low"), bank(4, "q_high")
-        product(q_low[:, low], w3_mx, 0, x_mx, low)
-        product(q_high[:, low], w3_mx, 0, x_mx, high)
+        product(q_low[:, low], w3_first, 0, x_mx, low)
+        product(q_high[:, low], w3_first, 0, x_mx, high)
         nc.vector.tensor_copy(q_win[0][:, low], q_low[:, low])
         nc.scalar.copy(q_win[0][:, high], q_high[:, low])
-        for t in range(1, PACK):
+        quantise(w3_mx, 0, w3_home[:, H // 2 : 5 * H // 2])
+        for t, place in ((1, 2), (2, 0), (3, 1)):
             acc = bank(t, "q_acc%d" % t)
-            product(acc[:], w3_mx, t, x_mx)
+            product(acc[:], w3_mx, place, x_mx)
             nc.scalar.copy(q_win[t][:, :S], acc[:])
 
         w1_mx, w2_mx = mx_tiles("w1", H), mx_tiles("w2", H)
         w1_grouped = sb.tile([P, PACK * H], BF16, name="w1_grouped", align_bytes=64)
         w2_grouped = sb.tile([P, PACK * H], BF16, name="w2_grouped", align_bytes=64)
         pair_cols = [slice(u * 2 * H, (u + 1) * 2 * H) for u in range(2)]
-        round_tile(nc.scalar.copy, w1_grouped, w1_raw, slice(None))
+        round_tiles(w1_grouped, w1_raw, slice(None))
         for u in range(2):
-            round_tile(nc.scalar.copy, w2_grouped, w2_raw[:], slice(2 * u, 2 * u + 2))
+            round_tiles(w2_grouped, w2_raw[:], slice(2 * u, 2 * u + 2))
         quantise(w1_mx, 0, w1_grouped[:])
         for u in range(2):
             quantise(w2_mx, 2 * u * P, w2_grouped[:, pair_cols[u]])

@@ -61,13 +61,13 @@ def tile_picked_painn8_none_p_kernel(
         nc.sync.dma_start(directions[0][:], dir1)
         nc.sync.dma_start(p2_sb[:], p2)
         nc.sync.dma_start(directions[1][:], dir2)
-        w1_home = sb.tile([P, S + PACK * H], F32, name="w1_home")
-        w1_raw = w1_home[:, S:].rearrange("p (j c) -> p j c", j=PACK)
-        w2_raw = sb.tile([P, PACK, H], F32, name="w2_raw", tag="w2_raw")
+        w1_raw = sb.tile([P, PACK, H], F32, name="w1_raw")
+        w2_home = sb.tile([P, S + PACK * H], F32, name="w2_home")
+        w2_raw = w2_home[:, S:].rearrange("p (j c) -> p j c", j=PACK)
         w4_home = sb.tile([P, PACK * N], F32, name="w4_home")
         w4_raw = w4_home[:].rearrange("p (t c) -> p t c", t=PACK)
-        nc.sync.dma_start(w1_raw, by_rows(w1))
-        nc.sync.dma_start(w2_raw[:], by_rows(w2))
+        nc.sync.dma_start(w1_raw[:], by_rows(w1))
+        nc.sync.dma_start(w2_raw, by_rows(w2))
         for t in range(PACK):
             nc.sync.dma_start(w4_raw[:, t, :], w4.rearrange("(b t r) c -> t b r c", t=PACK, r=ROWS)[t])
 
@@ -147,12 +147,27 @@ def tile_picked_painn8_none_p_kernel(
         w1_grouped = sb.tile([P, PACK * H], BF16, name="w1_grouped", align_bytes=64)
         w2_grouped = sb.tile([P, PACK * H], BF16, name="w2_grouped", align_bytes=64)
         pair_cols = [slice(u * 2 * H, (u + 1) * 2 * H) for u in range(2)]
-        round_tiles(w1_grouped, w1_raw, slice(None))
+        round_tiles(w1_grouped, w1_raw[:], slice(None))
         for u in range(2):
-            round_tiles(w2_grouped, w2_raw[:], slice(2 * u, 2 * u + 2))
+            round_tiles(w2_grouped, w2_raw, slice(2 * u, 2 * u + 2))
+        early = sb.tile([P, 4 * S], F32, name="along_early")
+        late = [w2_home[:, : 2 * S], w2_home[:, 2 * S : 4 * S]]
+        along = {(t, side): early[:, (2 * t + side) * S : (2 * t + side + 1) * S] for t in range(2) for side in range(2)}
+        for t in (2, 3):
+            for side in range(2):
+                along[t, side] = late[side][:, (t - 2) * S : (t - 1) * S]
+
+        def fetch_along(t, side):
+            nc.vector.tensor_tensor(along[t, side], q_win[t][:].indirect(places[side][:]), directions[side][:], MULT)
+
+        for t, side in ((0, 0), (0, 1), (1, 0), (1, 1), (2, 0)):
+            fetch_along(t, side)
         quantise(w1_mx, 0, w1_grouped[:])
-        for u in range(2):
-            quantise(w2_mx, 2 * u * P, w2_grouped[:, pair_cols[u]])
+        quantise(w2_mx, 0, w2_grouped[:, pair_cols[0]])
+        fetch_along(3, 0)
+        quantise(w2_mx, 2 * P, w2_grouped[:, pair_cols[1]])
+        fetch_along(2, 1)
+        fetch_along(3, 1)
         y_tiles = [sb.tile([P, S], F32, name="y_sb%d" % t) for t in range(PACK - 1)]
         y3_home = sb.tile([P, 2 * S], F32, name="y3_home")
         y_sb = [tile[:] for tile in y_tiles] + [y3_home[:, S // 2 : 3 * S // 2]]
@@ -167,17 +182,6 @@ def tile_picked_painn8_none_p_kernel(
             nc.scalar.copy(y_sb[t], y_acc[:])
             if t > 0:
                 nc.scalar.copy(e_sb[t][:, on_gpsimd[t]], e_acc[t][:, on_gpsimd[t]])
-
-        early = sb.tile([P, 4 * S], F32, name="along_early")
-        late_second = sb.tile([P, 2 * S], F32, name="along_late1", tag="w2_raw")
-        late = [w1_home[:, : 2 * S], late_second[:]]
-        along = {}
-        for t, side in ((0, 0), (0, 1), (1, 0), (1, 1), (2, 0), (3, 0), (2, 1), (3, 1)):
-            if t < 2:
-                along[t, side] = early[:, (2 * t + side) * S : (2 * t + side + 1) * S]
-            else:
-                along[t, side] = late[side][:, (t - 2) * S : (t - 1) * S]
-            nc.vector.tensor_tensor(along[t, side], q_win[t][:].indirect(places[side][:]), directions[side][:], MULT)
 
         m_win = [q_win[0]] + [
             sb.tile([P, S], F32, name="m_win%d" % t, tag=tag) for t, tag in ((1, "dir2_sb"), (2, "m_win2"), (3, "m_win3"))

@@ -20,7 +20,7 @@ P = 128
 PACK = 4
 LIST = 16
 BANK = 512
-VECTOR_COLUMNS = 256
+VECTOR_COLUMNS = 192
 VECTOR_ATOMS = 80
 ROWS = 4
 
@@ -110,7 +110,7 @@ def tile_picked_painn8_none_p_kernel(
                 stop=True,
             )
 
-        q_win = [sb.tile([P, 2 * S], F32, name="q_win%d" % t) for t in range(PACK)]
+        q_win = [sb.tile([P, 2 * S], F32, name="q_win%d" % t, tag="q_win%d" % t) for t in range(PACK)]
         for t in range(PACK):
             nc.vector.memset(q_win[t][:, S:], 0.0)
         ident = sb.tile([P, P], F32, name="ident")
@@ -168,10 +168,11 @@ def tile_picked_painn8_none_p_kernel(
         quantise(w2_mx, 2 * P, w2_grouped[:, pair_cols[1]])
         fetch_along(2, 1)
         fetch_along(3, 1)
-        y_tiles = [sb.tile([P, S], F32, name="y_sb%d" % t) for t in range(PACK - 1)]
+        y_tiles = [sb.tile([P, S], F32, name="y_sb%d" % t) for t in (0, 2)]
         y3_home = sb.tile([P, 2 * S], F32, name="y3_home")
-        y_sb = [tile[:] for tile in y_tiles] + [y3_home[:, S // 2 : 3 * S // 2]]
-        e_sb = {t: sb.tile([P, S], F32, name="e_sb%d" % t) for t in (1, 2)}
+        ye1 = sb.tile([P, 2 * S], F32, name="ye1")
+        y_sb = [y_tiles[0][:], ye1[:, :S], y_tiles[1][:], y3_home[:, S // 2 : 3 * S // 2]]
+        e_sb = {1: ye1[:, S:], 2: sb.tile([P, S], F32, name="e_sb2")}
         e_sb[3] = shared.tile([P, S], F32, name="e_sb3", offset=0, align_bytes=64)
         on_gpsimd = {1: slice(VECTOR_COLUMNS, S), 2: slice(0, S), 3: slice(0, S)}
         e_acc = [bank(t, "e_acc%d" % t) for t in range(PACK)]
@@ -184,23 +185,28 @@ def tile_picked_painn8_none_p_kernel(
                 nc.scalar.copy(e_sb[t][:, on_gpsimd[t]], e_acc[t][:, on_gpsimd[t]])
 
         m_win = [q_win[0]] + [
-            sb.tile([P, S], F32, name="m_win%d" % t, tag=tag) for t, tag in ((1, "dir2_sb"), (2, "m_win2"), (3, "m_win3"))
+            sb.tile([P, S], F32, name="m_win%d" % t, tag=tag) for t, tag in ((1, "q_win2"), (2, "m_win2"), (3, "m_win3"))
         ]
         nc.vector.tensor_tensor(m_win[0][:, :S], e_acc[0][:], y_sb[0], MULT)
         nc.vector.tensor_tensor(
             m_win[1][:, :VECTOR_COLUMNS], e_acc[1][:, :VECTOR_COLUMNS], y_sb[1][:, :VECTOR_COLUMNS], MULT
         )
         half = S // 2
-        both_first = sb.tile([P, 2, half], F32, name="both_first")
+        both_first = ye1[:].rearrange("p (t n) -> p t n", t=2)[:, :, half:]
+
+        def multiply_on_gpsimd(t):
+            cols = on_gpsimd[t]
+            nc.gpsimd.tensor_tensor(m_win[t][:, cols], e_sb[t][:, cols], y_sb[t][:, cols], MULT)
+
+        multiply_on_gpsimd(1)
         nc.gpsimd.tensor_tensor(
-            both_first[:],
+            both_first,
             late[0].rearrange("p (t n) -> p t n", t=2)[:, :, :half],
             late[1].rearrange("p (t n) -> p t n", t=2)[:, :, :half],
             ADD,
         )
-        for t in range(1, PACK):
-            cols = on_gpsimd[t]
-            nc.gpsimd.tensor_tensor(m_win[t][:, cols], e_sb[t][:, cols], y_sb[t][:, cols], MULT)
+        for t in (2, 3):
+            multiply_on_gpsimd(t)
 
         def summed(name, b, blocks, row):
             turned = bank(b, name + "_turned")

@@ -48,15 +48,17 @@ def tile_picked_painn8_none_p_kernel(
 
         words_all = sb.tile([P, T], I32, name="words_all", align_bytes=64)
         scales_all = sb.tile([P, T], U8, name="scales_all", align_bytes=64)
-        nc.vector.memset(scales_all[:].bitcast(I32), 0)
+        nc.gpsimd.memset(scales_all[:].bitcast(I32), 0)
 
         w3_raw = sb.tile([P, PACK, H], F32, name="w3_raw")
-        nc.sync.dma_start(words_all[:], x_words[0].rearrange("p n t -> p (n t)").bitcast(I32))
+        words_hbm = x_words[0].rearrange("p n t -> p (n t)").bitcast(I32)
+        nc.sync.dma_start(words_all[:, : T // 2], words_hbm[:, : T // 2])
         nc.sync.dma_start(offs_sb[:], offs)
-        nc.sync.dma_start(p1_sb[:], p1)
         for row in range(4):
             nc.sync.dma_start(scales_all[row:P:32, :].bitcast(I32), x_scales[0, row:16:4, :].bitcast(I32))
+        nc.sync.dma_start(words_all[:, T // 2 :], words_hbm[:, T // 2 :])
         nc.sync.dma_start(w3_raw[:], by_rows(w3))
+        nc.sync.dma_start(p1_sb[:], p1)
         directions = [sb.tile([P, S], F32, name=name, tag=name) for name in ("dir1_sb", "dir2_sb")]
         nc.sync.dma_start(directions[0][:], dir1)
         nc.sync.dma_start(p2_sb[:], p2)
@@ -73,8 +75,8 @@ def tile_picked_painn8_none_p_kernel(
 
         x_codes = sb.tile([P, S], U32, name="x_codes", align_bytes=64)
         x_plane = sb.tile([P, S], U8, name="x_plane", align_bytes=64)
-        nc.vector.tensor_copy(x_codes[:], words_all[:].bitcast(U32).indirect(offs_sb[:]))
         nc.vector.tensor_copy(x_plane[:], scales_all[:].indirect(offs_sb[:]))
+        nc.vector.tensor_copy(x_codes[:], words_all[:].bitcast(U32).indirect(offs_sb[:]))
         x_mx = (x_codes, x_plane)
 
         def round_tile(copy, grouped, raw, t, blocks=slice(None)):
@@ -112,9 +114,9 @@ def tile_picked_painn8_none_p_kernel(
 
         q_win = [sb.tile([P, 2 * S], F32, name="q_win%d" % t, tag="q_win%d" % t) for t in range(PACK)]
         for t in range(PACK):
-            nc.vector.memset(q_win[t][:, S:], 0.0)
+            nc.gpsimd.memset(q_win[t][:, S:], 0.0)
         ident = sb.tile([P, P], F32, name="ident")
-        nc.vector.memset(ident[:], 0.0)
+        nc.gpsimd.memset(ident[:], 0.0)
         make_identity(nc, ident[:], nomemset=True)
 
         w3_home = sb.tile([P, 7 * H // 2], BF16, name="w3_home", align_bytes=64)

@@ -15,14 +15,14 @@ U8 = mybir.dt.uint8
 FP8X4 = mybir.dt.float8_e4m3fn_x4
 MULT = mybir.AluOpType.mult
 ADD = mybir.AluOpType.add
+COPY = mybir.ActivationFunctionType.Copy
 
 P = 128
 PACK = 4
 LIST = 16
 BANK = 512
-VECTOR_COLUMNS = 192
-VECTOR_ATOMS = 80
 ROWS = 4
+CHUNKS = S // P
 
 
 def tile_picked_painn8_none_p_kernel(
@@ -32,7 +32,6 @@ def tile_picked_painn8_none_p_kernel(
     with ExitStack() as ctx:
         lists = ctx.enter_context(tc.tile_pool(name="lists", bufs=1))
         sb = ctx.enter_context(tc.tile_pool(name="sb", bufs=1))
-        shared = ctx.enter_context(tc.tile_pool(name="shared", bufs=1))
         psum = ctx.enter_context(tc.psum_pool(name="psum", bufs=1))
 
         def bank(b, name):
@@ -48,57 +47,50 @@ def tile_picked_painn8_none_p_kernel(
 
         words_all = sb.tile([P, T], I32, name="words_all", align_bytes=64)
         scales_all = sb.tile([P, T], U8, name="scales_all", align_bytes=64)
-        nc.gpsimd.memset(scales_all[:].bitcast(I32), 0)
+        nc.vector.memset(scales_all[:].bitcast(I32), 0)
+        scale_rows = sb.tile([4, 4, T // 4], I32, name="scale_rows")
+        nc.sync.dma_start(scale_rows[:], x_scales[0].bitcast(I32).rearrange("(q r) c -> r q c", r=4))
 
         w3_raw = sb.tile([P, PACK, H], F32, name="w3_raw")
-        words_hbm = x_words[0].rearrange("p n t -> p (n t)").bitcast(I32)
-        nc.sync.dma_start(words_all[:, : T // 2], words_hbm[:, : T // 2])
-        nc.sync.dma_start(offs_sb[:], offs)
-        for row in range(4):
-            nc.sync.dma_start(scales_all[row:P:32, :].bitcast(I32), x_scales[0, row:16:4, :].bitcast(I32))
-        nc.sync.dma_start(words_all[:, T // 2 :], words_hbm[:, T // 2 :])
         nc.sync.dma_start(w3_raw[:], by_rows(w3))
+        nc.sync.dma_start(offs_sb[:], offs)
+        nc.sync.dma_start(words_all[:], x_words[0].rearrange("p n t -> p (n t)").bitcast(I32))
         nc.sync.dma_start(p1_sb[:], p1)
-        directions = [sb.tile([P, S], F32, name=name, tag=name) for name in ("dir1_sb", "dir2_sb")]
+        directions = [sb.tile([P, S], F32, name=name) for name in ("dir1_sb", "dir2_sb")]
         nc.sync.dma_start(directions[0][:], dir1)
         nc.sync.dma_start(p2_sb[:], p2)
         nc.sync.dma_start(directions[1][:], dir2)
         w1_raw = sb.tile([P, PACK, H], F32, name="w1_raw")
-        w2_home = sb.tile([P, S + PACK * H], F32, name="w2_home")
-        w2_raw = w2_home[:, S:].rearrange("p (j c) -> p j c", j=PACK)
-        w4_home = sb.tile([P, PACK * N], F32, name="w4_home")
-        w4_raw = w4_home[:].rearrange("p (t c) -> p t c", t=PACK)
+        w2_raw = sb.tile([P, PACK, H], F32, name="w2_raw")
+        w4_raw = sb.tile([P, PACK, N], F32, name="w4_raw")
         nc.sync.dma_start(w1_raw[:], by_rows(w1))
-        nc.sync.dma_start(w2_raw, by_rows(w2))
+        nc.sync.dma_start(w2_raw[:], by_rows(w2))
+        nc.sync.dma_start(w4_raw[:], by_rows(w4))
+
+        for quarter in range(4):
+            nc.vector.tensor_copy(scales_all[32 * quarter : 32 * quarter + 4, :].bitcast(I32), scale_rows[:, quarter, :])
+
+        q_win = [sb.tile([P, 2 * S], F32, name="q_win%d" % t) for t in range(PACK)]
         for t in range(PACK):
-            nc.sync.dma_start(w4_raw[:, t, :], w4.rearrange("(b t r) c -> t b r c", t=PACK, r=ROWS)[t])
+            nc.gpsimd.memset(q_win[t][:, S:], 0.0)
+        ident = sb.tile([P, P], F32, name="ident")
+        nc.gpsimd.memset(ident[:], 0.0)
+        make_identity(nc, ident[:], nomemset=True)
 
-        x_codes = sb.tile([P, S], U32, name="x_codes", align_bytes=64)
-        x_plane = sb.tile([P, S], U8, name="x_plane", align_bytes=64)
-        nc.vector.tensor_copy(x_plane[:], scales_all[:].indirect(offs_sb[:]))
-        nc.vector.tensor_copy(x_codes[:], words_all[:].bitcast(U32).indirect(offs_sb[:]))
-        x_mx = (x_codes, x_plane)
-
-        def round_tile(copy, grouped, raw, t, blocks=slice(None)):
+        def round_tiles(copy, grouped, raw, tiles):
             copy(
-                grouped.rearrange("p (g r j) -> p g j r", r=ROWS, j=PACK)[:, blocks],
-                raw.rearrange("p j (g t r) -> p t g j r", t=PACK, r=ROWS)[:, t, blocks],
-            )
-
-        def round_tiles(grouped, raw, tiles):
-            nc.scalar.copy(
-                grouped[:].rearrange("p (t g r j) -> p t g j r", t=PACK, r=ROWS, j=PACK)[:, tiles],
+                grouped[tiles.start][:].rearrange("p (t g r j) -> p t g j r", t=2, r=ROWS, j=PACK),
                 raw.rearrange("p j (g t r) -> p t g j r", t=PACK, r=ROWS)[:, tiles],
             )
 
         def mx_tiles(name, width):
-            codes = sb.tile([P, width], U32, name=name + "_codes", align_bytes=64)
-            plane = sb.tile([P, width], U8, name=name + "_plane", align_bytes=64)
+            codes = sb.tile([P, width], U32, name=name + "_codes", tag=name + "_codes", align_bytes=64)
+            plane = sb.tile([P, width], U8, name=name + "_plane", tag=name + "_plane", align_bytes=64)
             return codes, plane
 
-        def quantise(mx, first, grouped):
-            cols = slice(first, first + grouped.shape[1] // PACK)
-            nc.vector.quantize_mx(out=mx[0][:, cols].bitcast(FP8X4), scales=mx[1][:, cols], in_=grouped)
+        def quantise(mx, values, tiles):
+            cols = slice(tiles.start * P, tiles.stop * P)
+            nc.vector.quantize_mx(out=mx[0][:, cols].bitcast(FP8X4), scales=mx[1][:, cols], in_=values)
 
         def product(acc, w_mx, tile_no, act_mx, atoms=slice(None)):
             cols = slice(tile_no * P, (tile_no + 1) * P)
@@ -112,247 +104,167 @@ def tile_picked_painn8_none_p_kernel(
                 stop=True,
             )
 
-        q_win = [sb.tile([P, 2 * S], F32, name="q_win%d" % t, tag="q_win%d" % t) for t in range(PACK)]
-        for t in range(PACK):
-            nc.gpsimd.memset(q_win[t][:, S:], 0.0)
-        ident = sb.tile([P, P], F32, name="ident")
-        nc.gpsimd.memset(ident[:], 0.0)
-        make_identity(nc, ident[:], nomemset=True)
+        def pair_tiles(name, tags):
+            return {2 * u: sb.tile([P, 2 * H], BF16, name=name + str(u), tag=tags[u], align_bytes=64) for u in range(2)}
 
-        w3_home = sb.tile([P, 7 * H // 2], BF16, name="w3_home", align_bytes=64)
-        w3_start = (0, 5 * H // 2, H // 2, 3 * H // 2)
-        w3_grouped = [w3_home[:, c0 : c0 + H] for c0 in w3_start]
-        w3_codes = sb.tile([P, 3 * P], U32, name="w3_codes", align_bytes=64)
-        w3_first = (w3_codes, sb.tile([P, P], U8, name="w3_plane0", align_bytes=64))
-        w3_mx = (w3_codes, sb.tile([P, 3 * P], U8, name="w3_plane", align_bytes=64))
-        blocks_half = H // (2 * PACK * ROWS)
-        round_tile(nc.vector.tensor_copy, w3_grouped[0], w3_raw[:], 0, slice(0, blocks_half))
-        round_tile(nc.scalar.copy, w3_grouped[0], w3_raw[:], 0, slice(blocks_half, 2 * blocks_half))
-        quantise(w3_first, 0, w3_grouped[0])
-        for t in (1, 3):
-            round_tile(nc.scalar.copy, w3_grouped[t], w3_raw[:], t)
-        round_tile(nc.vector.tensor_copy, w3_grouped[2], w3_raw[:], 2)
-        quantise(w3_mx, 2 * P, w3_grouped[1])
-        low, high = slice(0, S // 2), slice(S // 2, S)
-        q_low, q_high = bank(0, "q_low"), bank(4, "q_high")
-        product(q_low[:, low], w3_first, 0, x_mx, low)
-        product(q_high[:, low], w3_first, 0, x_mx, high)
-        nc.vector.tensor_copy(q_win[0][:, low], q_low[:, low])
-        nc.scalar.copy(q_win[0][:, high], q_high[:, low])
-        quantise(w3_mx, 0, w3_home[:, H // 2 : 5 * H // 2])
-        for t, place in ((1, 2), (2, 0), (3, 1)):
-            acc = bank(t, "q_acc%d" % t)
-            product(acc[:], w3_mx, place, x_mx)
+        grouped = {"w3": pair_tiles("w3_grouped", ("w3_low", "w3_high"))}
+        w1_mx, w2_mx, w3_mx, w4_mx = (mx_tiles(name, H) for name in ("w1", "w2", "w3", "w4"))
+        low, high = slice(0, 2), slice(2, 4)
+
+        x_codes = sb.tile([P, S], U32, name="x_codes", align_bytes=64)
+        x_plane = sb.tile([P, S], U8, name="x_plane", align_bytes=64)
+        x_mx = (x_codes, x_plane)
+        nc.vector.tensor_copy(x_plane[:], scales_all[:].indirect(offs_sb[:]))
+        round_tiles(nc.vector.tensor_copy, grouped["w3"], w3_raw[:], low)
+        round_tiles(nc.scalar.copy, grouped["w3"], w3_raw[:], high)
+        quantise(w3_mx, grouped["w3"][0][:], low)
+        quantise(w3_mx, grouped["w3"][2][:], high)
+        half = S // 2
+        halves = (slice(0, half), slice(half, S))
+        for h in range(2):
+            entries = offs_sb[:, h * half // LIST : (h + 1) * half // LIST]
+            nc.vector.tensor_copy(x_codes[:, halves[h]], words_all[:].bitcast(U32).indirect(entries))
+
+        for h in range(2):
+            acc = bank(4 * h, "q0_%d" % h)
+            product(acc[:, :half], w3_mx, 0, x_mx, halves[h])
+            nc.scalar.copy(q_win[0][:, halves[h]], acc[:, :half])
+        for t in (1, 2, 3):
+            acc = bank(t, "q%d" % t)
+            product(acc[:], w3_mx, t, x_mx)
             nc.scalar.copy(q_win[t][:, :S], acc[:])
 
-        w1_mx, w2_mx = mx_tiles("w1", H), mx_tiles("w2", H)
-        w1_grouped = sb.tile([P, PACK * H], BF16, name="w1_grouped", align_bytes=64)
-        w2_grouped = sb.tile([P, PACK * H], BF16, name="w2_grouped", align_bytes=64)
-        pair_cols = [slice(u * 2 * H, (u + 1) * 2 * H) for u in range(2)]
-        round_tiles(w1_grouped, w1_raw[:], slice(None))
-        for u in range(2):
-            round_tiles(w2_grouped, w2_raw, slice(2 * u, 2 * u + 2))
-        early = sb.tile([P, 4 * S], F32, name="along_early")
-        late = [w2_home[:, : 2 * S], w2_home[:, 2 * S : 4 * S]]
-        along = {(t, side): early[:, (2 * t + side) * S : (2 * t + side + 1) * S] for t in range(2) for side in range(2)}
-        for t in (2, 3):
-            for side in range(2):
-                along[t, side] = late[side][:, (t - 2) * S : (t - 1) * S]
+        sums = [bank(4 + c, "sum%d" % c) for c in range(CHUNKS)]
+        turned = []
+
+        def turn(t, term):
+            for c in range(CHUNKS):
+                nc.tensor.matmul(
+                    sums[c][:, t * P : (t + 1) * P],
+                    term[:, c * P : (c + 1) * P],
+                    ident[:],
+                    is_transpose=True,
+                    start=len(turned) == 0,
+                    stop=len(turned) == 4 * PACK - 1,
+                )
+            turned.append(t)
+
+        early = sb.tile([P, 3 * S], F32, name="early")
+        order = [(t, side) for t in range(PACK) for side in range(2)]
+        behind_m0 = sb.tile([P, S], F32, name="behind_m0")
+        behind_m2 = sb.tile([P, 4, S], F32, name="behind_m2")
+        along = {key: early[:, no * S : (no + 1) * S] for no, key in enumerate(order[:3])}
+        along[1, 1] = behind_m0[:]
+        for no, key in enumerate(order[4:]):
+            along[key] = behind_m2[:, no, :]
 
         def fetch_along(t, side):
             nc.vector.tensor_tensor(along[t, side], q_win[t][:].indirect(places[side][:]), directions[side][:], MULT)
+            turn(t, along[t, side])
 
-        for t, side in ((0, 0), (0, 1), (1, 0), (1, 1), (2, 0)):
-            fetch_along(t, side)
-        quantise(w1_mx, 0, w1_grouped[:])
-        quantise(w2_mx, 0, w2_grouped[:, pair_cols[0]])
-        fetch_along(3, 0)
-        quantise(w2_mx, 2 * P, w2_grouped[:, pair_cols[1]])
+        m_win = {t: sb.tile([P, 2 * S], F32, name="m_win%d" % t) for t in (1, 3)}
+        m_win[0], m_win[2] = q_win[0], q_win[1]
+
+        def quarters(values):
+            return values.rearrange("p (c n) -> p c n", c=CHUNKS)
+
+        y_sb = {t: quarters(m_win[t][:, S:]) for t in (1, 3)}
+        y_sb[0], y_sb[2] = quarters(behind_m0[:]), behind_m2[:, :, :P]
+
+        def fetch_m(t, side):
+            fetched = sb.tile([P, S], F32, name="fetched%d_%d" % (t, side))
+            nc.scalar.activation(fetched[:], m_win[t][:].indirect(places[side][:]), COPY)
+            turn(t, fetched[:])
+
+        for key in order[:3]:
+            fetch_along(*key)
+
+        def make_y(t):
+            acc = bank(t, "y%d" % t)
+            product(acc[:], w1_mx, t, x_mx)
+            nc.scalar.copy(y_sb[t], quarters(acc[:]))
+
+        def make_m(t):
+            acc = bank(t, "e%d" % t)
+            product(acc[:], w2_mx, t, x_mx)
+            nc.vector.tensor_tensor(quarters(m_win[t][:, :S]), quarters(acc[:]), y_sb[t], MULT)
+
+        grouped["w1"] = pair_tiles("w12_grouped", ("w3_codes", "w3_plane"))
+        grouped["w2"] = grouped["w1"]
+        round_tiles(nc.scalar.copy, grouped["w1"], w1_raw[:], low)
+        round_tiles(nc.scalar.copy, grouped["w1"], w1_raw[:], high)
+        quantise(w1_mx, grouped["w1"][0][:], low)
+        make_y(0)
+        make_y(1)
+        round_tiles(nc.vector.tensor_copy, grouped["w2"], w2_raw[:], low)
+        quantise(w1_mx, grouped["w1"][2][:], high)
+        make_y(2)
+        make_y(3)
+        quantise(w2_mx, grouped["w2"][0][:], low)
+        round_tiles(nc.vector.tensor_copy, grouped["w2"], w2_raw[:], high)
+        make_m(0)
+        quantise(w2_mx, grouped["w2"][2][:], high)
+        make_m(1)
+        fetch_m(0, 0)
+        fetch_along(1, 1)
+        make_m(2)
+        make_m(3)
+        fetch_m(0, 1)
+        fetch_m(1, 0)
+        fetch_along(2, 0)
+        fetch_m(1, 1)
         fetch_along(2, 1)
+        fetch_m(2, 0)
+        w4_grouped = sb.tile([P, PACK * N], BF16, name="w4_grouped", tag="w2_codes", align_bytes=64)
+        nc.vector.tensor_copy(
+            w4_grouped[:].rearrange("p (c i j) -> p c j i", i=4, j=PACK),
+            w4_raw[:].rearrange("p j (c i) -> p c j i", i=4),
+        )
+        fetch_m(2, 1)
+        fetch_m(3, 0)
+        fetch_along(3, 0)
+        quantise(w4_mx, w4_grouped[:], slice(0, 4))
+        fetch_m(3, 1)
         fetch_along(3, 1)
-        y_tiles = [sb.tile([P, S], F32, name="y_sb%d" % t) for t in (0, 2)]
-        y3_home = sb.tile([P, 2 * S], F32, name="y3_home")
-        ye1 = sb.tile([P, 2 * S], F32, name="ye1")
-        y_sb = [y_tiles[0][:], ye1[:, :S], y_tiles[1][:], y3_home[:, S // 2 : 3 * S // 2]]
-        e_sb = {1: ye1[:, S:], 2: sb.tile([P, S], F32, name="e_sb2")}
-        e_sb[3] = shared.tile([P, S], F32, name="e_sb3", offset=0, align_bytes=64)
-        on_gpsimd = {1: slice(VECTOR_COLUMNS, S), 2: slice(0, S), 3: slice(0, S)}
-        e_acc = [bank(t, "e_acc%d" % t) for t in range(PACK)]
-        for t in range(PACK):
-            y_acc = bank(4 + t % 2, "y_acc%d" % t)
-            product(y_acc[:], w1_mx, t, x_mx)
-            product(e_acc[t][:], w2_mx, t, x_mx)
-            nc.scalar.copy(y_sb[t], y_acc[:])
-            if t > 0:
-                nc.scalar.copy(e_sb[t][:, on_gpsimd[t]], e_acc[t][:, on_gpsimd[t]])
-
-        m_win = [q_win[0]] + [
-            sb.tile([P, S], F32, name="m_win%d" % t, tag=tag) for t, tag in ((1, "q_win2"), (2, "m_win2"), (3, "m_win3"))
-        ]
-        nc.vector.tensor_tensor(m_win[0][:, :S], e_acc[0][:], y_sb[0], MULT)
-        nc.vector.tensor_tensor(
-            m_win[1][:, :VECTOR_COLUMNS], e_acc[1][:, :VECTOR_COLUMNS], y_sb[1][:, :VECTOR_COLUMNS], MULT
-        )
-        half = S // 2
-        both_first = ye1[:].rearrange("p (t n) -> p t n", t=2)[:, :, half:]
-
-        def multiply_on_gpsimd(t):
-            cols = on_gpsimd[t]
-            nc.gpsimd.tensor_tensor(m_win[t][:, cols], e_sb[t][:, cols], y_sb[t][:, cols], MULT)
-
-        multiply_on_gpsimd(1)
-        nc.gpsimd.tensor_tensor(
-            both_first,
-            late[0].rearrange("p (t n) -> p t n", t=2)[:, :, :half],
-            late[1].rearrange("p (t n) -> p t n", t=2)[:, :, :half],
-            ADD,
-        )
-        for t in (2, 3):
-            multiply_on_gpsimd(t)
-
-        def summed(name, b, blocks, row):
-            turned = bank(b, name + "_turned")
-            count = len(blocks[0])
-            for no in range(count):
-                for blk, terms in enumerate(blocks):
-                    nc.tensor.matmul(
-                        turned[:, blk * P : (blk + 1) * P],
-                        terms[no],
-                        ident[:],
-                        is_transpose=True,
-                        start=(no == 0 and blk == 0),
-                        stop=(no == count - 1 and blk == len(blocks) - 1),
-                    )
-            width = len(blocks) * P
-            held = w4_raw[:, row, :width]
-            nc.scalar.copy(held, turned[:, :width])
-            back = bank(b, name + "_back")
-            for blk in range(len(blocks)):
-                nc.tensor.transpose(back[:, blk * P : (blk + 1) * P], held[:, blk * P : (blk + 1) * P], ident[:])
-            return back
-
-        def block(values, blk):
-            return values[:, blk * P : (blk + 1) * P]
-
-        fetched = {}
-        for t, width in ((0, S), (1, half)):
-            for side in range(2):
-                fetched[t, side] = sb.tile([P, width], F32, name="fetched%d_%d" % (t, side))
-                nc.vector.tensor_copy(fetched[t, side][:], m_win[t][:].indirect(places[side][:, : width // LIST]))
-
-        def terms_of(t, blk):
-            return [block(values, blk) for values in (along[t, 0], along[t, 1], fetched[t, 0], fetched[t, 1])]
-
-        def directions_of(t, blk):
-            return [block(along[t, side], blk) for side in range(2)]
-
-        z_home = sb.tile([P, 9 * half], F32, name="z_home", align_bytes=64)
-        slots = z_home[:].rearrange("p (s n) -> p s n", n=half)
-        z_first = slots[:, 5:, :]
-        chunks = {"a": (0, half, z_first), "b": (half, P, slots[:, 4:8, :P]), "c": (half + P, P, slots[:, :4, :P])}
-
-        w4_grouped = sb.tile([P, PACK * N], BF16, name="w4_grouped", align_bytes=64)
-        for part in range(2):
-            column_pairs = slice(part * N // 8, (part + 1) * N // 8)
-            nc.scalar.copy(
-                w4_grouped[:].rearrange("p (c i j) -> p c j i", i=4, j=PACK)[:, column_pairs],
-                w4_raw.rearrange("p j (c i) -> p c j i", i=4)[:, column_pairs],
-            )
-
-        both_second = sb.tile([P, 3 * half], F32, name="both_second")
-        back = summed("both1", 4, [directions_of(1, blk) for blk in (2, 3)], 2)
-        nc.scalar.copy(both_second[:, :half], back[:, :half])
-        back = summed("both23", 5, [directions_of(t, blk) for t in (2, 3) for blk in (2, 3)], 3)
-        nc.scalar.copy(both_second[:, half:], back[:])
-        back = summed("z0", 6, [terms_of(0, blk) for blk in (0, 1, 3, 2)], 0)
-        nc.scalar.copy(z_first[:, 0, :], back[:, :half])
-        nc.scalar.copy(slots[:, 0:5:4, :P], back[:, half:].rearrange("p (s n) -> p s n", n=P))
-        back = summed("z1", 7, [terms_of(1, blk) for blk in (0, 1)], 1)
-        nc.scalar.copy(z_first[:, 1, :], back[:, :half])
-
-        def entries(side, c0, width):
-            return places[side][:, c0 // LIST : (c0 + width) // LIST]
-
-        partial3 = sb.tile([P, half], F32, name="partial3")
-        first_partial = {2: y3_home[:, P : P + half], 3: partial3[:]}
-        second_partial = {
-            1: y3_home[:, P + half : P + 2 * half],
-            2: y3_home[:, P + 2 * half : P + 3 * half],
-            3: slots[:, 8, :],
-        }
-        for t in (2, 3):
-            nc.vector.tensor_tensor(first_partial[t], m_win[t][:].indirect(entries(0, 0, half)), both_first[:, t - 2, :], ADD)
-        for t in (2, 3):
-            nc.vector.tensor_tensor(z_first[:, t, :], m_win[t][:].indirect(entries(1, 0, half)), first_partial[t], ADD)
 
         out_rows = out.rearrange("(a p) n -> p a n", p=P)
-        w4_codes = shared.tile([P, N], U32, name="w4_codes", offset=0, align_bytes=64)
-        w4_plane = sb.tile([P, N], U8, name="w4_plane", align_bytes=64)
-        w4_mx = (w4_codes, w4_plane)
-        quantise(w4_mx, 0, w4_grouped[:])
+        copies = (nc.scalar.copy, nc.vector.tensor_copy)
+        z_turned = [sb.tile([P, H], BF16, name="z_turned%d" % c) for c in range(CHUNKS)]
+        z_grouped = [sb.tile([P, PACK * P], BF16, name="z_grouped%d" % c, align_bytes=64) for c in range(CHUNKS)]
+        z_mx = [mx_tiles("z%d" % c, P) for c in range(CHUNKS)]
 
-        def round_chunk(name, copy, grouped, fours=slice(None)):
-            copy(
-                grouped.rearrange("p (c i t) -> p c t i", t=PACK, i=4)[:, fours],
-                chunks[name][2].rearrange("p t (c i) -> p c t i", i=4)[:, fours],
+        def round_z(c):
+            copies[c % 2](
+                z_turned[c][:].rearrange("p (u g t e) -> p u g t e", u=2, t=PACK, e=2),
+                sums[c][:].rearrange("p (t g u e) -> p u g t e", u=2, t=PACK, e=2),
             )
 
-        def multiply(name, z_mx, out_banks):
-            width = chunks[name][1]
-            per_bank = PACK // len(out_banks)
-            accs = [bank(b, name + "_out%d" % no) for no, b in enumerate(out_banks)]
+        def turn_back(c):
+            back = bank(c, "back%d" % c)
+            words = z_turned[c][:].bitcast(F32)
+            for u in range(2):
+                nc.tensor.transpose(back[:, u * P : (u + 1) * P], words[:, u * P : (u + 1) * P], ident[:])
+            nc.scalar.copy(
+                z_grouped[c][:].bitcast(F32).rearrange("p (n u) -> p n u", u=2),
+                back[:, : 2 * P].rearrange("p (u n) -> p n u", u=2),
+            )
+            quantise(z_mx[c], z_grouped[c][:], slice(0, 1))
+
+        def finish(c):
+            acc = bank(4 + c, "out%d" % c)
             for a in range(PACK):
-                col = a % per_bank * width
-                product(accs[a // per_bank][:, col : col + width], w4_mx, a, z_mx)
-            return accs
+                product(acc[:, a * P : (a + 1) * P], w4_mx, a, z_mx[c])
+            staged = sb.tile([P, BANK], F32, name="staged%d" % c)
+            copies[c % 2](staged[:], acc[:])
+            nc.sync.dma_start(out_rows[:, :, c * P : (c + 1) * P], staged[:].rearrange("p (a n) -> p a n", a=PACK))
 
-        def store(name, accs, no, copy, home=None):
-            c0, width, z = chunks[name]
-            per_bank = PACK // len(accs)
-            if home is None:
-                home = sb.tile([P, per_bank * width], F32, name=name + "_staged%d" % no)[:]
-            staged = home.rearrange("p (a n) -> p a n", a=per_bank)
-            copy(staged, accs[no][:, : per_bank * width].rearrange("p (a n) -> p a n", a=per_bank))
-            nc.sync.dma_start(out_rows[:, no * per_bank : (no + 1) * per_bank, c0 : c0 + width], staged)
-
-        a_grouped = z_home[:, half : 3 * half].bitcast(BF16)
-        round_chunk("a", nc.scalar.copy, a_grouped)
-        a_codes = shared.tile([P, half], U32, name="a_codes", offset=4 * N, align_bytes=64)
-        a_plane = sb.tile([P, half], U8, name="a_plane", align_bytes=64)
-        a_mx = (a_codes, a_plane)
-        quantise(a_mx, 0, a_grouped)
-        a_out = multiply("a", a_mx, (0, 1))
-        store("a", a_out, 0, nc.scalar.copy)
-
-        def begin(t, c0, width):
-            cols = slice(c0 - half, c0 - half + width)
-            summed_directions = both_second[:, (t - 1) * half : t * half][:, cols]
-            nc.vector.tensor_tensor(second_partial[t][:, cols], m_win[t][:].indirect(entries(0, c0, width)), summed_directions, ADD)
-
-        for t in (1, 2):
-            begin(t, half, half)
-
-        def finish(name):
-            c0, width, z = chunks[name]
-            for t in (1, 2, 3):
-                partial = second_partial[t][:, c0 - half : c0 - half + width]
-                nc.vector.tensor_tensor(z[:, t, :], m_win[t][:].indirect(entries(1, c0, width)), partial, ADD)
-
-        begin(3, half, half)
-        finish("b")
-        b_grouped = shared.tile([P, PACK * P], BF16, name="b_grouped", offset=4 * N, align_bytes=64)
-        round_chunk("b", nc.scalar.copy, b_grouped[:])
-        store("a", a_out, 1, nc.scalar.copy)
-        finish("c")
-        c_grouped = slots[:, 7, :].bitcast(BF16)
-        round_chunk("c", nc.scalar.copy, c_grouped, slice(VECTOR_ATOMS // 4, P // 4))
-        b_mx, c_mx = mx_tiles("zb", P), mx_tiles("zc", P)
-        quantise(b_mx, 0, b_grouped[:])
-        round_chunk("c", nc.vector.tensor_copy, c_grouped, slice(0, VECTOR_ATOMS // 4))
-        quantise(c_mx, 0, c_grouped)
-        b_out = multiply("b", b_mx, (2, 3))
-        c_out = multiply("c", c_mx, (4, 5, 6, 7))
-        store("b", b_out, 0, nc.scalar.copy)
-        store("b", b_out, 1, nc.vector.tensor_copy, slots[:, 7, :])
-        for no in range(PACK):
-            store("c", c_out, no, nc.vector.tensor_copy if no % 2 else nc.scalar.copy)
+        round_z(0)
+        round_z(1)
+        turn_back(0)
+        round_z(2)
+        round_z(3)
+        turn_back(1)
+        turn_back(2)
+        turn_back(3)
+        for c in range(CHUNKS):
+            finish(c)

@@ -55,23 +55,24 @@ def tile_picked_painn8_none_p_kernel(
         nc.sync.dma_start(w3_raw[:], by_rows(w3))
         nc.sync.dma_start(offs_sb[:], offs)
         nc.sync.dma_start(words_all[:], x_words[0].rearrange("p n t -> p (n t)").bitcast(I32))
-        nc.sync.dma_start(p1_sb[:], p1)
-        directions = [sb.tile([P, S], F32, name=name) for name in ("dir1_sb", "dir2_sb")]
-        nc.sync.dma_start(directions[0][:], dir1)
-        nc.sync.dma_start(p2_sb[:], p2)
-        nc.sync.dma_start(directions[1][:], dir2)
         w1_raw = sb.tile([P, PACK, H], F32, name="w1_raw")
-        w2_raw = sb.tile([P, PACK, H], F32, name="w2_raw")
+        w2_home = sb.tile([P, 7, S], F32, name="w2_home", align_bytes=64)
+        w2_raw = w2_home[:, :PACK, :]
         w4_raw = sb.tile([P, PACK, N], F32, name="w4_raw")
+        directions = [sb.tile([P, S], F32, name=name)[:] for name in ("dir1_sb", "dir2_sb")]
         nc.sync.dma_start(w1_raw[:], by_rows(w1))
-        nc.sync.dma_start(w2_raw[:], by_rows(w2))
-        nc.sync.dma_start(w4_raw[:], by_rows(w4))
+        nc.sync.dma_start(w2_raw, by_rows(w2))
+        for side, given in enumerate((dir1, dir2)):
+            nc.sync.dma_start(places[side][:], (p1, p2)[side])
+            nc.sync.dma_start(directions[side], given)
+        for t in range(PACK):
+            nc.sync.dma_start(w4_raw[:, t, :], w4.rearrange("(b t r) c -> t b r c", t=PACK, r=ROWS)[t])
 
         for quarter in range(4):
             nc.vector.tensor_copy(scales_all[32 * quarter : 32 * quarter + 4, :].bitcast(I32), scale_rows[:, quarter, :])
 
-        q_win = [sb.tile([P, 2 * S], F32, name="q_win%d" % t) for t in range(PACK)]
-        for t in range(PACK):
+        q_win = [sb.tile([P, 2 * S], F32, name="q_win%d" % t, tag="q_win%d" % t, align_bytes=64) for t in range(PACK + 1)]
+        for t in range(PACK + 1):
             nc.gpsimd.memset(q_win[t][:, S:], 0.0)
         ident = sb.tile([P, P], F32, name="ident")
         nc.gpsimd.memset(ident[:], 0.0)
@@ -107,7 +108,7 @@ def tile_picked_painn8_none_p_kernel(
         def pair_tiles(name, tags):
             return {2 * u: sb.tile([P, 2 * H], BF16, name=name + str(u), tag=tags[u], align_bytes=64) for u in range(2)}
 
-        grouped = {"w3": pair_tiles("w3_grouped", ("w3_low", "w3_high"))}
+        grouped = {name: pair_tiles(name + "_grouped", (name + "_low", name + "_high")) for name in ("w3", "w1")}
         w1_mx, w2_mx, w3_mx, w4_mx = (mx_tiles(name, H) for name in ("w1", "w2", "w3", "w4"))
         low, high = slice(0, 2), slice(2, 4)
 
@@ -134,137 +135,185 @@ def tile_picked_painn8_none_p_kernel(
             product(acc[:], w3_mx, t, x_mx)
             nc.scalar.copy(q_win[t][:, :S], acc[:])
 
-        sums = [bank(4 + c, "sum%d" % c) for c in range(CHUNKS)]
-        turned = []
+        TURNED = 3
+        sums = [bank(5 + c, "sum%d" % c) for c in range(TURNED)]
+        turned = {c: [] for c in range(TURNED)}
 
-        def turn(t, term):
-            for c in range(CHUNKS):
+        def turn(t, term, chunks=range(TURNED)):
+            for c in chunks:
                 nc.tensor.matmul(
                     sums[c][:, t * P : (t + 1) * P],
                     term[:, c * P : (c + 1) * P],
                     ident[:],
                     is_transpose=True,
-                    start=len(turned) == 0,
-                    stop=len(turned) == 4 * PACK - 1,
+                    start=len(turned[c]) == 0,
+                    stop=len(turned[c]) == 4 * PACK - 1,
                 )
-            turned.append(t)
+                turned[c].append(t)
 
-        early = sb.tile([P, 3 * S], F32, name="early")
-        order = [(t, side) for t in range(PACK) for side in range(2)]
-        behind_m0 = sb.tile([P, S], F32, name="behind_m0")
-        behind_m2 = sb.tile([P, 4, S], F32, name="behind_m2")
-        along = {key: early[:, no * S : (no + 1) * S] for no, key in enumerate(order[:3])}
-        along[1, 1] = behind_m0[:]
-        for no, key in enumerate(order[4:]):
-            along[key] = behind_m2[:, no, :]
+        def like_y(values, t):
+            return values.rearrange("p (c n) -> p c n", c=y_sb[t].shape[1])
 
-        def fetch_along(t, side):
-            nc.vector.tensor_tensor(along[t, side], q_win[t][:].indirect(places[side][:]), directions[side][:], MULT)
-            turn(t, along[t, side])
+        round_tiles(nc.vector.tensor_copy, grouped["w1"], w1_raw[:], low)
+        round_tiles(nc.vector.tensor_copy, grouped["w1"], w1_raw[:], high)
+        m_win = {1: q_win[4], 2: q_win[0], 3: q_win[1]}
+        along = {key: w2_home[:, slot, :] for slot, key in enumerate(((0, 1), (1, 0), (1, 1)))}
+        for no in range(4):
+            along[2 + no // 2, no % 2] = w2_home[:, 3 + no, :]
+        y_last = sb.tile([P, 1, S], F32, name="y_last")
+        y_sb = {0: w2_home[:, :1, :], 1: w2_home[:, 1:3, :half], 2: w2_home[:, 3:, :P], 3: y_last[:]}
 
-        m_win = {t: sb.tile([P, 2 * S], F32, name="m_win%d" % t) for t in (1, 3)}
-        m_win[0], m_win[2] = q_win[0], q_win[1]
+        early, last = slice(0, TURNED * P), slice(TURNED * P, S)
 
-        def quarters(values):
-            return values.rearrange("p (c n) -> p c n", c=CHUNKS)
+        def fetch_along(t, side, atoms=slice(0, S)):
+            entries = places[side][:, atoms.start // LIST : atoms.stop // LIST]
+            nc.vector.tensor_tensor(along[t, side][:, atoms], q_win[t][:].indirect(entries), directions[side][:, atoms], MULT)
+            if atoms != last:
+                turn(t, along[t, side])
 
-        y_sb = {t: quarters(m_win[t][:, S:]) for t in (1, 3)}
-        y_sb[0], y_sb[2] = quarters(behind_m0[:]), behind_m2[:, :, :P]
+        fetched = [sb.tile([P, PACK, S], F32, name="fetched%d" % side) for side in range(2)]
 
         def fetch_m(t, side):
-            fetched = sb.tile([P, S], F32, name="fetched%d_%d" % (t, side))
-            nc.scalar.activation(fetched[:], m_win[t][:].indirect(places[side][:]), COPY)
-            turn(t, fetched[:])
+            nc.scalar.activation(fetched[side][:, t, :], m_win[t][:].indirect(places[side][:]), COPY)
+            turn(t, fetched[side][:, t, :])
 
-        for key in order[:3]:
-            fetch_along(*key)
+        y_acc = {}
 
-        def make_y(t):
-            acc = bank(t, "y%d" % t)
-            product(acc[:], w1_mx, t, x_mx)
-            nc.scalar.copy(y_sb[t], quarters(acc[:]))
+        def multiply_y(t):
+            y_acc[t] = bank(t % 3, "y%d" % t)
+            product(y_acc[t][:], w1_mx, t, x_mx)
 
         def make_m(t):
-            acc = bank(t, "e%d" % t)
+            acc = bank((4, 3, 1, 2)[t], "e%d" % t)
             product(acc[:], w2_mx, t, x_mx)
-            nc.vector.tensor_tensor(quarters(m_win[t][:, :S]), quarters(acc[:]), y_sb[t], MULT)
+            nc.vector.tensor_tensor(like_y(m_win[t][:, :S], t), like_y(acc[:], t), y_sb[t], MULT)
 
-        grouped["w1"] = pair_tiles("w12_grouped", ("w3_codes", "w3_plane"))
-        grouped["w2"] = grouped["w1"]
-        round_tiles(nc.scalar.copy, grouped["w1"], w1_raw[:], low)
-        round_tiles(nc.scalar.copy, grouped["w1"], w1_raw[:], high)
         quantise(w1_mx, grouped["w1"][0][:], low)
-        make_y(0)
-        make_y(1)
-        round_tiles(nc.vector.tensor_copy, grouped["w2"], w2_raw[:], low)
+        multiply_y(0)
+        multiply_y(1)
         quantise(w1_mx, grouped["w1"][2][:], high)
-        make_y(2)
-        make_y(3)
+        multiply_y(2)
+        grouped["w2"] = pair_tiles("w2_grouped", ("w1_low", "w3_plane"))
+        round_tiles(nc.vector.tensor_copy, grouped["w2"], w2_raw, low)
+        round_tiles(nc.scalar.copy, grouped["w2"], w2_raw, high)
+        for t in range(3):
+            nc.scalar.copy(y_sb[t], like_y(y_acc[t][:], t))
+        multiply_y(3)
+        nc.scalar.copy(y_sb[3], like_y(y_acc[3][:], 3))
         quantise(w2_mx, grouped["w2"][0][:], low)
-        round_tiles(nc.vector.tensor_copy, grouped["w2"], w2_raw[:], high)
-        make_m(0)
+        m_win[0] = sb.tile([P, 2 * S], F32, name="m_win0", tag="w1_low", align_bytes=64)
+        along[0, 0] = m_win[0][:, S:]
+        fetch_along(0, 0)
         quantise(w2_mx, grouped["w2"][2][:], high)
+        w4_pieces = []
+
+        def round_w4(a, piece):
+            values = w4_raw[:, :, a * P : (a + 1) * P].rearrange("p j c -> p c j")
+            nc.gpsimd.tensor_scalar(piece.rearrange("p (c j) -> p c j", j=PACK), values, 1.0, 0.0, MULT, ADD)
+            w4_pieces.append((piece, slice(a, a + 1)))
+
+        w4_first = sb.tile([P, PACK * P], BF16, name="w4_first", tag="w3_plane", align_bytes=64)
+        round_w4(0, w4_first[:])
+        make_m(0)
         make_m(1)
         fetch_m(0, 0)
+        fetch_along(0, 1)
+        fetch_m(0, 1)
+        fetch_along(1, 0)
+        fetch_m(1, 0)
         fetch_along(1, 1)
         make_m(2)
         make_m(3)
-        fetch_m(0, 1)
-        fetch_m(1, 0)
-        fetch_along(2, 0)
+        round_w4(1, along[1, 0][:, :half].bitcast(BF16))
         fetch_m(1, 1)
-        fetch_along(2, 1)
+        fetch_along(2, 0, early)
         fetch_m(2, 0)
-        w4_grouped = sb.tile([P, PACK * N], BF16, name="w4_grouped", tag="w2_codes", align_bytes=64)
-        nc.vector.tensor_copy(
-            w4_grouped[:].rearrange("p (c i j) -> p c j i", i=4, j=PACK),
-            w4_raw[:].rearrange("p j (c i) -> p c j i", i=4),
-        )
+        fetch_along(2, 1, early)
+        fetch_along(3, 0, early)
         fetch_m(2, 1)
+        fetch_along(3, 1, early)
         fetch_m(3, 0)
-        fetch_along(3, 0)
-        quantise(w4_mx, w4_grouped[:], slice(0, 4))
-        fetch_m(3, 1)
-        fetch_along(3, 1)
+        for h in range(2):
+            entries = slice(h * half // LIST, (h + 1) * half // LIST)
+            window = m_win[3][:].indirect(places[1][:, entries])
+            if h == 0:
+                nc.vector.tensor_copy(fetched[1][:, 3, halves[h]], window)
+            else:
+                nc.scalar.activation(fetched[1][:, 3, halves[h]], window, COPY)
+            turn(3, fetched[1][:, 3, :], ((0, 1), (2,))[h])
+
+        def quantise_w4(no):
+            piece, tiles = w4_pieces[no]
+            quantise(w4_mx, piece, tiles)
 
         out_rows = out.rearrange("(a p) n -> p a n", p=P)
-        copies = (nc.scalar.copy, nc.vector.tensor_copy)
-        z_turned = [sb.tile([P, H], BF16, name="z_turned%d" % c) for c in range(CHUNKS)]
+        z_turned = [sb.tile([P, H], BF16, name="z_turned%d" % c) for c in range(TURNED)]
         z_grouped = [sb.tile([P, PACK * P], BF16, name="z_grouped%d" % c, align_bytes=64) for c in range(CHUNKS)]
         z_mx = [mx_tiles("z%d" % c, P) for c in range(CHUNKS)]
 
-        def round_z(c):
-            copies[c % 2](
-                z_turned[c][:].rearrange("p (u g t e) -> p u g t e", u=2, t=PACK, e=2),
-                sums[c][:].rearrange("p (t g u e) -> p u g t e", u=2, t=PACK, e=2),
+        def round_z(c, copy):
+            copy(
+                z_turned[c][:].rearrange("p (u m e) -> p u m e", u=2, e=2),
+                sums[c][:].rearrange("p (u e m) -> p u m e", u=2, e=2),
             )
 
-        def turn_back(c):
+        def turn_back(c, copy):
             back = bank(c, "back%d" % c)
             words = z_turned[c][:].bitcast(F32)
             for u in range(2):
                 nc.tensor.transpose(back[:, u * P : (u + 1) * P], words[:, u * P : (u + 1) * P], ident[:])
-            nc.scalar.copy(
+            copy(
                 z_grouped[c][:].bitcast(F32).rearrange("p (n u) -> p n u", u=2),
                 back[:, : 2 * P].rearrange("p (u n) -> p n u", u=2),
             )
+
+        def quantise_z(c):
             quantise(z_mx[c], z_grouped[c][:], slice(0, 1))
 
-        def finish(c):
-            acc = bank(4 + c, "out%d" % c)
-            for a in range(PACK):
-                product(acc[:, a * P : (a + 1) * P], w4_mx, a, z_mx[c])
-            staged = sb.tile([P, BANK], F32, name="staged%d" % c)
-            copies[c % 2](staged[:], acc[:])
-            nc.sync.dma_start(out_rows[:, :, c * P : (c + 1) * P], staged[:].rearrange("p (a n) -> p a n", a=PACK))
+        def finish(c, banks, copies):
+            rows = PACK // len(banks)
+            for no, (b, copy) in enumerate(zip(banks, copies)):
+                acc = bank(b, "out%d_%d" % (c, no))
+                for a in range(rows):
+                    product(acc[:, a * P : (a + 1) * P], w4_mx, no * rows + a, z_mx[c])
+                staged = sb.tile([P, rows, P], F32, name="staged%d_%d" % (c, no))
+                copy(staged[:], acc[:, : rows * P].rearrange("p (a n) -> p a n", a=rows))
+                nc.sync.dma_start(out_rows[:, no * rows : (no + 1) * rows, c * P : (c + 1) * P], staged[:])
 
-        round_z(0)
-        round_z(1)
-        turn_back(0)
-        round_z(2)
-        round_z(3)
-        turn_back(1)
-        turn_back(2)
-        turn_back(3)
-        for c in range(CHUNKS):
-            finish(c)
+        scalar, vector = nc.scalar.copy, nc.vector.tensor_copy
+        partial = [sb.tile([P, PACK, P], F32, name="partial%d" % no) for no in range(2)]
+        for c in range(TURNED):
+            round_z(c, scalar)
+        rest = sb.tile([P, 2 * PACK * P], BF16, name="w4_rest", tag="w2_codes", align_bytes=64)
+        nc.vector.tensor_copy(
+            rest[:].rearrange("p (c i j) -> p c j i", i=4, j=PACK),
+            w4_raw[:, :, 2 * P :].rearrange("p j (c i) -> p c j i", i=4),
+        )
+        w4_pieces.append((rest[:], slice(2, 4)))
+        for t in (2, 3):
+            for side in range(2):
+                fetch_along(t, side, last)
+        quantise_w4(2)
+        for t in range(2):
+            nc.vector.tensor_tensor(partial[0][:, t, :], along[t, 0][:, last], along[t, 1][:, last], ADD)
+        late = w2_home[:, 3:, last].rearrange("p (t s) n -> p s t n", s=2)
+        nc.vector.tensor_tensor(partial[0][:, 2:, :], late[:, 0], late[:, 1], ADD)
+        nc.vector.tensor_tensor(partial[1][:], fetched[0][:, :, last], fetched[1][:, :, last], ADD)
+        for no in range(2):
+            quantise_w4(no)
+        for c in range(TURNED):
+            turn_back(c, scalar)
+        quantise_z(0)
+        z_last = sb.tile([P, PACK, P], F32, name="z_last")
+        nc.vector.tensor_tensor(z_last[:], partial[0][:], partial[1][:], ADD)
+        quantise_z(1)
+        scalar(
+            z_grouped[3][:].rearrange("p (c i t) -> p c t i", t=PACK, i=4),
+            z_last[:].rearrange("p t (c i) -> p c t i", i=4),
+        )
+        quantise_z(2)
+        quantise_z(3)
+        finish(0, (5,), (scalar,))
+        finish(1, (6,), (scalar,))
+        finish(2, (7,), (scalar,))
+        finish(3, (1, 2), (vector, vector))

@@ -56,8 +56,9 @@ def tile_picked_painn8_none_p_kernel(
         nc.sync.dma_start(offs_sb[:], offs)
         nc.sync.dma_start(words_all[:], x_words[0].rearrange("p n t -> p (n t)").bitcast(I32))
         w1_raw = sb.tile([P, PACK, H], F32, name="w1_raw")
-        w2_home = sb.tile([P, 7, S], F32, name="w2_home", align_bytes=64)
-        w2_raw = w2_home[:, :PACK, :]
+        home = sb.tile([P, 8 * S], F32, name="home", align_bytes=64)
+        slots = home[:].rearrange("p (s n) -> p s n", n=S)
+        w2_raw = slots[:, 1:5, :]
         w4_raw = sb.tile([P, PACK, N], F32, name="w4_raw")
         directions = [sb.tile([P, S], F32, name=name)[:] for name in ("dir1_sb", "dir2_sb")]
         nc.sync.dma_start(w1_raw[:], by_rows(w1))
@@ -80,7 +81,7 @@ def tile_picked_painn8_none_p_kernel(
 
         def round_tiles(copy, grouped, raw, tiles):
             copy(
-                grouped[tiles.start][:].rearrange("p (t g r j) -> p t g j r", t=2, r=ROWS, j=PACK),
+                grouped[tiles.start].rearrange("p (t g r j) -> p t g j r", t=2, r=ROWS, j=PACK),
                 raw.rearrange("p j (g t r) -> p t g j r", t=PACK, r=ROWS)[:, tiles],
             )
 
@@ -105,10 +106,12 @@ def tile_picked_painn8_none_p_kernel(
                 stop=True,
             )
 
-        def pair_tiles(name, tags):
-            return {2 * u: sb.tile([P, 2 * H], BF16, name=name + str(u), tag=tags[u], align_bytes=64) for u in range(2)}
+        def pair_tile(name, tag):
+            return sb.tile([P, 2 * H], BF16, name=name, tag=tag, align_bytes=64)[:]
 
-        grouped = {name: pair_tiles(name + "_grouped", (name + "_low", name + "_high")) for name in ("w3", "w1")}
+        first_slot = home[:, :S].bitcast(BF16)
+        grouped = {"w3": {0: pair_tile("w3_low", "w3_low"), 2: pair_tile("w3_high", "w3_high")}}
+        grouped["w1"] = {0: first_slot, 2: pair_tile("w1_high", "w1_high")}
         w1_mx, w2_mx, w3_mx, w4_mx = (mx_tiles(name, H) for name in ("w1", "w2", "w3", "w4"))
         low, high = slice(0, 2), slice(2, 4)
 
@@ -118,8 +121,8 @@ def tile_picked_painn8_none_p_kernel(
         nc.vector.tensor_copy(x_plane[:], scales_all[:].indirect(offs_sb[:]))
         round_tiles(nc.vector.tensor_copy, grouped["w3"], w3_raw[:], low)
         round_tiles(nc.scalar.copy, grouped["w3"], w3_raw[:], high)
-        quantise(w3_mx, grouped["w3"][0][:], low)
-        quantise(w3_mx, grouped["w3"][2][:], high)
+        quantise(w3_mx, grouped["w3"][0], low)
+        quantise(w3_mx, grouped["w3"][2], high)
         half = S // 2
         halves = (slice(0, half), slice(half, S))
         for h in range(2):
@@ -156,12 +159,11 @@ def tile_picked_painn8_none_p_kernel(
 
         round_tiles(nc.vector.tensor_copy, grouped["w1"], w1_raw[:], low)
         round_tiles(nc.vector.tensor_copy, grouped["w1"], w1_raw[:], high)
-        m_win = {1: q_win[4], 2: q_win[0], 3: q_win[1]}
-        along = {key: w2_home[:, slot, :] for slot, key in enumerate(((0, 1), (1, 0), (1, 1)))}
-        for no in range(4):
-            along[2 + no // 2, no % 2] = w2_home[:, 3 + no, :]
-        y_last = sb.tile([P, 1, S], F32, name="y_last")
-        y_sb = {0: w2_home[:, :1, :], 1: w2_home[:, 1:3, :half], 2: w2_home[:, 3:, :P], 3: y_last[:]}
+        m_first = sb.tile([P, 2 * S], F32, name="m_first")
+        m_win = {0: m_first, 1: q_win[4], 2: q_win[0], 3: q_win[1]}
+        along = {(t, side): slots[:, 2 * t + side, :] for t in range(PACK) for side in range(2)}
+        y_sb = {0: slots[:, 1:2, :], 1: slots[:, 2:4, :half], 2: slots[:, 4:, :P]}
+        y_sb[3] = m_first[:, S:].rearrange("p (c n) -> p c n", c=1)
 
         early, last = slice(0, TURNED * P), slice(TURNED * P, S)
 
@@ -188,23 +190,21 @@ def tile_picked_painn8_none_p_kernel(
             product(acc[:], w2_mx, t, x_mx)
             nc.vector.tensor_tensor(like_y(m_win[t][:, :S], t), like_y(acc[:], t), y_sb[t], MULT)
 
-        quantise(w1_mx, grouped["w1"][0][:], low)
+        quantise(w1_mx, grouped["w1"][0], low)
         multiply_y(0)
         multiply_y(1)
-        quantise(w1_mx, grouped["w1"][2][:], high)
+        quantise(w1_mx, grouped["w1"][2], high)
         multiply_y(2)
-        grouped["w2"] = pair_tiles("w2_grouped", ("w1_low", "w3_plane"))
+        grouped["w2"] = {0: first_slot, 2: pair_tile("w2_high", "w3_plane")}
         round_tiles(nc.vector.tensor_copy, grouped["w2"], w2_raw, low)
         round_tiles(nc.scalar.copy, grouped["w2"], w2_raw, high)
         for t in range(3):
             nc.scalar.copy(y_sb[t], like_y(y_acc[t][:], t))
         multiply_y(3)
         nc.scalar.copy(y_sb[3], like_y(y_acc[3][:], 3))
-        quantise(w2_mx, grouped["w2"][0][:], low)
-        m_win[0] = sb.tile([P, 2 * S], F32, name="m_win0", tag="w1_low", align_bytes=64)
-        along[0, 0] = m_win[0][:, S:]
+        quantise(w2_mx, grouped["w2"][0], low)
         fetch_along(0, 0)
-        quantise(w2_mx, grouped["w2"][2][:], high)
+        quantise(w2_mx, grouped["w2"][2], high)
         w4_pieces = []
 
         def round_w4(a, piece):
@@ -231,6 +231,7 @@ def tile_picked_painn8_none_p_kernel(
         fetch_along(2, 1, early)
         fetch_along(3, 0, early)
         fetch_m(2, 1)
+        round_w4(2, along[3, 0][:, :half].bitcast(BF16))
         fetch_along(3, 1, early)
         fetch_m(3, 0)
         for h in range(2):
@@ -248,7 +249,8 @@ def tile_picked_painn8_none_p_kernel(
 
         out_rows = out.rearrange("(a p) n -> p a n", p=P)
         z_turned = [sb.tile([P, H], BF16, name="z_turned%d" % c) for c in range(TURNED)]
-        z_grouped = [sb.tile([P, PACK * P], BF16, name="z_grouped%d" % c, align_bytes=64) for c in range(CHUNKS)]
+        z_grouped = [sb.tile([P, PACK * P], BF16, name="z_grouped%d" % c, align_bytes=64) for c in range(TURNED)]
+        z_grouped.append(z_grouped[0])
         z_mx = [mx_tiles("z%d" % c, P) for c in range(CHUNKS)]
 
         def round_z(c, copy):
@@ -284,33 +286,30 @@ def tile_picked_painn8_none_p_kernel(
         partial = [sb.tile([P, PACK, P], F32, name="partial%d" % no) for no in range(2)]
         for c in range(TURNED):
             round_z(c, scalar)
-        rest = sb.tile([P, 2 * PACK * P], BF16, name="w4_rest", tag="w2_codes", align_bytes=64)
+        rest = sb.tile([P, PACK * P], BF16, name="w4_rest", tag="w2_codes", align_bytes=64)
         nc.vector.tensor_copy(
             rest[:].rearrange("p (c i j) -> p c j i", i=4, j=PACK),
-            w4_raw[:, :, 2 * P :].rearrange("p j (c i) -> p c j i", i=4),
+            w4_raw[:, :, 3 * P :].rearrange("p j (c i) -> p c j i", i=4),
         )
-        w4_pieces.append((rest[:], slice(2, 4)))
+        w4_pieces.append((rest[:], slice(3, 4)))
         for t in (2, 3):
             for side in range(2):
                 fetch_along(t, side, last)
-        quantise_w4(2)
-        for t in range(2):
-            nc.vector.tensor_tensor(partial[0][:, t, :], along[t, 0][:, last], along[t, 1][:, last], ADD)
-        late = w2_home[:, 3:, last].rearrange("p (t s) n -> p s t n", s=2)
-        nc.vector.tensor_tensor(partial[0][:, 2:, :], late[:, 0], late[:, 1], ADD)
         nc.vector.tensor_tensor(partial[1][:], fetched[0][:, :, last], fetched[1][:, :, last], ADD)
-        for no in range(2):
+        sides = slots[:, :, last].rearrange("p (t s) n -> p s t n", s=2)
+        nc.vector.tensor_tensor(partial[0][:], sides[:, 0], sides[:, 1], ADD)
+        for no in range(PACK):
             quantise_w4(no)
         for c in range(TURNED):
             turn_back(c, scalar)
         quantise_z(0)
-        z_last = sb.tile([P, PACK, P], F32, name="z_last")
-        nc.vector.tensor_tensor(z_last[:], partial[0][:], partial[1][:], ADD)
-        quantise_z(1)
-        scalar(
+        nc.vector.tensor_tensor(
             z_grouped[3][:].rearrange("p (c i t) -> p c t i", t=PACK, i=4),
-            z_last[:].rearrange("p t (c i) -> p c t i", i=4),
+            partial[0][:].rearrange("p t (c i) -> p c t i", i=4),
+            partial[1][:].rearrange("p t (c i) -> p c t i", i=4),
+            ADD,
         )
+        quantise_z(1)
         quantise_z(2)
         quantise_z(3)
         finish(0, (5,), (scalar,))

@@ -60,7 +60,8 @@ def tile_picked_painn8_none_p_kernel(
         slots = home[:].rearrange("p (s n) -> p s n", n=S)
         w2_raw = slots[:, 1:5, :]
         w4_raw = sb.tile([P, PACK, N], F32, name="w4_raw")
-        directions = [sb.tile([P, S], F32, name=name)[:] for name in ("dir1_sb", "dir2_sb")]
+        m_early = [sb.tile([P, 2 * S], F32, name="m_win%d" % t) for t in range(2)]
+        directions = [window[:, S:] for window in m_early]
         nc.sync.dma_start(w1_raw[:], by_rows(w1))
         nc.sync.dma_start(w2_raw, by_rows(w2))
         for side, given in enumerate((dir1, dir2)):
@@ -72,8 +73,8 @@ def tile_picked_painn8_none_p_kernel(
         for quarter in range(4):
             nc.vector.tensor_copy(scales_all[32 * quarter : 32 * quarter + 4, :].bitcast(I32), scale_rows[:, quarter, :])
 
-        q_win = [sb.tile([P, 2 * S], F32, name="q_win%d" % t, tag="q_win%d" % t, align_bytes=64) for t in range(PACK + 1)]
-        for t in range(PACK + 1):
+        q_win = [sb.tile([P, 2 * S], F32, name="q_win%d" % t, tag="q_win%d" % t, align_bytes=64) for t in range(PACK)]
+        for t in range(PACK):
             nc.gpsimd.memset(q_win[t][:, S:], 0.0)
         ident = sb.tile([P, P], F32, name="ident")
         nc.gpsimd.memset(ident[:], 0.0)
@@ -159,11 +160,11 @@ def tile_picked_painn8_none_p_kernel(
 
         round_tiles(nc.vector.tensor_copy, grouped["w1"], w1_raw[:], low)
         round_tiles(nc.vector.tensor_copy, grouped["w1"], w1_raw[:], high)
-        m_first = sb.tile([P, 2 * S], F32, name="m_first")
-        m_win = {0: m_first, 1: q_win[4], 2: q_win[0], 3: q_win[1]}
+        m_win = m_early + q_win[:2]
+        y_last = sb.tile([P, 1, S], F32, name="y_last")
         along = {(t, side): slots[:, 2 * t + side, :] for t in range(PACK) for side in range(2)}
         y_sb = {0: slots[:, 1:2, :], 1: slots[:, 2:4, :half], 2: slots[:, 4:, :P]}
-        y_sb[3] = m_first[:, S:].rearrange("p (c n) -> p c n", c=1)
+        y_sb[3] = y_last[:]
 
         early, last = slice(0, TURNED * P), slice(TURNED * P, S)
 
@@ -200,8 +201,6 @@ def tile_picked_painn8_none_p_kernel(
         round_tiles(nc.scalar.copy, grouped["w2"], w2_raw, high)
         for t in range(3):
             nc.scalar.copy(y_sb[t], like_y(y_acc[t][:], t))
-        multiply_y(3)
-        nc.scalar.copy(y_sb[3], like_y(y_acc[3][:], 3))
         quantise(w2_mx, grouped["w2"][0], low)
         fetch_along(0, 0)
         quantise(w2_mx, grouped["w2"][2], high)
@@ -216,7 +215,9 @@ def tile_picked_painn8_none_p_kernel(
         round_w4(0, w4_first[:])
         make_m(0)
         make_m(1)
+        multiply_y(3)
         fetch_m(0, 0)
+        nc.scalar.copy(y_sb[3], like_y(y_acc[3][:], 3))
         fetch_along(0, 1)
         fetch_m(0, 1)
         fetch_along(1, 0)
@@ -249,8 +250,10 @@ def tile_picked_painn8_none_p_kernel(
 
         out_rows = out.rearrange("(a p) n -> p a n", p=P)
         z_turned = [sb.tile([P, H], BF16, name="z_turned%d" % c) for c in range(TURNED)]
-        z_grouped = [sb.tile([P, PACK * P], BF16, name="z_grouped%d" % c, align_bytes=64) for c in range(TURNED)]
-        z_grouped.append(z_grouped[0])
+        z_grouped = [
+            sb.tile([P, PACK * P], BF16, name="z_grouped%d" % c, tag="z_grouped%d" % c, align_bytes=64)
+            for c in range(CHUNKS)
+        ]
         z_mx = [mx_tiles("z%d" % c, P) for c in range(CHUNKS)]
 
         def round_z(c, copy):
@@ -284,14 +287,14 @@ def tile_picked_painn8_none_p_kernel(
 
         scalar, vector = nc.scalar.copy, nc.vector.tensor_copy
         partial = [sb.tile([P, PACK, P], F32, name="partial%d" % no) for no in range(2)]
-        for c in range(TURNED):
-            round_z(c, scalar)
-        rest = sb.tile([P, PACK * P], BF16, name="w4_rest", tag="w2_codes", align_bytes=64)
-        nc.vector.tensor_copy(
+        rest = sb.tile([P, PACK * P], BF16, name="w4_rest", tag="q_win0", align_bytes=64)
+        nc.scalar.copy(
             rest[:].rearrange("p (c i j) -> p c j i", i=4, j=PACK),
             w4_raw[:, :, 3 * P :].rearrange("p j (c i) -> p c j i", i=4),
         )
         w4_pieces.append((rest[:], slice(3, 4)))
+        for c in range(TURNED):
+            round_z(c, scalar)
         for t in (2, 3):
             for side in range(2):
                 fetch_along(t, side, last)
@@ -303,13 +306,13 @@ def tile_picked_painn8_none_p_kernel(
         for c in range(TURNED):
             turn_back(c, scalar)
         quantise_z(0)
-        nc.vector.tensor_tensor(
-            z_grouped[3][:].rearrange("p (c i t) -> p c t i", t=PACK, i=4),
-            partial[0][:].rearrange("p t (c i) -> p c t i", i=4),
-            partial[1][:].rearrange("p t (c i) -> p c t i", i=4),
-            ADD,
-        )
+        z_last = sb.tile([P, PACK, P], F32, name="z_last", tag="z_grouped0", align_bytes=64)
+        nc.vector.tensor_tensor(z_last[:], partial[0][:], partial[1][:], ADD)
         quantise_z(1)
+        vector(
+            z_grouped[3][:].rearrange("p (c i t) -> p c t i", t=PACK, i=4),
+            z_last[:].rearrange("p t (c i) -> p c t i", i=4),
+        )
         quantise_z(2)
         quantise_z(3)
         finish(0, (5,), (scalar,))

@@ -47,13 +47,13 @@ def tile_picked_painn8_none_p_kernel(
 
         words_all = sb.tile([P, T], I32, name="words_all", align_bytes=64)
         scales_all = sb.tile([P, T], U8, name="scales_all", align_bytes=64)
-        nc.vector.memset(scales_all[:].bitcast(I32), 0)
-        scale_rows = sb.tile([4, 4, T // 4], I32, name="scale_rows")
-        nc.sync.dma_start(scale_rows[:], x_scales[0].bitcast(I32).rearrange("(q r) c -> r q c", r=4))
+        nc.gpsimd.memset(scales_all[:].bitcast(I32), 0)
 
         w3_raw = sb.tile([P, PACK, H], F32, name="w3_raw")
         nc.sync.dma_start(w3_raw[:], by_rows(w3))
         nc.sync.dma_start(offs_sb[:], offs)
+        for row in range(4):
+            nc.sync.dma_start(scales_all[row:P:32, :].bitcast(I32), x_scales[0, row:16:4, :].bitcast(I32))
         nc.sync.dma_start(words_all[:], x_words[0].rearrange("p n t -> p (n t)").bitcast(I32))
         w1_raw = sb.tile([P, PACK, H], F32, name="w1_raw")
         home = sb.tile([P, 8 * S], F32, name="home", align_bytes=64)
@@ -69,9 +69,6 @@ def tile_picked_painn8_none_p_kernel(
             nc.sync.dma_start(directions[side], given)
         for t in range(PACK):
             nc.sync.dma_start(w4_raw[:, t, :], w4.rearrange("(b t r) c -> t b r c", t=PACK, r=ROWS)[t])
-
-        for quarter in range(4):
-            nc.vector.tensor_copy(scales_all[32 * quarter : 32 * quarter + 4, :].bitcast(I32), scale_rows[:, quarter, :])
 
         q_win = [sb.tile([P, 2 * S], F32, name="q_win%d" % t, tag="q_win%d" % t, align_bytes=64) for t in range(PACK)]
         for t in range(PACK):
@@ -119,8 +116,8 @@ def tile_picked_painn8_none_p_kernel(
         x_codes = sb.tile([P, S], U32, name="x_codes", align_bytes=64)
         x_plane = sb.tile([P, S], U8, name="x_plane", align_bytes=64)
         x_mx = (x_codes, x_plane)
-        nc.vector.tensor_copy(x_plane[:], scales_all[:].indirect(offs_sb[:]))
         round_tiles(nc.vector.tensor_copy, grouped["w3"], w3_raw[:], low)
+        nc.vector.tensor_copy(x_plane[:], scales_all[:].indirect(offs_sb[:]))
         round_tiles(nc.scalar.copy, grouped["w3"], w3_raw[:], high)
         quantise(w3_mx, grouped["w3"][0], low)
         quantise(w3_mx, grouped["w3"][2], high)

@@ -203,13 +203,14 @@ def tile_picked_painn8_none_p_kernel(
         quantise(w2_mx, grouped["w2"][2], high)
         w4_pieces = []
 
-        def round_w4(a, piece):
-            values = w4_raw[:, :, a * P : (a + 1) * P].rearrange("p j c -> p c j")
-            nc.gpsimd.tensor_scalar(piece.rearrange("p (c j) -> p c j", j=PACK), values, 1.0, 0.0, MULT, ADD)
-            w4_pieces.append((piece, slice(a, a + 1)))
+        def round_w4(copy, tiles, tag):
+            piece = sb.tile([P, 2 * N], BF16, name="w4_grouped%d" % tiles.start, tag=tag, align_bytes=64)
+            copy(
+                piece[:].rearrange("p (c i j) -> p c j i", i=4, j=PACK),
+                w4_raw[:, :, tiles.start * P : tiles.stop * P].rearrange("p j (c i) -> p c j i", i=4),
+            )
+            w4_pieces.append((piece[:], tiles))
 
-        w4_first = sb.tile([P, PACK * P], BF16, name="w4_first", tag="w3_plane", align_bytes=64)
-        round_w4(0, w4_first[:])
         make_m(0)
         make_m(1)
         multiply_y(3)
@@ -222,14 +223,12 @@ def tile_picked_painn8_none_p_kernel(
         fetch_along(1, 1)
         make_m(2)
         make_m(3)
-        round_w4(1, along[1, 0][:, :half].bitcast(BF16))
         fetch_m(1, 1)
         fetch_along(2, 0, early)
         fetch_m(2, 0)
         fetch_along(2, 1, early)
         fetch_along(3, 0, early)
         fetch_m(2, 1)
-        round_w4(2, along[3, 0][:, :half].bitcast(BF16))
         fetch_along(3, 1, early)
         fetch_m(3, 0)
         for h in range(2):
@@ -284,12 +283,8 @@ def tile_picked_painn8_none_p_kernel(
 
         scalar, vector = nc.scalar.copy, nc.vector.tensor_copy
         partial = [sb.tile([P, PACK, P], F32, name="partial%d" % no) for no in range(2)]
-        rest = sb.tile([P, PACK * P], BF16, name="w4_rest", tag="q_win0", align_bytes=64)
-        nc.scalar.copy(
-            rest[:].rearrange("p (c i j) -> p c j i", i=4, j=PACK),
-            w4_raw[:, :, 3 * P :].rearrange("p j (c i) -> p c j i", i=4),
-        )
-        w4_pieces.append((rest[:], slice(3, 4)))
+        round_w4(vector, low, "w2_codes")
+        round_w4(scalar, high, "q_win0")
         for c in range(TURNED):
             round_z(c, scalar)
         for t in (2, 3):
@@ -298,7 +293,7 @@ def tile_picked_painn8_none_p_kernel(
         nc.vector.tensor_tensor(partial[1][:], fetched[0][:, :, last], fetched[1][:, :, last], ADD)
         sides = slots[:, :, last].rearrange("p (t s) n -> p s t n", s=2)
         nc.vector.tensor_tensor(partial[0][:], sides[:, 0], sides[:, 1], ADD)
-        for no in range(PACK):
+        for no in range(2):
             quantise_w4(no)
         for c in range(TURNED):
             turn_back(c, scalar)

@@ -204,7 +204,7 @@ def tile_picked_painn8_none_p_kernel(
         w4_pieces = []
 
         def round_w4(copy, tiles, tag):
-            piece = sb.tile([P, 2 * N], BF16, name="w4_grouped%d" % tiles.start, tag=tag, align_bytes=64)
+            piece = sb.tile([P, (tiles.stop - tiles.start) * N], BF16, name="w4_grouped%d" % tiles.start, tag=tag, align_bytes=64)
             copy(
                 piece[:].rearrange("p (c i j) -> p c j i", i=4, j=PACK),
                 w4_raw[:, :, tiles.start * P : tiles.stop * P].rearrange("p j (c i) -> p c j i", i=4),
@@ -282,30 +282,31 @@ def tile_picked_painn8_none_p_kernel(
                 nc.sync.dma_start(out_rows[:, no * rows : (no + 1) * rows, c * P : (c + 1) * P], staged[:])
 
         scalar, vector = nc.scalar.copy, nc.vector.tensor_copy
-        partial = [sb.tile([P, PACK, P], F32, name="partial%d" % no) for no in range(2)]
-        round_w4(vector, low, "w2_codes")
-        round_w4(scalar, high, "q_win0")
+        round_w4(vector, slice(0, 3), "w2_codes")
+        round_w4(scalar, slice(3, 4), "q_win0")
         for c in range(TURNED):
             round_z(c, scalar)
         for t in (2, 3):
             for side in range(2):
                 fetch_along(t, side, last)
-        nc.vector.tensor_tensor(partial[1][:], fetched[0][:, :, last], fetched[1][:, :, last], ADD)
-        sides = slots[:, :, last].rearrange("p (t s) n -> p s t n", s=2)
-        nc.vector.tensor_tensor(partial[0][:], sides[:, 0], sides[:, 1], ADD)
         for no in range(2):
             quantise_w4(no)
+        both_m = sb.tile([P, PACK, P], F32, name="both_m")
+        nc.vector.tensor_tensor(both_m[:], fetched[0][:, :, last], fetched[1][:, :, last], ADD)
         for c in range(TURNED):
             turn_back(c, scalar)
         quantise_z(0)
-        z_last = sb.tile([P, PACK, P], F32, name="z_last", tag="z_grouped0", align_bytes=64)
-        nc.vector.tensor_tensor(z_last[:], partial[0][:], partial[1][:], ADD)
+        both_along = sb.tile([P, PACK, P], F32, name="both_along", tag="z_grouped0", align_bytes=64)
+        sides = slots[:, :, last].rearrange("p (t s) n -> p s t n", s=2)
+        nc.vector.tensor_tensor(both_along[:], sides[:, 0], sides[:, 1], ADD)
         quantise_z(1)
+        z_last = sb.tile([P, PACK, P], F32, name="z_last")
+        nc.vector.tensor_tensor(z_last[:], both_along[:], both_m[:], ADD)
+        quantise_z(2)
         vector(
             z_grouped[3][:].rearrange("p (c i t) -> p c t i", t=PACK, i=4),
             z_last[:].rearrange("p t (c i) -> p c t i", i=4),
         )
-        quantise_z(2)
         quantise_z(3)
         finish(0, (5,), (scalar,))
         finish(1, (6,), (scalar,))

@@ -78,8 +78,9 @@ def tile_picked_painn8_none_p_kernel(
         make_identity(nc, ident[:], nomemset=True)
 
         def round_tiles(copy, grouped, raw, tiles):
+            count = tiles.stop - tiles.start
             copy(
-                grouped[tiles.start].rearrange("p (t g r j) -> p t g j r", t=2, r=ROWS, j=PACK),
+                grouped[tiles.start].rearrange("p (t g r j) -> p t g j r", t=count, r=ROWS, j=PACK),
                 raw.rearrange("p j (g t r) -> p t g j r", t=PACK, r=ROWS)[:, tiles],
             )
 
@@ -108,7 +109,11 @@ def tile_picked_painn8_none_p_kernel(
             return sb.tile([P, 2 * H], BF16, name=name, tag=tag, align_bytes=64)[:]
 
         first_slot = home[:, :S].bitcast(BF16)
-        grouped = {"w3": {0: pair_tile("w3_low", "w3_low"), 2: pair_tile("w3_high", "w3_high")}}
+        w3_parts = (slice(0, 1), slice(1, 4))
+        grouped = {"w3": {}}
+        for tiles in w3_parts:
+            part = sb.tile([P, (tiles.stop - tiles.start) * H], BF16, name="w3_part%d" % tiles.start, align_bytes=64)
+            grouped["w3"][tiles.start] = part[:]
         grouped["w1"] = {0: first_slot, 2: pair_tile("w1_high", "w1_high")}
         w1_mx, w2_mx, w3_mx, w4_mx = (mx_tiles(name, H) for name in ("w1", "w2", "w3", "w4"))
         low, high = slice(0, 2), slice(2, 4)
@@ -116,11 +121,11 @@ def tile_picked_painn8_none_p_kernel(
         x_codes = sb.tile([P, S], U32, name="x_codes", align_bytes=64)
         x_plane = sb.tile([P, S], U8, name="x_plane", align_bytes=64)
         x_mx = (x_codes, x_plane)
-        round_tiles(nc.vector.tensor_copy, grouped["w3"], w3_raw[:], low)
+        round_tiles(nc.vector.tensor_copy, grouped["w3"], w3_raw[:], w3_parts[0])
         nc.vector.tensor_copy(x_plane[:], scales_all[:].indirect(offs_sb[:]))
-        round_tiles(nc.scalar.copy, grouped["w3"], w3_raw[:], high)
-        quantise(w3_mx, grouped["w3"][0], low)
-        quantise(w3_mx, grouped["w3"][2], high)
+        round_tiles(nc.scalar.copy, grouped["w3"], w3_raw[:], w3_parts[1])
+        for tiles in w3_parts:
+            quantise(w3_mx, grouped["w3"][tiles.start], tiles)
         half = S // 2
         halves = (slice(0, half), slice(half, S))
         for h in range(2):
@@ -193,12 +198,15 @@ def tile_picked_painn8_none_p_kernel(
         multiply_y(1)
         quantise(w1_mx, grouped["w1"][2], high)
         multiply_y(2)
-        grouped["w2"] = {0: first_slot, 2: pair_tile("w2_high", "w3_plane")}
-        round_tiles(nc.vector.tensor_copy, grouped["w2"], w2_raw, low)
+        second = sb.tile([P, H], BF16, name="w2_second", tag="w1_high", align_bytes=64)
+        grouped["w2"] = {0: first_slot[:, :H], 1: second[:], 2: pair_tile("w2_high", "w3_plane")}
+        for t in range(2):
+            round_tiles(nc.vector.tensor_copy, grouped["w2"], w2_raw, slice(t, t + 1))
         round_tiles(nc.scalar.copy, grouped["w2"], w2_raw, high)
         for t in range(3):
             nc.scalar.copy(y_sb[t], like_y(y_acc[t][:], t))
-        quantise(w2_mx, grouped["w2"][0], low)
+        for t in range(2):
+            quantise(w2_mx, grouped["w2"][t], slice(t, t + 1))
         fetch_along(0, 0)
         quantise(w2_mx, grouped["w2"][2], high)
         w4_pieces = []
@@ -311,4 +319,4 @@ def tile_picked_painn8_none_p_kernel(
         finish(0, (5,), (scalar,))
         finish(1, (6,), (scalar,))
         finish(2, (7,), (scalar,))
-        finish(3, (1, 2), (vector, vector))
+        finish(3, (1, 2, 3, 4), (vector, scalar, vector, scalar))

@@ -287,7 +287,8 @@ def tile_picked_painn8_none_p_kernel(
                     product(acc[:, a * P : (a + 1) * P], w4_mx, no * rows + a, z_mx[c])
                 staged = sb.tile([P, rows, P], F32, name="staged%d_%d" % (c, no))
                 copy(staged[:], acc[:, : rows * P].rearrange("p (a n) -> p a n", a=rows))
-                nc.sync.dma_start(out_rows[:, no * rows : (no + 1) * rows, c * P : (c + 1) * P], staged[:])
+                queue = nc.scalar if c == TURNED and no % 2 == 1 else nc.sync
+                queue.dma_start(out_rows[:, no * rows : (no + 1) * rows, c * P : (c + 1) * P], staged[:])
 
         scalar, vector = nc.scalar.copy, nc.vector.tensor_copy
         round_w4(vector, slice(0, 3), "w2_codes")

from contextlib import ExitStack

import concourse.mybir as mybir
from concourse.masks import make_identity

K, T, S, H, N = 512, 2048, 512, 512, 512
FLOPS = 2 * K * H * S * 3 + 2 * H * N * S

F32 = mybir.dt.float32
BF16 = mybir.dt.bfloat16
I32 = mybir.dt.int32
U32 = mybir.dt.uint32
U16 = mybir.dt.uint16
U8 = mybir.dt.uint8
FP8X4 = mybir.dt.float8_e4m3fn_x4
MULT = mybir.AluOpType.mult
ADD = mybir.AluOpType.add
COPY = mybir.ActivationFunctionType.Copy

P = 128
PACK = 4
LIST = 16
BANK = 512
ROWS = 4
CHUNKS = S // P


def tile_picked_painn8_none_p_kernel(
    tc, x_words, x_scales, w1, w2, w3, dir1, dir2, w4, offs, p1, p2, out
):
    nc = tc.nc
    with ExitStack() as ctx:
        lists = ctx.enter_context(tc.tile_pool(name="lists", bufs=1))
        sb = ctx.enter_context(tc.tile_pool(name="sb", bufs=1))
        psum = ctx.enter_context(tc.psum_pool(name="psum", bufs=1))

        def bank(b, name):
            return psum.tile([P, BANK], F32, tag="bank%d" % b, name=name)

        def by_rows(w):
            return w.rearrange("(p j) c -> p j c", j=PACK)

        offs_sb = lists.tile([P, S // LIST], U16, name="offs_sb")
        p1_sb = lists.tile([P, S // LIST], U16, name="p1_sb")
        p2_sb = lists.tile([P, S // LIST], U16, name="p2_sb")
        places = (p1_sb, p2_sb)

        words_all = sb.tile([P, T], I32, name="words_all", align_bytes=64)
        scales_all = sb.tile([P, T], U8, name="scales_all", align_bytes=64)
        nc.gpsimd.memset(scales_all[:].bitcast(I32), 0)

        w3_raw = sb.tile([P, PACK, H], F32, name="w3_raw")
        nc.sync.dma_start(w3_raw[:], by_rows(w3))
        nc.sync.dma_start(offs_sb[:], offs)
        for row in range(4):
            nc.sync.dma_start(scales_all[row:P:32, :].bitcast(I32), x_scales[0, row:16:4, :].bitcast(I32))
        nc.sync.dma_start(words_all[:], x_words[0].rearrange("p n t -> p (n t)").bitcast(I32))
        w1_raw = sb.tile([P, PACK, H], F32, name="w1_raw")
        home = sb.tile([P, 8 * S], F32, name="home", align_bytes=64)
        slots = home[:].rearrange("p (s n) -> p s n", n=S)
        w2_raw = slots[:, 1:5, :]
        w4_raw = sb.tile([P, PACK, N], F32, name="w4_raw")
        m_early = [sb.tile([P, 2 * S], F32, name="m_win%d" % t) for t in range(2)]
        directions = [window[:, S:] for window in m_early]
        nc.sync.dma_start(w1_raw[:], by_rows(w1))
        nc.sync.dma_start(w2_raw, by_rows(w2))
        for side, given in enumerate((dir1, dir2)):
            nc.sync.dma_start(places[side][:], (p1, p2)[side])
            nc.sync.dma_start(directions[side], given)
        for t in range(PACK):
            nc.sync.dma_start(w4_raw[:, t, :], w4.rearrange("(b t r) c -> t b r c", t=PACK, r=ROWS)[t])

        q_win = [sb.tile([P, 2 * S], F32, name="q_win%d" % t, tag="q_win%d" % t, align_bytes=64) for t in range(PACK)]
        for t in range(PACK):
            nc.gpsimd.memset(q_win[t][:, S:], 0.0)
        ident = sb.tile([P, P], F32, name="ident")
        nc.gpsimd.memset(ident[:], 0.0)
        make_identity(nc, ident[:], nomemset=True)

        def round_tiles(copy, grouped, raw, tiles):
            count = tiles.stop - tiles.start
            copy(
                grouped[tiles.start].rearrange("p (t g r j) -> p t g j r", t=count, r=ROWS, j=PACK),
                raw.rearrange("p j (g t r) -> p t g j r", t=PACK, r=ROWS)[:, tiles],
            )

        def mx_tiles(name, width):
            codes = sb.tile([P, width], U32, name=name + "_codes", tag=name + "_codes", align_bytes=64)
            plane = sb.tile([P, width], U8, name=name + "_plane", tag=name + "_plane", align_bytes=64)
            return codes, plane

        def quantise(mx, values, tiles):
            cols = slice(tiles.start * P, tiles.stop * P)
            nc.vector.quantize_mx(out=mx[0][:, cols].bitcast(FP8X4), scales=mx[1][:, cols], in_=values)

        def product(acc, w_mx, tile_no, act_mx, atoms=slice(None)):
            cols = slice(tile_no * P, (tile_no + 1) * P)
            nc.tensor.matmul_mx(
                out=acc,
                lhsT=w_mx[0][:, cols].bitcast(FP8X4),
                lhsT_scale=w_mx[1][:, cols],
                rhs=act_mx[0][:, atoms].bitcast(FP8X4),
                rhs_scale=act_mx[1][:, atoms],
                start=True,
                stop=True,
            )

        def pair_tile(name, tag):
            return sb.tile([P, 2 * H], BF16, name=name, tag=tag, align_bytes=64)[:]

        first_slot = home[:, :S].bitcast(BF16)
        w3_parts = (slice(0, 1), slice(1, 4))
        grouped = {"w3": {}}
        for tiles in w3_parts:
            part = sb.tile([P, (tiles.stop - tiles.start) * H], BF16, name="w3_part%d" % tiles.start, align_bytes=64)
            grouped["w3"][tiles.start] = part[:]
        grouped["w1"] = {0: first_slot, 2: pair_tile("w1_high", "w1_high")}
        w1_mx, w2_mx, w3_mx, w4_mx = (mx_tiles(name, H) for name in ("w1", "w2", "w3", "w4"))
        low, high = slice(0, 2), slice(2, 4)

        x_codes = sb.tile([P, S], U32, name="x_codes", align_bytes=64)
        x_plane = sb.tile([P, S], U8, name="x_plane", align_bytes=64)
        x_mx = (x_codes, x_plane)
        round_tiles(nc.vector.tensor_copy, grouped["w3"], w3_raw[:], w3_parts[0])
        nc.vector.tensor_copy(x_plane[:], scales_all[:].indirect(offs_sb[:]))
        round_tiles(nc.scalar.copy, grouped["w3"], w3_raw[:], w3_parts[1])
        for tiles in w3_parts:
            quantise(w3_mx, grouped["w3"][tiles.start], tiles)
        half = S // 2
        halves = (slice(0, half), slice(half, S))
        for h in range(2):
            entries = offs_sb[:, h * half // LIST : (h + 1) * half // LIST]
            nc.vector.tensor_copy(x_codes[:, halves[h]], words_all[:].bitcast(U32).indirect(entries))

        for h in range(2):
            acc = bank(4 * h, "q0_%d" % h)
            product(acc[:, :half], w3_mx, 0, x_mx, halves[h])
            nc.scalar.copy(q_win[0][:, halves[h]], acc[:, :half])
        for t in (1, 2, 3):
            acc = bank(t, "q%d" % t)
            product(acc[:], w3_mx, t, x_mx)
            nc.scalar.copy(q_win[t][:, :S], acc[:])

        TURNED = 3
        sums = [bank(5 + c, "sum%d" % c) for c in range(TURNED)]
        turned = {c: [] for c in range(TURNED)}

        def turn(t, term, chunks=range(TURNED)):
            for c in chunks:
                nc.tensor.matmul(
                    sums[c][:, t * P : (t + 1) * P],
                    term[:, c * P : (c + 1) * P],
                    ident[:],
                    is_transpose=True,
                    start=len(turned[c]) == 0,
                    stop=len(turned[c]) == 4 * PACK - 1,
                )
                turned[c].append(t)

        def like_y(values, t):
            return values.rearrange("p (c n) -> p c n", c=y_sb[t].shape[1])

        round_tiles(nc.vector.tensor_copy, grouped["w1"], w1_raw[:], low)
        round_tiles(nc.vector.tensor_copy, grouped["w1"], w1_raw[:], high)
        m_win = m_early + q_win[:2]
        y_last = sb.tile([P, 1, S], F32, name="y_last")
        along = {(t, side): slots[:, 2 * t + side, :] for t in range(PACK) for side in range(2)}
        y_sb = {0: slots[:, 1:2, :], 1: slots[:, 2:4, :half], 2: slots[:, 4:, :P]}
        y_sb[3] = y_last[:]

        early, last = slice(0, TURNED * P), slice(TURNED * P, S)

        def fetch_along(t, side, atoms=slice(0, S)):
            entries = places[side][:, atoms.start // LIST : atoms.stop // LIST]
            nc.vector.tensor_tensor(along[t, side][:, atoms], q_win[t][:].indirect(entries), directions[side][:, atoms], MULT)
            if atoms != last:
                turn(t, along[t, side])

        fetched = [sb.tile([P, PACK, S], F32, name="fetched%d" % side) for side in range(2)]

        def fetch_m(t, side):
            nc.scalar.activation(fetched[side][:, t, :], m_win[t][:].indirect(places[side][:]), COPY)
            turn(t, fetched[side][:, t, :])

        y_acc = {}

        def multiply_y(t):
            y_acc[t] = bank(t % 3, "y%d" % t)
            product(y_acc[t][:], w1_mx, t, x_mx)

        def make_m(t):
            acc = bank((4, 3, 1, 2)[t], "e%d" % t)
            product(acc[:], w2_mx, t, x_mx)
            nc.vector.tensor_tensor(like_y(m_win[t][:, :S], t), like_y(acc[:], t), y_sb[t], MULT)

        quantise(w1_mx, grouped["w1"][0], low)
        multiply_y(0)
        multiply_y(1)
        quantise(w1_mx, grouped["w1"][2], high)
        multiply_y(2)
        second = sb.tile([P, H], BF16, name="w2_second", tag="w1_high", align_bytes=64)
        grouped["w2"] = {0: first_slot[:, :H], 1: second[:], 2: pair_tile("w2_high", "w3_plane")}
        for t in range(2):
            round_tiles(nc.vector.tensor_copy, grouped["w2"], w2_raw, slice(t, t + 1))
        round_tiles(nc.scalar.copy, grouped["w2"], w2_raw, high)
        for t in range(3):
            nc.scalar.copy(y_sb[t], like_y(y_acc[t][:], t))
        for t in range(2):
            quantise(w2_mx, grouped["w2"][t], slice(t, t + 1))
        fetch_along(0, 0)
        quantise(w2_mx, grouped["w2"][2], high)
        w4_pieces = []

        def round_w4(copy, tiles, tag):
            piece = sb.tile([P, (tiles.stop - tiles.start) * N], BF16, name="w4_grouped%d" % tiles.start, tag=tag, align_bytes=64)
            copy(
                piece[:].rearrange("p (c i j) -> p c j i", i=4, j=PACK),
                w4_raw[:, :, tiles.start * P : tiles.stop * P].rearrange("p j (c i) -> p c j i", i=4),
            )
            w4_pieces.append((piece[:], tiles))

        make_m(0)
        make_m(1)
        multiply_y(3)
        fetch_m(0, 0)
        nc.scalar.copy(y_sb[3], like_y(y_acc[3][:], 3))
        fetch_along(0, 1)
        fetch_m(0, 1)
        fetch_along(1, 0)
        fetch_m(1, 0)
        fetch_along(1, 1)
        make_m(2)
        make_m(3)
        fetch_m(1, 1)
        fetch_along(2, 0, early)
        fetch_m(2, 0)
        fetch_along(2, 1, early)
        fetch_along(3, 0, early)
        fetch_m(2, 1)
        fetch_along(3, 1, early)
        fetch_m(3, 0)
        for h in range(2):
            entries = slice(h * half // LIST, (h + 1) * half // LIST)
            window = m_win[3][:].indirect(places[1][:, entries])
            if h == 0:
                nc.vector.tensor_copy(fetched[1][:, 3, halves[h]], window)
            else:
                nc.scalar.activation(fetched[1][:, 3, halves[h]], window, COPY)
            turn(3, fetched[1][:, 3, :], ((0, 1), (2,))[h])

        def quantise_w4(no):
            piece, tiles = w4_pieces[no]
            quantise(w4_mx, piece, tiles)

        out_rows = out.rearrange("(a p) n -> p a n", p=P)
        z_turned = [sb.tile([P, H], BF16, name="z_turned%d" % c) for c in range(TURNED)]
        z_grouped = [
            sb.tile([P, PACK * P], BF16, name="z_grouped%d" % c, tag="z_grouped%d" % c, align_bytes=64)
            for c in range(CHUNKS)
        ]
        z_mx = [mx_tiles("z%d" % c, P) for c in range(CHUNKS)]

        def round_z(c, copy):
            copy(
                z_turned[c][:].rearrange("p (u m e) -> p u m e", u=2, e=2),
                sums[c][:].rearrange("p (u e m) -> p u m e", u=2, e=2),
            )

        def turn_back(c, copy):
            back = bank(c, "back%d" % c)
            words = z_turned[c][:].bitcast(F32)
            for u in range(2):
                nc.tensor.transpose(back[:, u * P : (u + 1) * P], words[:, u * P : (u + 1) * P], ident[:])
            copy(
                z_grouped[c][:].bitcast(F32).rearrange("p (n u) -> p n u", u=2),
                back[:, : 2 * P].rearrange("p (u n) -> p n u", u=2),
            )

        def quantise_z(c):
            quantise(z_mx[c], z_grouped[c][:], slice(0, 1))

        def finish(c, banks, copies):
            rows = PACK // len(banks)
            for no, (b, copy) in enumerate(zip(banks, copies)):
                acc = bank(b, "out%d_%d" % (c, no))
                for a in range(rows):
                    product(acc[:, a * P : (a + 1) * P], w4_mx, no * rows + a, z_mx[c])
                staged = sb.tile([P, rows, P], F32, name="staged%d_%d" % (c, no))
                copy(staged[:], acc[:, : rows * P].rearrange("p (a n) -> p a n", a=rows))
                queue = nc.scalar if c == TURNED and no % 2 == 1 else nc.sync
                queue.dma_start(out_rows[:, no * rows : (no + 1) * rows, c * P : (c + 1) * P], staged[:])

        scalar, vector = nc.scalar.copy, nc.vector.tensor_copy
        round_w4(vector, slice(0, 3), "w2_codes")
        round_w4(scalar, slice(3, 4), "q_win0")
        for c in range(TURNED):
            round_z(c, scalar)
        for t in (2, 3):
            for side in range(2):
                fetch_along(t, side, last)
        for no in range(2):
            quantise_w4(no)
        both_m = sb.tile([P, PACK, P], F32, name="both_m")
        nc.vector.tensor_tensor(both_m[:], fetched[0][:, :, last], fetched[1][:, :, last], ADD)
        for c in range(TURNED):
            turn_back(c, scalar)
        quantise_z(0)
        both_along = sb.tile([P, PACK, P], F32, name="both_along", tag="z_grouped0", align_bytes=64)
        sides = slots[:, :, last].rearrange("p (t s) n -> p s t n", s=2)
        nc.vector.tensor_tensor(both_along[:], sides[:, 0], sides[:, 1], ADD)
        quantise_z(1)
        z_last = sb.tile([P, PACK, P], F32, name="z_last")
        nc.vector.tensor_tensor(z_last[:], both_along[:], both_m[:], ADD)
        quantise_z(2)
        vector(
            z_grouped[3][:].rearrange("p (c i t) -> p c t i", t=PACK, i=4),
            z_last[:].rearrange("p t (c i) -> p c t i", i=4),
        )
        quantise_z(3)
        finish(0, (5,), (scalar,))
        finish(1, (6,), (scalar,))
        finish(2, (7,), (scalar,))
        finish(3, (1, 2, 3, 4), (vector, scalar, vector, scalar))
